import numpy as np
import ml_dtypes


def mxq(x, axis, fmt="e4m3"):
    dtype, down = {"e4m3": (ml_dtypes.float8_e4m3fn, 7), "e5m2": (ml_dtypes.float8_e5m2, 14)}[fmt]
    v = np.moveaxis(np.asarray(x, np.float32).astype(ml_dtypes.bfloat16).astype(np.float64), axis, -1)
    blocks = v.reshape(v.shape[:-1] + (-1, 32))
    amax = np.abs(blocks).max(-1, keepdims=True)
    byte = np.maximum(np.where(amax > 0, np.frexp(amax)[1] - 1 + 127, 0) - down, 1)
    scale = np.exp2(byte - 127.0)
    codes = (blocks / scale).astype(np.float32).astype(dtype).astype(np.float64)
    return np.moveaxis((codes * scale).reshape(v.shape), -1, axis)


WIDE = False


def mx_kscale(k):
    if not WIDE:
        return np.ones(k)
    levels = np.array([10, -10, 5, -5, 0])
    if k % 512:
        return np.exp2(np.random.permutation(np.resize(levels, k // 32))).repeat(32)
    a = np.empty((k // 512, 16))
    for p in range(k // 512):
        a[p, :8] = np.random.permutation(np.resize(levels, 8))
        for g in range(8):
            far = levels[np.abs(levels - a[p, g]) >= 10]
            a[p, g + 8] = far[np.random.randint(len(far))]
    return np.exp2(a.ravel()).repeat(32)


def f64(x):
    return np.asarray(x).astype(np.float64)


def striped(idx):
    return np.tile(np.asarray(idx).reshape(-1, 16).T, (8, 1)).astype(np.uint16)


def unstriped(offs):
    return offs[:16].T.reshape(-1).astype(np.int64)


E2M1 = np.array([0.0, 0.5, 1.0, 1.5, 2.0, 3.0, 4.0, 6.0, -0.0, -0.5, -1.0, -1.5, -2.0, -3.0, -4.0, -6.0])


def pack_weight(w, fmt):
    k, n = w.shape
    w = f64(np.asarray(w, np.float32).astype(ml_dtypes.bfloat16)).reshape(k // 32, 32, n)
    amax = np.abs(w).max(1)
    if fmt == "e4m3":
        byte = np.frexp(amax)[1] - 1 + 127 - 7
    else:
        mant, ex = np.frexp(amax / 6.0)
        byte = np.where(mant > 0.5, ex, ex - 1) + 127
    byte = np.clip(np.where(amax > 0, byte, 1), 1, 254)
    scaled = (w * np.exp2(127.0 - byte)[:, None, :]).reshape(k, n).astype(np.float32)
    by_word = np.ascontiguousarray(scaled.reshape(k // 512, 128, 4, n).transpose(0, 1, 3, 2))
    if fmt == "e4m3":
        words = by_word.astype(ml_dtypes.float8_e4m3fn).view(np.uint8)
    else:
        c = by_word.astype(ml_dtypes.float4_e2m1fn).view(np.uint8) & 0xF
        words = (c[..., 0::2] | (c[..., 1::2] << 4)).reshape(k // 512, 128, 2 * n)
    return np.ascontiguousarray(words), np.ascontiguousarray(byte.astype(np.uint8).reshape(k // 512, 16, n))


def unpack_weight(words, scales, fmt):
    g, _, n = scales.shape
    words = np.ascontiguousarray(words).reshape(g, 128, n, -1)
    if fmt == "e4m3":
        vals = words.view(ml_dtypes.float8_e4m3fn).astype(np.float64)
    else:
        nib = np.empty((g, 128, n, 4), np.uint8)
        nib[..., 0::2] = words & 0xF
        nib[..., 1::2] = words >> 4
        vals = E2M1[nib]
    vals = vals * np.repeat(np.exp2(scales.astype(np.float64) - 127.0), 8, axis=1)[..., None]
    return vals.transpose(0, 1, 3, 2).reshape(g * 512, n)


B, N, T, D, DV, NQ = 2, 1024, 4096, 512, 128, 128
PAGE = 512


def setup_inputs():
    n = np.random.standard_normal
    pages = np.random.permutation(T // PAGE)[:B * N // PAGE]
    idx = (pages[:, None] * PAGE + np.arange(PAGE)[None, :]).reshape(-1)
    s = mx_kscale(D)[:, None]
    u = np.ones(T)
    u[idx] = mx_kscale(B * N)
    r = np.random.uniform(0.5, 2.0, T)
    k = n((D, T)) / s
    v = n((DV, T)) / (u * r)
    kp = pack_weight(k, "e4m3")
    vp = pack_weight(v.T, "e4m3")
    return {
        "qT": (n((B, D, NQ)) * s * (1.00 / np.sqrt(D))).astype(np.float32),
        "k_words": kp[0],
        "k_scales": kp[1],
        "v_words": vp[0],
        "v_scales": vp[1],
        "vs": np.tile(u * r, (128, 1)).astype(np.float32),
        "kb": np.tile(n(T), (128, 1)).astype(np.float32),
        "offs": striped(idx),
        "voffs": striped((pages[:, None] * DV + np.arange(DV)[None, :]).reshape(-1)),
    }


def reference(qT, k_words, k_scales, v_words, v_scales, vs, kb, offs, voffs):
    idx = unstriped(offs)
    k = unpack_weight(k_words, k_scales, "e4m3")
    v = unpack_weight(v_words, v_scales, "e4m3")
    v = v.reshape(T // 512, 512, DV)[unstriped(voffs)[::DV] // DV].reshape(B, N, DV)
    pick = lambda x: x[:, idx].reshape(x.shape[0], B, N).transpose(1, 0, 2)
    q = f64(qT)
    score = mxq(q, 1, "e4m3").transpose(0, 2, 1) @ pick(k)
    score = score + pick(f64(kb))[:, :1, :]
    m = score.max(-1, keepdims=True)
    p = np.exp(score - m)
    total = p.sum(-1, keepdims=True)
    w = p * pick(f64(vs))[:, :1, :]
    y = mxq(w, 2, "e4m3") @ v
    y = y / total
    return y

@@ -1,0 +1,212 @@
+from contextlib import ExitStack
+
+import concourse.mybir as mybir
+from concourse.masks import make_identity
+
+B, N, T, D, DV, NQ = 2, 1024, 4096, 512, 128, 128
+PAGES = 8
+P = 128
+PACK = 4
+PASS = P * PACK
+LIST = 16
+
+F32 = mybir.dt.float32
+BF16 = mybir.dt.bfloat16
+I32 = mybir.dt.int32
+U32 = mybir.dt.uint32
+U16 = mybir.dt.uint16
+U8 = mybir.dt.uint8
+FP8X4 = mybir.dt.float8_e4m3fn_x4
+ALU = mybir.AluOpType
+ACT = mybir.ActivationFunctionType
+AXIS = mybir.AxisListType
+
+BIAS_ROW = 16
+
+FLOPS = 2 * B * NQ * N * (D + DV)
+
+
+def tile_attend_pkv8_soft_kb_kernel(
+    tc, qT, k_words, k_scales, v_words, v_scales, vs, kb, offs, voffs, out
+):
+    nc = tc.nc
+    with ExitStack() as ctx:
+        lists = ctx.enter_context(tc.tile_pool(name="lists", bufs=1))
+        keep = ctx.enter_context(tc.tile_pool(name="keep", bufs=1))
+        psum = ctx.enter_context(tc.psum_pool(name="psum", bufs=1))
+
+        offsets = lists.tile([P, B * N // LIST], U16, name="offsets")
+        v_offsets = lists.tile([P, B * 2 * DV // LIST], U16, name="v_offsets")
+
+        ks_pool = keep.tile([P, T // 4], I32, name="ks_pool", tag="ks_then_vs", align_bytes=64)
+        kb_pool = keep.tile([P, T], F32, name="kb_pool", tag="kb_then_vsc", align_bytes=64)
+        q_raw = keep.tile([P, B, PACK, NQ], F32, name="q_raw", tag="q_then_vw", align_bytes=64)
+        kw_pool = keep.tile([P, T], I32, name="kw_pool", align_bytes=64)
+        warm = keep.tile([P, 1], F32, name="warm")
+        warm_out = keep.tile([P, 1], F32, name="warm_out")
+        ident = keep.tile([P, P], F32, name="ident")
+
+        nc.vector.memset(ks_pool[:], 0)
+        nc.vector.memset(warm[:], 0.0)
+        nc.vector.memset(kb_pool[:], 0.0)
+        nc.vector.memset(ident[:], 0.0)
+        make_identity(nc, ident[:], nomemset=True)
+
+        nc.sync.dma_start(offsets[:], offs)
+        nc.sync.dma_start(
+            q_raw[:].rearrange("p b j q -> p b (j q)"),
+            qT.rearrange("b (p j) q -> p b (j q)", j=PACK),
+        )
+        nc.sync.dma_start(
+            kw_pool[:], k_words[0].rearrange("p t r -> p (t r)").bitcast(I32), max_dma_last_dim=4096
+        )
+        nc.sync.dma_start(v_offsets[:], voffs)
+        ks_rows = k_scales[0].bitcast(I32)
+        for r in range(4):
+            nc.scalar.dma_start(ks_pool[r:P:32, :], ks_rows[r:16:4, :])
+        nc.scalar.activation(warm_out[:], warm[:], ACT.Exp)
+        nc.scalar.dma_start(kb_pool[BIAS_ROW : BIAS_ROW + 1, :], kb[0:1, :])
+
+        q_bf = keep.tile([P, B, NQ, PACK], BF16, name="q_bf", align_bytes=64)
+        for b in range(B):
+            nc.scalar.copy(q_bf[:, b], q_raw[:, b].rearrange("p j q -> p q j"))
+        vw_pool = keep.tile([P, PAGES * DV], I32, name="vw_pool", tag="q_then_vw", align_bytes=64)
+        nc.sync.dma_start(
+            vw_pool[:].rearrange("p (u e) -> p u e", u=PAGES),
+            v_words.rearrange("u p e r -> p u (e r)").bitcast(I32),
+        )
+
+        ks_got = keep.tile([P, B * N], U8, name="ks_got", align_bytes=64)
+        nc.vector.tensor_copy(ks_got[:], ks_pool[:].bitcast(U8).indirect(offsets[:]))
+        vs_pool = keep.tile([P, T], F32, name="vs_pool", tag="ks_then_vs", align_bytes=64)
+        nc.sync.dma_start(vs_pool[:], vs)
+
+        kb_wide = []
+        for b in range(B):
+            kb_got = keep.tile([P, N], F32, name=f"kb_got{b}")
+            nc.vector.tensor_copy(
+                kb_got[:], kb_pool[:].indirect(offsets[:, b * N // LIST : (b + 1) * N // LIST])
+            )
+            kb_col = keep.tile([P, N // P], F32, name=f"kb_col{b}")
+            for h in range(2):
+                turned = psum.tile([P, 4, P], F32, name="turned", tag="turn", bufs=4)
+                for j in range(4):
+                    c0 = (4 * h + j) * P
+                    nc.tensor.transpose(turned[:, j, :], kb_got[:, c0 : c0 + P], ident[:])
+                nc.scalar.copy(kb_col[:, 4 * h : 4 * h + 4], turned[:, :, BIAS_ROW])
+            wide = keep.tile([P, N], F32, name=f"kb_wide{b}")
+            for h in range(2):
+                spread = psum.tile([P, 4, P], F32, name="spread", tag="turn", bufs=4)
+                for j in range(4):
+                    c = 4 * h + j
+                    nc.tensor.transpose(
+                        spread[:, j, :], kb_col[:, c : c + 1].to_broadcast([P, P]), ident[:]
+                    )
+                nc.scalar.copy(
+                    wide[:, h * PASS : (h + 1) * PASS], spread[:].rearrange("p j s -> p (j s)")
+                )
+            kb_wide.append(wide)
+
+        q_codes = keep.tile([P, B * NQ], U32, name="q_codes", align_bytes=64)
+        q_scales = keep.tile([P, B * NQ], U8, name="q_scales", align_bytes=64)
+        nc.vector.quantize_mx(
+            out=q_codes[:].bitcast(FP8X4),
+            scales=q_scales[:],
+            in_=q_bf[:].rearrange("p b q j -> p (b q j)"),
+        )
+
+        vsc_pool = keep.tile([P, PAGES * DV // 4], I32, name="vsc_pool", tag="kb_then_vsc", align_bytes=64)
+        nc.vector.memset(vsc_pool[:], 0)
+        vsc_rows = v_scales.bitcast(I32).rearrange("u f c -> f u c")
+        for r in range(4):
+            nc.scalar.dma_start(
+                vsc_pool[r:P:32, :].rearrange("p (u c) -> p u c", u=PAGES), vsc_rows[r:16:4]
+            )
+
+        banks = {}
+        for b in range(B):
+            for h in range(2):
+                s0 = b * N + h * PASS
+                kw_got = keep.tile([P, PASS], U32, name=f"kw_got{b}{h}", align_bytes=64)
+                nc.vector.tensor_copy(
+                    kw_got[:],
+                    kw_pool[:].bitcast(U32).indirect(offsets[:, s0 // LIST : (s0 + PASS) // LIST]),
+                )
+                bank = psum.tile([P, PASS], F32, name="score", tag="score", bufs=3)
+                nc.tensor.matmul_mx(
+                    out=bank[:],
+                    lhsT=q_codes[:, b * NQ : (b + 1) * NQ].bitcast(FP8X4),
+                    lhsT_scale=q_scales[:, b * NQ : (b + 1) * NQ],
+                    rhs=kw_got[:].bitcast(FP8X4),
+                    rhs_scale=ks_got[:, s0 : s0 + PASS],
+                    start=True,
+                    stop=True,
+                )
+                banks[b, h] = bank
+
+        probs, totals = [], []
+        for b in range(B):
+            s = keep.tile([P, N], F32, name=f"s{b}")
+            for h in range(2):
+                cols = slice(h * PASS, (h + 1) * PASS)
+                nc.vector.tensor_tensor(s[:, cols], banks[b, h][:], kb_wide[b][:, cols], ALU.add)
+            neg_max = keep.tile([P, 1], F32, name=f"neg_max{b}")
+            nc.vector.tensor_reduce(neg_max[:], s[:], AXIS.X, ALU.max, negate=True)
+            p = keep.tile([P, N], F32, name=f"p{b}")
+            total = keep.tile([P, 1], F32, name=f"total{b}")
+            nc.scalar.activation(p[:], s[:], ACT.Exp, bias=neg_max[:], accum_out=total[:])
+            probs.append(p)
+            totals.append(total)
+
+        grouped = {}
+        for b in range(B):
+            for h in range(2):
+                s0 = b * N + h * PASS
+                w = keep.tile([P, PASS], F32, name=f"w{b}{h}")
+                nc.vector.tensor_tensor(
+                    w[:],
+                    vs_pool[:].indirect(offsets[:, s0 // LIST : (s0 + PASS) // LIST]),
+                    probs[b][:, h * PASS : (h + 1) * PASS],
+                    ALU.mult,
+                )
+                w_bf = keep.tile([P, 2, P, 2], BF16, name=f"w_bf{b}{h}")
+                nc.scalar.copy(w_bf[:], w[:].rearrange("q (p u e) -> q u p e", u=2, e=2))
+                pairs = w_bf[:].rearrange("q u p e -> q (u p e)").bitcast(F32)
+                turned = psum.tile([P, 2, NQ], F32, name="w_turned", tag="turn", bufs=4)
+                for u in range(2):
+                    nc.tensor.transpose(turned[:, u, :], pairs[:, u * P : (u + 1) * P], ident[:])
+                w_grouped = keep.tile([P, NQ * PACK], BF16, name=f"w_grouped{b}{h}", align_bytes=64)
+                nc.scalar.copy(
+                    w_grouped[:].bitcast(F32).rearrange("p (q u) -> p q u", u=2),
+                    turned[:].rearrange("p u q -> p q u"),
+                )
+                grouped[b, h] = w_grouped
+
+        vw_got = keep.tile([P, B * 2 * DV], U32, name="vw_got", align_bytes=64)
+        nc.vector.tensor_copy(vw_got[:], vw_pool[:].bitcast(U32).indirect(v_offsets[:]))
+        vsc_got = keep.tile([P, B * 2 * DV], U8, name="vsc_got", align_bytes=64)
+        nc.vector.tensor_copy(vsc_got[:], vsc_pool[:].bitcast(U8).indirect(v_offsets[:]))
+
+        for b in range(B):
+            inverse = keep.tile([P, 1], F32, name=f"inverse{b}")
+            nc.vector.reciprocal(inverse[:], totals[b][:])
+            y = psum.tile([P, DV], F32, name="y", tag="score", bufs=3)
+            for h in range(2):
+                w_codes = keep.tile([P, NQ], U32, name=f"w_codes{b}{h}", align_bytes=64)
+                w_scales = keep.tile([P, NQ], U8, name=f"w_scales{b}{h}", align_bytes=64)
+                nc.vector.quantize_mx(
+                    out=w_codes[:].bitcast(FP8X4), scales=w_scales[:], in_=grouped[b, h][:]
+                )
+                page = slice((2 * b + h) * DV, (2 * b + h + 1) * DV)
+                nc.tensor.matmul_mx(
+                    out=y[:],
+                    lhsT=w_codes[:].bitcast(FP8X4),
+                    lhsT_scale=w_scales[:],
+                    rhs=vw_got[:, page].bitcast(FP8X4),
+                    rhs_scale=vsc_got[:, page],
+                    start=(h == 0),
+                    stop=(h == 1),
+                )
+            result = keep.tile([P, DV], F32, name=f"result{b}")
+            nc.scalar.activation(result[:], y[:], ACT.Copy, scale=inverse[:])
+            nc.sync.dma_start(out[b], result[:])

@@ -38,9 +38,9 @@ def tile_attend_pkv8_soft_kb_kernel(
         offsets = lists.tile([P, B * N // LIST], U16, name="offsets")
         v_offsets = lists.tile([P, B * 2 * DV // LIST], U16, name="v_offsets")
 
-        ks_pool = keep.tile([P, T // 4], I32, name="ks_pool", tag="ks_then_vs", align_bytes=64)
-        kb_pool = keep.tile([P, T], F32, name="kb_pool", tag="kb_then_vsc", align_bytes=64)
-        q_raw = keep.tile([P, B, PACK, NQ], F32, name="q_raw", tag="q_then_vw", align_bytes=64)
+        ks_pool = keep.tile([P, T // 4], I32, name="ks_pool", tag="ks_then_vw", align_bytes=64)
+        kb_pool = keep.tile([P, T], F32, name="kb_pool", tag="kb_then_kw", align_bytes=64)
+        q_raw = keep.tile([P, B, PACK, NQ], F32, name="q_raw", tag="q_then_vs", align_bytes=64)
         kw_pool = keep.tile([P, T], I32, name="kw_pool", align_bytes=64)
         warm = keep.tile([P, 1], F32, name="warm")
         warm_out = keep.tile([P, 1], F32, name="warm_out")
@@ -48,8 +48,8 @@ def tile_attend_pkv8_soft_kb_kernel(
 
         nc.vector.memset(ks_pool[:], 0)
         nc.vector.memset(warm[:], 0.0)
-        nc.vector.memset(kb_pool[:], 0.0)
         nc.vector.memset(ident[:], 0.0)
+        nc.vector.memset(kb_pool[:], 0.0)
         make_identity(nc, ident[:], nomemset=True)
 
         nc.sync.dma_start(offsets[:], offs)
@@ -67,23 +67,28 @@ def tile_attend_pkv8_soft_kb_kernel(
         nc.scalar.activation(warm_out[:], warm[:], ACT.Exp)
         nc.scalar.dma_start(kb_pool[BIAS_ROW : BIAS_ROW + 1, :], kb[0:1, :])
 
-        q_bf = keep.tile([P, B, NQ, PACK], BF16, name="q_bf", align_bytes=64)
+        for i in range(4):
+            idle = psum.tile([P, 4, P], F32, name="idle", tag="turn", bufs=4)
+            for j in range(4):
+                nc.tensor.transpose(idle[:, j, :], ident[:], ident[:])
+
+        q_bf = keep.tile([P, B, NQ, PACK], BF16, name="q_bf", tag="q_bf_then_vsc", align_bytes=64)
         for b in range(B):
             nc.scalar.copy(q_bf[:, b], q_raw[:, b].rearrange("p j q -> p q j"))
-        vw_pool = keep.tile([P, PAGES * DV], I32, name="vw_pool", tag="q_then_vw", align_bytes=64)
+
+        ks_got = keep.tile([P, B * N], U8, name="ks_got", align_bytes=64)
+        nc.vector.tensor_copy(ks_got[:], ks_pool[:].bitcast(U8).indirect(offsets[:]))
+        vw_pool = keep.tile([P, PAGES * DV], I32, name="vw_pool", tag="ks_then_vw", align_bytes=64)
         nc.sync.dma_start(
             vw_pool[:].rearrange("p (u e) -> p u e", u=PAGES),
             v_words.rearrange("u p e r -> p u (e r)").bitcast(I32),
         )
-
-        ks_got = keep.tile([P, B * N], U8, name="ks_got", align_bytes=64)
-        nc.vector.tensor_copy(ks_got[:], ks_pool[:].bitcast(U8).indirect(offsets[:]))
-        vs_pool = keep.tile([P, T], F32, name="vs_pool", tag="ks_then_vs", align_bytes=64)
+        vs_pool = keep.tile([P, T], F32, name="vs_pool", tag="q_then_vs", align_bytes=64)
         nc.sync.dma_start(vs_pool[:], vs)
 
-        kb_wide = []
+        kb_cols = []
         for b in range(B):
-            kb_got = keep.tile([P, N], F32, name=f"kb_got{b}")
+            kb_got = keep.tile([P, N], F32, name=f"kb_got{b}", tag=f"kb_got{b}", align_bytes=64)
             nc.vector.tensor_copy(
                 kb_got[:], kb_pool[:].indirect(offsets[:, b * N // LIST : (b + 1) * N // LIST])
             )
@@ -94,18 +99,7 @@ def tile_attend_pkv8_soft_kb_kernel(
                     c0 = (4 * h + j) * P
                     nc.tensor.transpose(turned[:, j, :], kb_got[:, c0 : c0 + P], ident[:])
                 nc.scalar.copy(kb_col[:, 4 * h : 4 * h + 4], turned[:, :, BIAS_ROW])
-            wide = keep.tile([P, N], F32, name=f"kb_wide{b}")
-            for h in range(2):
-                spread = psum.tile([P, 4, P], F32, name="spread", tag="turn", bufs=4)
-                for j in range(4):
-                    c = 4 * h + j
-                    nc.tensor.transpose(
-                        spread[:, j, :], kb_col[:, c : c + 1].to_broadcast([P, P]), ident[:]
-                    )
-                nc.scalar.copy(
-                    wide[:, h * PASS : (h + 1) * PASS], spread[:].rearrange("p j s -> p (j s)")
-                )
-            kb_wide.append(wide)
+            kb_cols.append(kb_col)
 
         q_codes = keep.tile([P, B * NQ], U32, name="q_codes", align_bytes=64)
         q_scales = keep.tile([P, B * NQ], U8, name="q_scales", align_bytes=64)
@@ -115,48 +109,66 @@ def tile_attend_pkv8_soft_kb_kernel(
             in_=q_bf[:].rearrange("p b q j -> p (b q j)"),
         )
 
-        vsc_pool = keep.tile([P, PAGES * DV // 4], I32, name="vsc_pool", tag="kb_then_vsc", align_bytes=64)
+        vsc_pool = keep.tile([P, PAGES * DV // 4], I32, name="vsc_pool", tag="q_bf_then_vsc", align_bytes=64)
         nc.vector.memset(vsc_pool[:], 0)
         vsc_rows = v_scales.bitcast(I32).rearrange("u f c -> f u c")
         for r in range(4):
-            nc.scalar.dma_start(
+            nc.sync.dma_start(
                 vsc_pool[r:P:32, :].rearrange("p (u c) -> p u c", u=PAGES), vsc_rows[r:16:4]
             )
 
-        banks = {}
-        for b in range(B):
-            for h in range(2):
-                s0 = b * N + h * PASS
-                kw_got = keep.tile([P, PASS], U32, name=f"kw_got{b}{h}", align_bytes=64)
-                nc.vector.tensor_copy(
-                    kw_got[:],
-                    kw_pool[:].bitcast(U32).indirect(offsets[:, s0 // LIST : (s0 + PASS) // LIST]),
-                )
-                bank = psum.tile([P, PASS], F32, name="score", tag="score", bufs=3)
-                nc.tensor.matmul_mx(
-                    out=bank[:],
-                    lhsT=q_codes[:, b * NQ : (b + 1) * NQ].bitcast(FP8X4),
-                    lhsT_scale=q_scales[:, b * NQ : (b + 1) * NQ],
-                    rhs=kw_got[:].bitcast(FP8X4),
-                    rhs_scale=ks_got[:, s0 : s0 + PASS],
-                    start=True,
-                    stop=True,
-                )
-                banks[b, h] = bank
+        kw_got = keep.tile([P, B * N], U32, name="kw_got", tag="kb_then_kw", align_bytes=64)
+        for s0 in range(0, B * N, PASS):
+            nc.vector.tensor_copy(
+                kw_got[:, s0 : s0 + PASS],
+                kw_pool[:].bitcast(U32).indirect(offsets[:, s0 // LIST : (s0 + PASS) // LIST]),
+            )
+        vw_got = keep.tile([P, B * 2 * DV], U32, name="vw_got", tag="kb_got0", align_bytes=64)
+        nc.vector.tensor_copy(vw_got[:], vw_pool[:].bitcast(U32).indirect(v_offsets[:]))
 
         probs, totals = [], []
         for b in range(B):
-            s = keep.tile([P, N], F32, name=f"s{b}")
+            banks = []
             for h in range(2):
-                cols = slice(h * PASS, (h + 1) * PASS)
-                nc.vector.tensor_tensor(s[:, cols], banks[b, h][:], kb_wide[b][:, cols], ALU.add)
+                raw = psum.tile([P, 4, NQ], F32, name="raw", tag="turn", bufs=4)
+                for j in range(4):
+                    c0 = b * N + h * PASS + j * P
+                    nc.tensor.matmul_mx(
+                        out=raw[:, j, :],
+                        lhsT=kw_got[:, c0 : c0 + P].bitcast(FP8X4),
+                        lhsT_scale=ks_got[:, c0 : c0 + P],
+                        rhs=q_codes[:, b * NQ : (b + 1) * NQ].bitcast(FP8X4),
+                        rhs_scale=q_scales[:, b * NQ : (b + 1) * NQ],
+                        start=True,
+                        stop=True,
+                    )
+                biased = keep.tile([P, 4, NQ], F32, name=f"biased{b}{h}")
+                for j in range(4):
+                    c = 4 * h + j
+                    nc.scalar.activation(
+                        biased[:, j, :], raw[:, j, :], ACT.Identity, bias=kb_cols[b][:, c : c + 1]
+                    )
+                bank = psum.tile([P, PASS], F32, name="score", tag="score", bufs=4)
+                for j in range(4):
+                    nc.tensor.transpose(bank[:, j * P : (j + 1) * P], biased[:, j, :], ident[:])
+                banks.append(bank)
+            half_max = keep.tile([P, 2], F32, name=f"half_max{b}")
+            for h in range(2):
+                nc.vector.tensor_reduce(half_max[:, h : h + 1], banks[h][:], AXIS.X, ALU.max)
             neg_max = keep.tile([P, 1], F32, name=f"neg_max{b}")
-            nc.vector.tensor_reduce(neg_max[:], s[:], AXIS.X, ALU.max, negate=True)
-            p = keep.tile([P, N], F32, name=f"p{b}")
-            total = keep.tile([P, 1], F32, name=f"total{b}")
-            nc.scalar.activation(p[:], s[:], ACT.Exp, bias=neg_max[:], accum_out=total[:])
+            nc.vector.tensor_reduce(neg_max[:], half_max[:], AXIS.X, ALU.max, negate=True)
+            p = keep.tile([P, N], F32, name=f"p{b}", tag=f"p{b}", align_bytes=64)
+            half_total = keep.tile([P, 2], F32, name=f"half_total{b}")
+            for h in range(2):
+                nc.scalar.activation(
+                    p[:, h * PASS : (h + 1) * PASS],
+                    banks[h][:],
+                    ACT.Exp,
+                    bias=neg_max[:],
+                    accum_out=half_total[:, h : h + 1],
+                )
             probs.append(p)
-            totals.append(total)
+            totals.append(half_total)
 
         grouped = {}
         for b in range(B):
@@ -175,27 +187,24 @@ def tile_attend_pkv8_soft_kb_kernel(
                 turned = psum.tile([P, 2, NQ], F32, name="w_turned", tag="turn", bufs=4)
                 for u in range(2):
                     nc.tensor.transpose(turned[:, u, :], pairs[:, u * P : (u + 1) * P], ident[:])
-                w_grouped = keep.tile([P, NQ * PACK], BF16, name=f"w_grouped{b}{h}", align_bytes=64)
-                nc.scalar.copy(
-                    w_grouped[:].bitcast(F32).rearrange("p (q u) -> p q u", u=2),
-                    turned[:].rearrange("p u q -> p q u"),
-                )
-                grouped[b, h] = w_grouped
+                grouped[b, h] = turned
 
-        vw_got = keep.tile([P, B * 2 * DV], U32, name="vw_got", align_bytes=64)
-        nc.vector.tensor_copy(vw_got[:], vw_pool[:].bitcast(U32).indirect(v_offsets[:]))
-        vsc_got = keep.tile([P, B * 2 * DV], U8, name="vsc_got", align_bytes=64)
+        vsc_got = keep.tile([P, B * 2 * DV], U8, name="vsc_got", tag="p0", align_bytes=64)
         nc.vector.tensor_copy(vsc_got[:], vsc_pool[:].bitcast(U8).indirect(v_offsets[:]))
 
         for b in range(B):
-            inverse = keep.tile([P, 1], F32, name=f"inverse{b}")
-            nc.vector.reciprocal(inverse[:], totals[b][:])
-            y = psum.tile([P, DV], F32, name="y", tag="score", bufs=3)
+            y = psum.tile([P, DV], F32, name="y", tag="score", bufs=4)
             for h in range(2):
+                w_grouped = keep.tile([P, NQ * PACK], BF16, name=f"w_grouped{b}{h}", align_bytes=64)
+                copy_out = nc.vector.tensor_copy if b == 0 else nc.scalar.copy
+                copy_out(
+                    w_grouped[:].bitcast(F32).rearrange("p (q u) -> p q u", u=2),
+                    grouped[b, h][:].rearrange("p u q -> p q u"),
+                )
                 w_codes = keep.tile([P, NQ], U32, name=f"w_codes{b}{h}", align_bytes=64)
                 w_scales = keep.tile([P, NQ], U8, name=f"w_scales{b}{h}", align_bytes=64)
                 nc.vector.quantize_mx(
-                    out=w_codes[:].bitcast(FP8X4), scales=w_scales[:], in_=grouped[b, h][:]
+                    out=w_codes[:].bitcast(FP8X4), scales=w_scales[:], in_=w_grouped[:]
                 )
                 page = slice((2 * b + h) * DV, (2 * b + h + 1) * DV)
                 nc.tensor.matmul_mx(
@@ -207,6 +216,10 @@ def tile_attend_pkv8_soft_kb_kernel(
                     start=(h == 0),
                     stop=(h == 1),
                 )
+            total = keep.tile([P, 1], F32, name=f"total{b}")
+            nc.vector.tensor_reduce(total[:], totals[b][:], AXIS.X, ALU.add)
+            inverse = keep.tile([P, 1], F32, name=f"inverse{b}")
+            nc.vector.reciprocal(inverse[:], total[:])
             result = keep.tile([P, DV], F32, name=f"result{b}")
             nc.scalar.activation(result[:], y[:], ACT.Copy, scale=inverse[:])
             nc.sync.dma_start(out[b], result[:])

@@ -38,10 +38,13 @@ def tile_attend_pkv8_soft_kb_kernel(
         offsets = lists.tile([P, B * N // LIST], U16, name="offsets")
         v_offsets = lists.tile([P, B * 2 * DV // LIST], U16, name="v_offsets")
 
-        ks_pool = keep.tile([P, T // 4], I32, name="ks_pool", tag="ks_then_vw", align_bytes=64)
-        kb_pool = keep.tile([P, T], F32, name="kb_pool", tag="kb_then_kw", align_bytes=64)
-        q_raw = keep.tile([P, B, PACK, NQ], F32, name="q_raw", tag="q_then_vs", align_bytes=64)
+        ks_pool = keep.tile([P, T // 4], I32, name="ks_pool", align_bytes=64)
+        kb_pool = keep.tile([P, T], F32, name="kb_pool", align_bytes=64)
         kw_pool = keep.tile([P, T], I32, name="kw_pool", align_bytes=64)
+        vw_pool = keep.tile([P, PAGES * DV], I32, name="vw_pool", align_bytes=64)
+        vs_pool = keep.tile([P, T], F32, name="vs_pool", align_bytes=64)
+        vsc_pool = keep.tile([P, PAGES * DV // 4], I32, name="vsc_pool", align_bytes=64)
+        q_raw = [keep.tile([P, PACK, NQ], F32, name=f"q_raw{b}") for b in range(B)]
         warm = keep.tile([P, 1], F32, name="warm")
         warm_out = keep.tile([P, 1], F32, name="warm_out")
         ident = keep.tile([P, P], F32, name="ident")
@@ -50,45 +53,52 @@ def tile_attend_pkv8_soft_kb_kernel(
         nc.vector.memset(warm[:], 0.0)
         nc.vector.memset(ident[:], 0.0)
         nc.vector.memset(kb_pool[:], 0.0)
+        nc.vector.memset(vsc_pool[:], 0)
         make_identity(nc, ident[:], nomemset=True)
 
+        def load_queries(b):
+            nc.sync.dma_start(q_raw[b][:], qT[b].rearrange("(p j) q -> p j q", j=PACK))
+
         nc.sync.dma_start(offsets[:], offs)
-        nc.sync.dma_start(
-            q_raw[:].rearrange("p b j q -> p b (j q)"),
-            qT.rearrange("b (p j) q -> p b (j q)", j=PACK),
-        )
-        nc.sync.dma_start(
-            kw_pool[:], k_words[0].rearrange("p t r -> p (t r)").bitcast(I32), max_dma_last_dim=4096
-        )
         nc.sync.dma_start(v_offsets[:], voffs)
+        load_queries(0)
         ks_rows = k_scales[0].bitcast(I32)
         for r in range(4):
-            nc.scalar.dma_start(ks_pool[r:P:32, :], ks_rows[r:16:4, :])
-        nc.scalar.activation(warm_out[:], warm[:], ACT.Exp)
-        nc.scalar.dma_start(kb_pool[BIAS_ROW : BIAS_ROW + 1, :], kb[0:1, :])
-
-        for i in range(4):
-            idle = psum.tile([P, 4, P], F32, name="idle", tag="turn", bufs=4)
-            for j in range(4):
-                nc.tensor.transpose(idle[:, j, :], ident[:], ident[:])
-
-        q_bf = keep.tile([P, B, NQ, PACK], BF16, name="q_bf", tag="q_bf_then_vsc", align_bytes=64)
-        for b in range(B):
-            nc.scalar.copy(q_bf[:, b], q_raw[:, b].rearrange("p j q -> p q j"))
-
-        ks_got = keep.tile([P, B * N], U8, name="ks_got", align_bytes=64)
-        nc.vector.tensor_copy(ks_got[:], ks_pool[:].bitcast(U8).indirect(offsets[:]))
-        vw_pool = keep.tile([P, PAGES * DV], I32, name="vw_pool", tag="ks_then_vw", align_bytes=64)
+            nc.sync.dma_start(ks_pool[r:P:32, :], ks_rows[r:16:4, :])
+        kw_rows = k_words[0].rearrange("p t r -> p (t r)").bitcast(I32)
+        nc.sync.dma_start(kw_pool[:, : T // 2], kw_rows[:, : T // 2])
+        nc.sync.dma_start(kb_pool[BIAS_ROW : BIAS_ROW + 1, :], kb[0:1, :])
+        nc.sync.dma_start(kw_pool[:, T // 2 :], kw_rows[:, T // 2 :])
+        load_queries(1)
         nc.sync.dma_start(
             vw_pool[:].rearrange("p (u e) -> p u e", u=PAGES),
             v_words.rearrange("u p e r -> p u (e r)").bitcast(I32),
         )
-        vs_pool = keep.tile([P, T], F32, name="vs_pool", tag="q_then_vs", align_bytes=64)
         nc.sync.dma_start(vs_pool[:], vs)
+        vsc_rows = v_scales.bitcast(I32).rearrange("u f c -> f u c")
+        for r in range(4):
+            nc.sync.dma_start(
+                vsc_pool[r:P:32, :].rearrange("p (u c) -> p u c", u=PAGES), vsc_rows[r:16:4]
+            )
+        nc.scalar.activation(warm_out[:], warm[:], ACT.Exp)
 
-        kb_cols = []
-        for b in range(B):
-            kb_got = keep.tile([P, N], F32, name=f"kb_got{b}", tag=f"kb_got{b}", align_bytes=64)
+        for i in range(6):
+            idle = psum.tile([P, 4, P], F32, name="idle", tag="turn", bufs=4)
+            for j in range(4):
+                nc.tensor.transpose(idle[:, j, :], ident[:], ident[:])
+
+        def quantise_queries(b):
+            q_bf = keep.tile([P, NQ, PACK], BF16, name=f"q_bf{b}", align_bytes=64)
+            nc.scalar.copy(q_bf[:], q_raw[b][:].rearrange("p j q -> p q j"))
+            codes = keep.tile([P, NQ], U32, name=f"q_codes{b}", align_bytes=64)
+            scales = keep.tile([P, NQ], U8, name=f"q_scales{b}", align_bytes=64)
+            nc.vector.quantize_mx(
+                out=codes[:].bitcast(FP8X4), scales=scales[:], in_=q_bf[:].rearrange("p q j -> p (q j)")
+            )
+            return codes, scales
+
+        def gather_bias(b, tag):
+            kb_got = keep.tile([P, N], F32, name=f"kb_got{b}", tag=tag, align_bytes=64)
             nc.vector.tensor_copy(
                 kb_got[:], kb_pool[:].indirect(offsets[:, b * N // LIST : (b + 1) * N // LIST])
             )
@@ -99,59 +109,63 @@ def tile_attend_pkv8_soft_kb_kernel(
                     c0 = (4 * h + j) * P
                     nc.tensor.transpose(turned[:, j, :], kb_got[:, c0 : c0 + P], ident[:])
                 nc.scalar.copy(kb_col[:, 4 * h : 4 * h + 4], turned[:, :, BIAS_ROW])
-            kb_cols.append(kb_col)
+            return kb_col
 
-        q_codes = keep.tile([P, B * NQ], U32, name="q_codes", align_bytes=64)
-        q_scales = keep.tile([P, B * NQ], U8, name="q_scales", align_bytes=64)
-        nc.vector.quantize_mx(
-            out=q_codes[:].bitcast(FP8X4),
-            scales=q_scales[:],
-            in_=q_bf[:].rearrange("p b q j -> p (b q j)"),
-        )
-
-        vsc_pool = keep.tile([P, PAGES * DV // 4], I32, name="vsc_pool", tag="q_bf_then_vsc", align_bytes=64)
-        nc.vector.memset(vsc_pool[:], 0)
-        vsc_rows = v_scales.bitcast(I32).rearrange("u f c -> f u c")
-        for r in range(4):
-            nc.sync.dma_start(
-                vsc_pool[r:P:32, :].rearrange("p (u c) -> p u c", u=PAGES), vsc_rows[r:16:4]
-            )
-
-        kw_got = keep.tile([P, B * N], U32, name="kw_got", tag="kb_then_kw", align_bytes=64)
-        for s0 in range(0, B * N, PASS):
+        def gather_keys(b, h):
+            s0 = b * N + h * PASS
+            got = keep.tile([P, PASS], U32, name=f"kw_got{b}{h}", tag=f"kw_got{b}{h}", align_bytes=64)
             nc.vector.tensor_copy(
-                kw_got[:, s0 : s0 + PASS],
-                kw_pool[:].bitcast(U32).indirect(offsets[:, s0 // LIST : (s0 + PASS) // LIST]),
+                got[:], kw_pool[:].bitcast(U32).indirect(offsets[:, s0 // LIST : (s0 + PASS) // LIST])
             )
+            return got
+
+        def raw_scores(b, h):
+            raw = psum.tile([P, 4, NQ], F32, name="raw", tag="turn", bufs=4)
+            for j in range(4):
+                c0 = b * N + h * PASS + j * P
+                nc.tensor.matmul_mx(
+                    out=raw[:, j, :],
+                    lhsT=kw_got[b, h][:, j * P : (j + 1) * P].bitcast(FP8X4),
+                    lhsT_scale=ks_got[:, c0 : c0 + P],
+                    rhs=queries[b][0][:].bitcast(FP8X4),
+                    rhs_scale=queries[b][1][:],
+                    start=True,
+                    stop=True,
+                )
+            return raw
+
+        def biased_scores(b, h, raw):
+            biased = keep.tile([P, 4, NQ], F32, name=f"biased{b}{h}")
+            for j in range(4):
+                c = 4 * h + j
+                nc.scalar.activation(
+                    biased[:, j, :], raw[:, j, :], ACT.Identity, bias=kb_cols[b][:, c : c + 1]
+                )
+            bank = psum.tile([P, PASS], F32, name="score", tag="score", bufs=4)
+            for j in range(4):
+                nc.tensor.transpose(bank[:, j * P : (j + 1) * P], biased[:, j, :], ident[:])
+            return bank
+
+        ks_got = keep.tile([P, B * N], U8, name="ks_got", align_bytes=64)
+        nc.vector.tensor_copy(ks_got[:], ks_pool[:].bitcast(U8).indirect(offsets[:]))
+
+        queries, kb_cols, kw_got, scores = {}, {}, {}, {}
+        for b in range(B):
+            if b == 0:
+                queries[b] = quantise_queries(b)
+            kb_cols[b] = gather_bias(b, "kb_got0" if b == 0 else "kw_got00")
+            if b == 1:
+                queries[b] = quantise_queries(b)
+            for h in range(2):
+                kw_got[b, h] = gather_keys(b, h)
+            for h in range(2):
+                scores[b, h] = biased_scores(b, h, raw_scores(b, h))
         vw_got = keep.tile([P, B * 2 * DV], U32, name="vw_got", tag="kb_got0", align_bytes=64)
         nc.vector.tensor_copy(vw_got[:], vw_pool[:].bitcast(U32).indirect(v_offsets[:]))
 
         probs, totals = [], []
         for b in range(B):
-            banks = []
-            for h in range(2):
-                raw = psum.tile([P, 4, NQ], F32, name="raw", tag="turn", bufs=4)
-                for j in range(4):
-                    c0 = b * N + h * PASS + j * P
-                    nc.tensor.matmul_mx(
-                        out=raw[:, j, :],
-                        lhsT=kw_got[:, c0 : c0 + P].bitcast(FP8X4),
-                        lhsT_scale=ks_got[:, c0 : c0 + P],
-                        rhs=q_codes[:, b * NQ : (b + 1) * NQ].bitcast(FP8X4),
-                        rhs_scale=q_scales[:, b * NQ : (b + 1) * NQ],
-                        start=True,
-                        stop=True,
-                    )
-                biased = keep.tile([P, 4, NQ], F32, name=f"biased{b}{h}")
-                for j in range(4):
-                    c = 4 * h + j
-                    nc.scalar.activation(
-                        biased[:, j, :], raw[:, j, :], ACT.Identity, bias=kb_cols[b][:, c : c + 1]
-                    )
-                bank = psum.tile([P, PASS], F32, name="score", tag="score", bufs=4)
-                for j in range(4):
-                    nc.tensor.transpose(bank[:, j * P : (j + 1) * P], biased[:, j, :], ident[:])
-                banks.append(bank)
+            banks = [scores[b, h] for h in range(2)]
             half_max = keep.tile([P, 2], F32, name=f"half_max{b}")
             for h in range(2):
                 nc.vector.tensor_reduce(half_max[:, h : h + 1], banks[h][:], AXIS.X, ALU.max)

@@ -39,7 +39,6 @@ def tile_attend_pkv8_soft_kb_kernel(
         v_offsets = lists.tile([P, B * 2 * DV // LIST], U16, name="v_offsets")
 
         ks_pool = keep.tile([P, T // 4], I32, name="ks_pool", align_bytes=64)
-        kb_pool = keep.tile([P, T], F32, name="kb_pool", align_bytes=64)
         kw_pool = keep.tile([P, T], I32, name="kw_pool", align_bytes=64)
         vw_pool = keep.tile([P, PAGES * DV], I32, name="vw_pool", align_bytes=64)
         vs_pool = keep.tile([P, T], F32, name="vs_pool", align_bytes=64)
@@ -49,24 +48,27 @@ def tile_attend_pkv8_soft_kb_kernel(
         warm_out = keep.tile([P, 1], F32, name="warm_out")
         ident = keep.tile([P, P], F32, name="ident")
 
+        kb_pool = keep.tile([P, T], F32, name="kb_pool", align_bytes=64)
+        nc.vector.memset(ident[:], 0.0)
         nc.vector.memset(ks_pool[:], 0)
         nc.vector.memset(warm[:], 0.0)
-        nc.vector.memset(ident[:], 0.0)
-        nc.vector.memset(kb_pool[:], 0.0)
-        nc.vector.memset(vsc_pool[:], 0)
         make_identity(nc, ident[:], nomemset=True)
+        nc.vector.memset(kb_pool[:].bitcast(I32), 0)
+        nc.vector.memset(vsc_pool[:], 0)
+        vs_rows = keep.tile([P, P], F32, name="vs_rows")
 
         def load_queries(b):
             nc.sync.dma_start(q_raw[b][:], qT[b].rearrange("(p j) q -> p j q", j=PACK))
 
         nc.sync.dma_start(offsets[:], offs)
-        nc.sync.dma_start(v_offsets[:], voffs)
+        nc.sync.dma_start(vs_rows[:], vs[0:4, :].rearrange("r (c n) -> (r c) n", n=P))
         load_queries(0)
         ks_rows = k_scales[0].bitcast(I32)
         for r in range(4):
             nc.sync.dma_start(ks_pool[r:P:32, :], ks_rows[r:16:4, :])
         kw_rows = k_words[0].rearrange("p t r -> p (t r)").bitcast(I32)
         nc.sync.dma_start(kw_pool[:, : T // 2], kw_rows[:, : T // 2])
+        nc.sync.dma_start(v_offsets[:], voffs)
         nc.sync.dma_start(kb_pool[BIAS_ROW : BIAS_ROW + 1, :], kb[0:1, :])
         nc.sync.dma_start(kw_pool[:, T // 2 :], kw_rows[:, T // 2 :])
         load_queries(1)
@@ -74,7 +76,6 @@ def tile_attend_pkv8_soft_kb_kernel(
             vw_pool[:].rearrange("p (u e) -> p u e", u=PAGES),
             v_words.rearrange("u p e r -> p u (e r)").bitcast(I32),
         )
-        nc.sync.dma_start(vs_pool[:], vs)
         vsc_rows = v_scales.bitcast(I32).rearrange("u f c -> f u c")
         for r in range(4):
             nc.sync.dma_start(
@@ -82,10 +83,23 @@ def tile_attend_pkv8_soft_kb_kernel(
             )
         nc.scalar.activation(warm_out[:], warm[:], ACT.Exp)
 
-        for i in range(6):
-            idle = psum.tile([P, 4, P], F32, name="idle", tag="turn", bufs=4)
-            for j in range(4):
-                nc.tensor.transpose(idle[:, j, :], ident[:], ident[:])
+        def spread_token_scales():
+            turned = psum.tile([P, P], F32, name="vs_turned", tag="turn", bufs=4)
+            nc.tensor.transpose(turned[:], vs_rows[:], ident[:])
+            vs_cols = keep.tile([P, T // P], F32, name="vs_cols")
+            nc.scalar.activation(vs_cols[:], turned[:, : T // P], ACT.Copy)
+            for g in range(T // PASS):
+                spread = psum.tile([P, 4, P], F32, name="spread", tag="turn", bufs=4)
+                for j in range(4):
+                    c = 4 * g + j
+                    nc.tensor.transpose(
+                        spread[:, j, :], vs_cols[:, c : c + 1].to_broadcast([P, P]), ident[:]
+                    )
+                nc.scalar.activation(
+                    vs_pool[:, g * PASS : (g + 1) * PASS],
+                    spread[:].rearrange("p j n -> p (j n)"),
+                    ACT.Copy,
+                )
 
         def quantise_queries(b):
             q_bf = keep.tile([P, NQ, PACK], BF16, name=f"q_bf{b}", align_bytes=64)
@@ -153,6 +167,7 @@ def tile_attend_pkv8_soft_kb_kernel(
         for b in range(B):
             if b == 0:
                 queries[b] = quantise_queries(b)
+                spread_token_scales()
             kb_cols[b] = gather_bias(b, "kb_got0" if b == 0 else "kw_got00")
             if b == 1:
                 queries[b] = quantise_queries(b)
@@ -160,10 +175,9 @@ def tile_attend_pkv8_soft_kb_kernel(
                 kw_got[b, h] = gather_keys(b, h)
             for h in range(2):
                 scores[b, h] = biased_scores(b, h, raw_scores(b, h))
-        vw_got = keep.tile([P, B * 2 * DV], U32, name="vw_got", tag="kb_got0", align_bytes=64)
-        nc.vector.tensor_copy(vw_got[:], vw_pool[:].bitcast(U32).indirect(v_offsets[:]))
 
-        probs, totals = [], []
+        probs = []
+        half_totals = keep.tile([P, B, 2], F32, name="half_totals")
         for b in range(B):
             banks = [scores[b, h] for h in range(2)]
             half_max = keep.tile([P, 2], F32, name=f"half_max{b}")
@@ -172,39 +186,49 @@ def tile_attend_pkv8_soft_kb_kernel(
             neg_max = keep.tile([P, 1], F32, name=f"neg_max{b}")
             nc.vector.tensor_reduce(neg_max[:], half_max[:], AXIS.X, ALU.max, negate=True)
             p = keep.tile([P, N], F32, name=f"p{b}", tag=f"p{b}", align_bytes=64)
-            half_total = keep.tile([P, 2], F32, name=f"half_total{b}")
             for h in range(2):
                 nc.scalar.activation(
                     p[:, h * PASS : (h + 1) * PASS],
                     banks[h][:],
                     ACT.Exp,
                     bias=neg_max[:],
-                    accum_out=half_total[:, h : h + 1],
+                    accum_out=half_totals[:, b, h : h + 1],
                 )
             probs.append(p)
-            totals.append(half_total)
 
         grouped = {}
         for b in range(B):
             for h in range(2):
                 s0 = b * N + h * PASS
                 w = keep.tile([P, PASS], F32, name=f"w{b}{h}")
-                nc.vector.tensor_tensor(
-                    w[:],
-                    vs_pool[:].indirect(offsets[:, s0 // LIST : (s0 + PASS) // LIST]),
-                    probs[b][:, h * PASS : (h + 1) * PASS],
-                    ALU.mult,
-                )
                 w_bf = keep.tile([P, 2, P, 2], BF16, name=f"w_bf{b}{h}")
-                nc.scalar.copy(w_bf[:], w[:].rearrange("q (p u e) -> q u p e", u=2, e=2))
+                piece = PASS // 2 if (b, h) == (B - 1, 1) else PASS
+                for c0 in range(0, PASS, piece):
+                    nc.vector.tensor_tensor(
+                        w[:, c0 : c0 + piece],
+                        vs_pool[:].indirect(offsets[:, (s0 + c0) // LIST : (s0 + c0 + piece) // LIST]),
+                        probs[b][:, h * PASS + c0 : h * PASS + c0 + piece],
+                        ALU.mult,
+                    )
+                    nc.scalar.copy(
+                        w_bf[:, :, c0 // PACK : (c0 + piece) // PACK, :],
+                        w[:, c0 : c0 + piece].rearrange("q (p u e) -> q u p e", u=2, e=2),
+                    )
                 pairs = w_bf[:].rearrange("q u p e -> q (u p e)").bitcast(F32)
                 turned = psum.tile([P, 2, NQ], F32, name="w_turned", tag="turn", bufs=4)
                 for u in range(2):
                     nc.tensor.transpose(turned[:, u, :], pairs[:, u * P : (u + 1) * P], ident[:])
                 grouped[b, h] = turned
 
-        vsc_got = keep.tile([P, B * 2 * DV], U8, name="vsc_got", tag="p0", align_bytes=64)
+        vw_got = keep.tile([P, B * 2 * DV], U32, name="vw_got", tag="kb_got0", align_bytes=64)
+        nc.vector.tensor_copy(vw_got[:], vw_pool[:].bitcast(U32).indirect(v_offsets[:]))
+        vsc_got = keep.tile([P, B * 2 * DV], U8, name="vsc_got", tag="kw_got01", align_bytes=64)
         nc.vector.tensor_copy(vsc_got[:], vsc_pool[:].bitcast(U8).indirect(v_offsets[:]))
+
+        total = keep.tile([P, B], F32, name="total")
+        nc.vector.tensor_reduce(total[:], half_totals[:], AXIS.X, ALU.add)
+        inverse = keep.tile([P, B], F32, name="inverse")
+        nc.vector.reciprocal(inverse[:], total[:])
 
         for b in range(B):
             y = psum.tile([P, DV], F32, name="y", tag="score", bufs=4)
@@ -230,10 +254,6 @@ def tile_attend_pkv8_soft_kb_kernel(
                     start=(h == 0),
                     stop=(h == 1),
                 )
-            total = keep.tile([P, 1], F32, name=f"total{b}")
-            nc.vector.tensor_reduce(total[:], totals[b][:], AXIS.X, ALU.add)
-            inverse = keep.tile([P, 1], F32, name=f"inverse{b}")
-            nc.vector.reciprocal(inverse[:], total[:])
             result = keep.tile([P, DV], F32, name=f"result{b}")
-            nc.scalar.activation(result[:], y[:], ACT.Copy, scale=inverse[:])
+            nc.scalar.activation(result[:], y[:], ACT.Copy, scale=inverse[:, b : b + 1])
             nc.sync.dma_start(out[b], result[:])

@@ -49,11 +49,11 @@ def tile_attend_pkv8_soft_kb_kernel(
         ident = keep.tile([P, P], F32, name="ident")
 
         kb_pool = keep.tile([P, T], F32, name="kb_pool", align_bytes=64)
-        nc.vector.memset(ident[:], 0.0)
         nc.vector.memset(ks_pool[:], 0)
         nc.vector.memset(warm[:], 0.0)
-        make_identity(nc, ident[:], nomemset=True)
-        nc.vector.memset(kb_pool[:].bitcast(I32), 0)
+        make_identity(nc, ident[:])
+        nc.vector.memset(kb_pool[:, :2560].bitcast(I32), 0)
+        nc.gpsimd.memset(kb_pool[:, 2560:].bitcast(I32), 0)
         nc.vector.memset(vsc_pool[:], 0)
         vs_rows = keep.tile([P, P], F32, name="vs_rows")
 
@@ -163,12 +163,11 @@ def tile_attend_pkv8_soft_kb_kernel(
         ks_got = keep.tile([P, B * N], U8, name="ks_got", align_bytes=64)
         nc.vector.tensor_copy(ks_got[:], ks_pool[:].bitcast(U8).indirect(offsets[:]))
 
-        queries, kb_cols, kw_got, scores = {}, {}, {}, {}
+        queries, kw_got, scores = {}, {}, {}
+        queries[0] = quantise_queries(0)
+        spread_token_scales()
+        kb_cols = [gather_bias(b, f"kb_got{b}") for b in range(B)]
         for b in range(B):
-            if b == 0:
-                queries[b] = quantise_queries(b)
-                spread_token_scales()
-            kb_cols[b] = gather_bias(b, "kb_got0" if b == 0 else "kw_got00")
             if b == 1:
                 queries[b] = quantise_queries(b)
             for h in range(2):

@@ -21,7 +21,8 @@ ALU = mybir.AluOpType
 ACT = mybir.ActivationFunctionType
 AXIS = mybir.AxisListType
 
-BIAS_ROW = 16
+ROW = P - 1
+ON_SCALAR = ((0, 0), (0, 1))
 
 FLOPS = 2 * B * NQ * N * (D + DV)
 
@@ -35,43 +36,46 @@ def tile_attend_pkv8_soft_kb_kernel(
         keep = ctx.enter_context(tc.tile_pool(name="keep", bufs=1))
         psum = ctx.enter_context(tc.psum_pool(name="psum", bufs=1))
 
+        def sb(shape, dtype, name, tag=None):
+            return keep.tile(shape, dtype, name=name, tag=tag or name, align_bytes=64)
+
         offsets = lists.tile([P, B * N // LIST], U16, name="offsets")
         v_offsets = lists.tile([P, B * 2 * DV // LIST], U16, name="v_offsets")
 
-        ks_pool = keep.tile([P, T // 4], I32, name="ks_pool", align_bytes=64)
-        kw_pool = keep.tile([P, T], I32, name="kw_pool", align_bytes=64)
-        vw_pool = keep.tile([P, PAGES * DV], I32, name="vw_pool", align_bytes=64)
-        vs_pool = keep.tile([P, T], F32, name="vs_pool", align_bytes=64)
-        vsc_pool = keep.tile([P, PAGES * DV // 4], I32, name="vsc_pool", align_bytes=64)
-        q_raw = [keep.tile([P, PACK, NQ], F32, name=f"q_raw{b}") for b in range(B)]
-        warm = keep.tile([P, 1], F32, name="warm")
-        warm_out = keep.tile([P, 1], F32, name="warm_out")
-        ident = keep.tile([P, P], F32, name="ident")
+        ks_pool = sb([P, T // 4], I32, "ks_pool")
+        kw_pool = sb([P, T], I32, "kw_pool")
+        vw_pool = sb([P, PAGES * DV], I32, "vw_pool")
+        vs_pool = sb([P, T], F32, "vs_pool")
+        kb_pool = sb([P, T], F32, "kb_pool")
+        vsc_pool = sb([P, PAGES * DV // 4], I32, "vsc_pool")
+        q_raw = [sb([P, PACK, NQ], F32, f"q_raw{b}") for b in range(B)]
+        warm = sb([P, 1], F32, "warm")
+        warm_out = sb([P, 1], F32, "warm_out")
+        ident = sb([P, P], F32, "ident")
 
-        kb_pool = keep.tile([P, T], F32, name="kb_pool", align_bytes=64)
-        nc.vector.memset(ks_pool[:], 0)
+        nc.gpsimd.memset(ks_pool[:], 0)
         nc.vector.memset(warm[:], 0.0)
+        nc.vector.memset(vs_pool[:ROW, :].bitcast(I32), 0)
         make_identity(nc, ident[:])
-        nc.vector.memset(kb_pool[:, :2560].bitcast(I32), 0)
-        nc.gpsimd.memset(kb_pool[:, 2560:].bitcast(I32), 0)
-        nc.vector.memset(vsc_pool[:], 0)
-        vs_rows = keep.tile([P, P], F32, name="vs_rows")
+        for c0 in range(0, T, 1024):
+            nc.gpsimd.memset(kb_pool[:ROW, c0 : c0 + 1024].bitcast(I32), 0)
+        nc.gpsimd.memset(vsc_pool[:], 0)
 
         def load_queries(b):
             nc.sync.dma_start(q_raw[b][:], qT[b].rearrange("(p j) q -> p j q", j=PACK))
 
         nc.sync.dma_start(offsets[:], offs)
-        nc.sync.dma_start(vs_rows[:], vs[0:4, :].rearrange("r (c n) -> (r c) n", n=P))
+        nc.sync.dma_start(vs_pool[ROW:, :], vs[0:1, :])
         load_queries(0)
         ks_rows = k_scales[0].bitcast(I32)
         for r in range(4):
             nc.sync.dma_start(ks_pool[r:P:32, :], ks_rows[r:16:4, :])
+        nc.sync.dma_start(kb_pool[ROW:, :], kb[0:1, :])
         kw_rows = k_words[0].rearrange("p t r -> p (t r)").bitcast(I32)
         nc.sync.dma_start(kw_pool[:, : T // 2], kw_rows[:, : T // 2])
-        nc.sync.dma_start(v_offsets[:], voffs)
-        nc.sync.dma_start(kb_pool[BIAS_ROW : BIAS_ROW + 1, :], kb[0:1, :])
         nc.sync.dma_start(kw_pool[:, T // 2 :], kw_rows[:, T // 2 :])
         load_queries(1)
+        nc.sync.dma_start(v_offsets[:], voffs)
         nc.sync.dma_start(
             vw_pool[:].rearrange("p (u e) -> p u e", u=PAGES),
             v_words.rearrange("u p e r -> p u (e r)").bitcast(I32),
@@ -83,58 +87,53 @@ def tile_attend_pkv8_soft_kb_kernel(
             )
         nc.scalar.activation(warm_out[:], warm[:], ACT.Exp)
 
-        def spread_token_scales():
-            turned = psum.tile([P, P], F32, name="vs_turned", tag="turn", bufs=4)
-            nc.tensor.transpose(turned[:], vs_rows[:], ident[:])
-            vs_cols = keep.tile([P, T // P], F32, name="vs_cols")
-            nc.scalar.activation(vs_cols[:], turned[:, : T // P], ACT.Copy)
-            for g in range(T // PASS):
-                spread = psum.tile([P, 4, P], F32, name="spread", tag="turn", bufs=4)
-                for j in range(4):
-                    c = 4 * g + j
-                    nc.tensor.transpose(
-                        spread[:, j, :], vs_cols[:, c : c + 1].to_broadcast([P, P]), ident[:]
-                    )
-                nc.scalar.activation(
-                    vs_pool[:, g * PASS : (g + 1) * PASS],
-                    spread[:].rearrange("p j n -> p (j n)"),
-                    ACT.Copy,
-                )
+        def entries(s0, n):
+            return offsets[:, s0 // LIST : (s0 + n) // LIST]
 
         def quantise_queries(b):
-            q_bf = keep.tile([P, NQ, PACK], BF16, name=f"q_bf{b}", align_bytes=64)
+            q_bf = sb([P, NQ, PACK], BF16, f"q_bf{b}")
             nc.scalar.copy(q_bf[:], q_raw[b][:].rearrange("p j q -> p q j"))
-            codes = keep.tile([P, NQ], U32, name=f"q_codes{b}", align_bytes=64)
-            scales = keep.tile([P, NQ], U8, name=f"q_scales{b}", align_bytes=64)
+            codes = sb([P, NQ], U32, f"q_codes{b}")
+            scales = sb([P, NQ], U8, f"q_scales{b}")
             nc.vector.quantize_mx(
                 out=codes[:].bitcast(FP8X4), scales=scales[:], in_=q_bf[:].rearrange("p q j -> p (q j)")
             )
             return codes, scales
 
-        def gather_bias(b, tag):
-            kb_got = keep.tile([P, N], F32, name=f"kb_got{b}", tag=tag, align_bytes=64)
-            nc.vector.tensor_copy(
-                kb_got[:], kb_pool[:].indirect(offsets[:, b * N // LIST : (b + 1) * N // LIST])
-            )
-            kb_col = keep.tile([P, N // P], F32, name=f"kb_col{b}")
+        def row_to_columns(name, blocks):
+            turned = psum.tile([P, 4, P], F32, name="turned", tag="turn", bufs=3)
+            for j in range(4):
+                nc.tensor.transpose(turned[:, j, :], blocks[j], ident[:])
+            cols = sb([P, 4], F32, name)
+            nc.scalar.copy(cols[:], turned[:, :, ROW])
+            return cols
+
+        def gather_token_scales(b, tag, piece):
+            got = sb([P, N], F32, f"vs_got{b}", tag)
+            for c0 in range(0, N, piece):
+                nc.vector.tensor_copy(
+                    got[:, c0 : c0 + piece], vs_pool[:].indirect(entries(b * N + c0, piece))
+                )
             for h in range(2):
-                turned = psum.tile([P, 4, P], F32, name="turned", tag="turn", bufs=4)
-                for j in range(4):
-                    c0 = (4 * h + j) * P
-                    nc.tensor.transpose(turned[:, j, :], kb_got[:, c0 : c0 + P], ident[:])
-                nc.scalar.copy(kb_col[:, 4 * h : 4 * h + 4], turned[:, :, BIAS_ROW])
-            return kb_col
+                vs_cols[b, h] = row_to_columns(
+                    f"vs_cols{b}{h}", [got[:, h * PASS + t : (h + 1) * PASS : PACK] for t in range(PACK)]
+                )
 
-        def gather_keys(b, h):
-            s0 = b * N + h * PASS
-            got = keep.tile([P, PASS], U32, name=f"kw_got{b}{h}", tag=f"kw_got{b}{h}", align_bytes=64)
-            nc.vector.tensor_copy(
-                got[:], kw_pool[:].bitcast(U32).indirect(offsets[:, s0 // LIST : (s0 + PASS) // LIST])
-            )
-            return got
+        def gather_bias(b, tag):
+            got = sb([P, N], F32, f"kb_got{b}", tag)
+            nc.vector.tensor_copy(got[:], kb_pool[:].indirect(entries(b * N, N)))
+            for h in range(2):
+                kb_cols[b, h] = row_to_columns(
+                    f"kb_cols{b}{h}", [got[:, (4 * h + j) * P : (4 * h + j + 1) * P] for j in range(4)]
+                )
 
-        def raw_scores(b, h):
-            raw = psum.tile([P, 4, NQ], F32, name="raw", tag="turn", bufs=4)
+        def gather_keys(b, h, tag):
+            got = sb([P, PASS], U32, f"kw_got{b}{h}", tag)
+            nc.vector.tensor_copy(got[:], kw_pool[:].bitcast(U32).indirect(entries(b * N + h * PASS, PASS)))
+            kw_got[b, h] = got
+
+        def score_page(b, h):
+            raw = psum.tile([P, 4, NQ], F32, name="raw", tag="turn", bufs=3)
             for j in range(4):
                 c0 = b * N + h * PASS + j * P
                 nc.tensor.matmul_mx(
@@ -146,102 +145,112 @@ def tile_attend_pkv8_soft_kb_kernel(
                     start=True,
                     stop=True,
                 )
-            return raw
-
-        def biased_scores(b, h, raw):
-            biased = keep.tile([P, 4, NQ], F32, name=f"biased{b}{h}")
+            biased = sb([P, 4, NQ], F32, f"biased{b}{h}")
             for j in range(4):
-                c = 4 * h + j
                 nc.scalar.activation(
-                    biased[:, j, :], raw[:, j, :], ACT.Identity, bias=kb_cols[b][:, c : c + 1]
+                    biased[:, j, :], raw[:, j, :], ACT.Identity, bias=kb_cols[b, h][:, j : j + 1]
                 )
-            bank = psum.tile([P, PASS], F32, name="score", tag="score", bufs=4)
+            bank = psum.tile([P, PASS], F32, name="score", tag="score", bufs=3)
             for j in range(4):
                 nc.tensor.transpose(bank[:, j * P : (j + 1) * P], biased[:, j, :], ident[:])
-            return bank
+            negated = sb([P, PASS], F32, f"negated{b}{h}")
+            least = sb([P, 1], F32, f"least{b}{h}")
+            nc.vector.tensor_scalar(
+                negated[:],
+                bank[:],
+                -1.0,
+                None if h == 0 else neg_max[b, 0][:],
+                ALU.mult,
+                ALU.min,
+                accum_out=least[:],
+            )
+            neg_scores[b, h] = negated
+            neg_max[b, h] = least
 
-        ks_got = keep.tile([P, B * N], U8, name="ks_got", align_bytes=64)
-        nc.vector.tensor_copy(ks_got[:], ks_pool[:].bitcast(U8).indirect(offsets[:]))
+        def weigh_page(b, h):
+            p = sb([P, PACK, P], F32, f"p{b}{h}")
+            total = sb([P, 1], F32, f"total{b}{h}")
+            nc.scalar.activation(
+                p[:].rearrange("q t s -> q s t"),
+                neg_scores[b, h][:].rearrange("q (s t) -> q s t", t=PACK),
+                ACT.Exp,
+                bias=neg_max[b, 1][:],
+                scale=-1.0,
+                accum_out=total[:],
+            )
+            page_totals[b, h] = total
+            turned = psum.tile([P, PACK, NQ], F32, name="p_turned", tag="score", bufs=3)
+            for t in range(PACK):
+                nc.tensor.transpose(turned[:, t, :], p[:, t, :], ident[:])
+            p_turned[b, h] = turned
 
-        queries, kw_got, scores = {}, {}, {}
-        queries[0] = quantise_queries(0)
-        spread_token_scales()
-        kb_cols = [gather_bias(b, f"kb_got{b}") for b in range(B)]
-        for b in range(B):
-            if b == 1:
-                queries[b] = quantise_queries(b)
-            for h in range(2):
-                kw_got[b, h] = gather_keys(b, h)
-            for h in range(2):
-                scores[b, h] = biased_scores(b, h, raw_scores(b, h))
-
-        probs = []
-        half_totals = keep.tile([P, B, 2], F32, name="half_totals")
-        for b in range(B):
-            banks = [scores[b, h] for h in range(2)]
-            half_max = keep.tile([P, 2], F32, name=f"half_max{b}")
-            for h in range(2):
-                nc.vector.tensor_reduce(half_max[:, h : h + 1], banks[h][:], AXIS.X, ALU.max)
-            neg_max = keep.tile([P, 1], F32, name=f"neg_max{b}")
-            nc.vector.tensor_reduce(neg_max[:], half_max[:], AXIS.X, ALU.max, negate=True)
-            p = keep.tile([P, N], F32, name=f"p{b}", tag=f"p{b}", align_bytes=64)
-            for h in range(2):
-                nc.scalar.activation(
-                    p[:, h * PASS : (h + 1) * PASS],
-                    banks[h][:],
-                    ACT.Exp,
-                    bias=neg_max[:],
-                    accum_out=half_totals[:, b, h : h + 1],
+        def scale_page(b, h):
+            turned = p_turned[b, h]
+            w = sb([P, NQ, PACK], BF16, f"w{b}{h}")
+            if (b, h) in ON_SCALAR:
+                planes = sb([P, PACK, NQ], BF16, f"w_planes{b}{h}")
+                for t in range(PACK):
+                    nc.scalar.activation(
+                        planes[:, t, :], turned[:, t, :], ACT.Copy, scale=vs_cols[b, h][:, t : t + 1]
+                    )
+                nc.scalar.copy(w[:], planes[:].rearrange("s t q -> s q t"))
+            else:
+                nc.vector.tensor_tensor(
+                    w[:],
+                    turned[:].rearrange("s t q -> s q t"),
+                    vs_cols[b, h][:].unsqueeze(1).to_broadcast([P, NQ, PACK]),
+                    ALU.mult,
                 )
-            probs.append(p)
+            weights[b, h] = w
 
-        grouped = {}
-        for b in range(B):
-            for h in range(2):
-                s0 = b * N + h * PASS
-                w = keep.tile([P, PASS], F32, name=f"w{b}{h}")
-                w_bf = keep.tile([P, 2, P, 2], BF16, name=f"w_bf{b}{h}")
-                piece = PASS // 2 if (b, h) == (B - 1, 1) else PASS
-                for c0 in range(0, PASS, piece):
-                    nc.vector.tensor_tensor(
-                        w[:, c0 : c0 + piece],
-                        vs_pool[:].indirect(offsets[:, (s0 + c0) // LIST : (s0 + c0 + piece) // LIST]),
-                        probs[b][:, h * PASS + c0 : h * PASS + c0 + piece],
-                        ALU.mult,
-                    )
-                    nc.scalar.copy(
-                        w_bf[:, :, c0 // PACK : (c0 + piece) // PACK, :],
-                        w[:, c0 : c0 + piece].rearrange("q (p u e) -> q u p e", u=2, e=2),
-                    )
-                pairs = w_bf[:].rearrange("q u p e -> q (u p e)").bitcast(F32)
-                turned = psum.tile([P, 2, NQ], F32, name="w_turned", tag="turn", bufs=4)
-                for u in range(2):
-                    nc.tensor.transpose(turned[:, u, :], pairs[:, u * P : (u + 1) * P], ident[:])
-                grouped[b, h] = turned
+        queries, kw_got, vs_cols, kb_cols = {}, {}, {}, {}
+        neg_scores, neg_max, page_totals, p_turned, weights = {}, {}, {}, {}, {}
 
-        vw_got = keep.tile([P, B * 2 * DV], U32, name="vw_got", tag="kb_got0", align_bytes=64)
+        gather_token_scales(0, None, N)
+        ks_got = sb([P, B * N], U8, "ks_got")
+        nc.vector.tensor_copy(ks_got[:], ks_pool[:].bitcast(U8).indirect(offsets[:]))
+        gather_bias(0, None)
+        queries[0] = quantise_queries(0)
+        gather_keys(0, 0, "first_keys")
+        gather_keys(0, 1, None)
+        queries[1] = quantise_queries(1)
+        score_page(0, 0)
+        score_page(0, 1)
+        gather_bias(1, "first_keys")
+        gather_keys(1, 0, "kb_pool")
+        gather_keys(1, 1, "biased01")
+        score_page(1, 0)
+        weigh_page(0, 0)
+        weigh_page(0, 1)
+        score_page(1, 1)
+        gather_token_scales(1, "kb_pool", PASS)
+        weigh_page(1, 0)
+        weigh_page(1, 1)
+
+        vw_got = sb([P, B * 2 * DV], U32, "vw_got", "biased11")
         nc.vector.tensor_copy(vw_got[:], vw_pool[:].bitcast(U32).indirect(v_offsets[:]))
-        vsc_got = keep.tile([P, B * 2 * DV], U8, name="vsc_got", tag="kw_got01", align_bytes=64)
+        vsc_got = sb([P, B * 2 * DV], U8, "vsc_got", "negated10")
         nc.vector.tensor_copy(vsc_got[:], vsc_pool[:].bitcast(U8).indirect(v_offsets[:]))
 
-        total = keep.tile([P, B], F32, name="total")
-        nc.vector.tensor_reduce(total[:], half_totals[:], AXIS.X, ALU.add)
-        inverse = keep.tile([P, B], F32, name="inverse")
-        nc.vector.reciprocal(inverse[:], total[:])
+        totals = sb([P, B], F32, "totals")
+        for b in range(B):
+            for h in range(2):
+                scale_page(b, h)
+            nc.scalar.activation(
+                totals[:, b : b + 1], page_totals[b, 0][:], ACT.Identity, bias=page_totals[b, 1][:]
+            )
+        inverse = sb([P, B], F32, "inverse")
+        nc.vector.reciprocal(inverse[:], totals[:])
 
         for b in range(B):
-            y = psum.tile([P, DV], F32, name="y", tag="score", bufs=4)
+            y = psum.tile([P, DV], F32, name="y", tag="y", bufs=2)
             for h in range(2):
-                w_grouped = keep.tile([P, NQ * PACK], BF16, name=f"w_grouped{b}{h}", align_bytes=64)
-                copy_out = nc.vector.tensor_copy if b == 0 else nc.scalar.copy
-                copy_out(
-                    w_grouped[:].bitcast(F32).rearrange("p (q u) -> p q u", u=2),
-                    grouped[b, h][:].rearrange("p u q -> p q u"),
-                )
-                w_codes = keep.tile([P, NQ], U32, name=f"w_codes{b}{h}", align_bytes=64)
-                w_scales = keep.tile([P, NQ], U8, name=f"w_scales{b}{h}", align_bytes=64)
+                w_codes = sb([P, NQ], U32, f"w_codes{b}{h}")
+                w_scales = sb([P, NQ], U8, f"w_scales{b}{h}")
                 nc.vector.quantize_mx(
-                    out=w_codes[:].bitcast(FP8X4), scales=w_scales[:], in_=w_grouped[:]
+                    out=w_codes[:].bitcast(FP8X4),
+                    scales=w_scales[:],
+                    in_=weights[b, h][:].rearrange("s q t -> s (q t)"),
                 )
                 page = slice((2 * b + h) * DV, (2 * b + h + 1) * DV)
                 nc.tensor.matmul_mx(
@@ -253,6 +262,6 @@ def tile_attend_pkv8_soft_kb_kernel(
                     start=(h == 0),
                     stop=(h == 1),
                 )
-            result = keep.tile([P, DV], F32, name=f"result{b}")
+            result = sb([P, DV], F32, f"result{b}")
             nc.scalar.activation(result[:], y[:], ACT.Copy, scale=inverse[:, b : b + 1])
             nc.sync.dma_start(out[b], result[:])

@@ -53,24 +53,24 @@ def tile_attend_pkv8_soft_kb_kernel(
         warm_out = sb([P, 1], F32, "warm_out")
         ident = sb([P, P], F32, "ident")
 
-        nc.gpsimd.memset(ks_pool[:], 0)
-        nc.vector.memset(warm[:], 0.0)
-        nc.vector.memset(vs_pool[:ROW, :].bitcast(I32), 0)
+        vs_dealt = sb([P, PAGES, PACK], F32, "vs_dealt")
+
         make_identity(nc, ident[:])
-        for c0 in range(0, T, 1024):
-            nc.gpsimd.memset(kb_pool[:ROW, c0 : c0 + 1024].bitcast(I32), 0)
-        nc.gpsimd.memset(vsc_pool[:], 0)
+        nc.vector.memset(ks_pool[:], 0)
+        nc.vector.memset(warm[:], 0.0)
+        nc.vector.memset(kb_pool[:ROW, :].bitcast(I32), 0)
+        nc.vector.memset(vsc_pool[:], 0)
 
         def load_queries(b):
             nc.sync.dma_start(q_raw[b][:], qT[b].rearrange("(p j) q -> p j q", j=PACK))
 
         nc.sync.dma_start(offsets[:], offs)
-        nc.sync.dma_start(vs_pool[ROW:, :], vs[0:1, :])
+        nc.sync.dma_start(vs_dealt[:], vs[0].rearrange("(u s t) -> s u t", u=PAGES, t=PACK))
+        nc.sync.dma_start(kb_pool[ROW:, :], kb[0:1, :])
         load_queries(0)
         ks_rows = k_scales[0].bitcast(I32)
         for r in range(4):
             nc.sync.dma_start(ks_pool[r:P:32, :], ks_rows[r:16:4, :])
-        nc.sync.dma_start(kb_pool[ROW:, :], kb[0:1, :])
         kw_rows = k_words[0].rearrange("p t r -> p (t r)").bitcast(I32)
         nc.sync.dma_start(kw_pool[:, : T // 2], kw_rows[:, : T // 2])
         nc.sync.dma_start(kw_pool[:, T // 2 :], kw_rows[:, T // 2 :])
@@ -89,6 +89,17 @@ def tile_attend_pkv8_soft_kb_kernel(
 
         def entries(s0, n):
             return offsets[:, s0 // LIST : (s0 + n) // LIST]
+
+        def spread_token_scales():
+            for u in range(PAGES):
+                spread = psum.tile([P, PACK, P], F32, name="spread", tag="score", bufs=3)
+                for t in range(PACK):
+                    nc.tensor.transpose(
+                        spread[:, t, :], vs_dealt[:, u, t : t + 1].to_broadcast([P, P]), ident[:]
+                    )
+                nc.scalar.activation(
+                    vs_pool[:, u * PASS : (u + 1) * PASS], spread[:].rearrange("p t s -> p (t s)"), ACT.Copy
+                )
 
         def quantise_queries(b):
             q_bf = sb([P, NQ, PACK], BF16, f"q_bf{b}")
@@ -116,7 +127,7 @@ def tile_attend_pkv8_soft_kb_kernel(
                 )
             for h in range(2):
                 vs_cols[b, h] = row_to_columns(
-                    f"vs_cols{b}{h}", [got[:, h * PASS + t : (h + 1) * PASS : PACK] for t in range(PACK)]
+                    f"vs_cols{b}{h}", [got[:, (4 * h + t) * P : (4 * h + t + 1) * P] for t in range(PACK)]
                 )
 
         def gather_bias(b, tag):
@@ -206,11 +217,12 @@ def tile_attend_pkv8_soft_kb_kernel(
         queries, kw_got, vs_cols, kb_cols = {}, {}, {}, {}
         neg_scores, neg_max, page_totals, p_turned, weights = {}, {}, {}, {}, {}
 
-        gather_token_scales(0, None, N)
+        spread_token_scales()
+        gather_bias(0, None)
         ks_got = sb([P, B * N], U8, "ks_got")
         nc.vector.tensor_copy(ks_got[:], ks_pool[:].bitcast(U8).indirect(offsets[:]))
-        gather_bias(0, None)
         queries[0] = quantise_queries(0)
+        gather_token_scales(0, None, N)
         gather_keys(0, 0, "first_keys")
         gather_keys(0, 1, None)
         queries[1] = quantise_queries(1)

@@ -22,7 +22,6 @@ ACT = mybir.ActivationFunctionType
 AXIS = mybir.AxisListType
 
 ROW = P - 1
-ON_SCALAR = ((0, 0), (0, 1))
 
 FLOPS = 2 * B * NQ * N * (D + DV)
 
@@ -119,17 +118,6 @@ def tile_attend_pkv8_soft_kb_kernel(
             nc.scalar.copy(cols[:], turned[:, :, ROW])
             return cols
 
-        def gather_token_scales(b, tag, piece):
-            got = sb([P, N], F32, f"vs_got{b}", tag)
-            for c0 in range(0, N, piece):
-                nc.vector.tensor_copy(
-                    got[:, c0 : c0 + piece], vs_pool[:].indirect(entries(b * N + c0, piece))
-                )
-            for h in range(2):
-                vs_cols[b, h] = row_to_columns(
-                    f"vs_cols{b}{h}", [got[:, (4 * h + t) * P : (4 * h + t + 1) * P] for t in range(PACK)]
-                )
-
         def gather_bias(b, tag):
             got = sb([P, N], F32, f"kb_got{b}", tag)
             nc.vector.tensor_copy(got[:], kb_pool[:].indirect(entries(b * N, N)))
@@ -190,39 +178,31 @@ def tile_attend_pkv8_soft_kb_kernel(
                 accum_out=total[:],
             )
             page_totals[b, h] = total
-            turned = psum.tile([P, PACK, NQ], F32, name="p_turned", tag="score", bufs=3)
-            for t in range(PACK):
-                nc.tensor.transpose(turned[:, t, :], p[:, t, :], ident[:])
-            p_turned[b, h] = turned
+            probs[b, h] = p
 
         def scale_page(b, h):
-            turned = p_turned[b, h]
+            w32 = sb([P, PASS], F32, f"w32{b}{h}")
+            nc.vector.tensor_tensor(
+                w32[:],
+                vs_pool[:].indirect(entries(b * N + h * PASS, PASS)),
+                probs[b, h][:].rearrange("q t s -> q (t s)"),
+                ALU.mult,
+            )
+            turned = psum.tile([P, PACK, NQ], F32, name="w_turned", tag="score", bufs=3)
+            for t in range(PACK):
+                nc.tensor.transpose(turned[:, t, :], w32[:, t * P : (t + 1) * P], ident[:])
             w = sb([P, NQ, PACK], BF16, f"w{b}{h}")
-            if (b, h) in ON_SCALAR:
-                planes = sb([P, PACK, NQ], BF16, f"w_planes{b}{h}")
-                for t in range(PACK):
-                    nc.scalar.activation(
-                        planes[:, t, :], turned[:, t, :], ACT.Copy, scale=vs_cols[b, h][:, t : t + 1]
-                    )
-                nc.scalar.copy(w[:], planes[:].rearrange("s t q -> s q t"))
-            else:
-                nc.vector.tensor_tensor(
-                    w[:],
-                    turned[:].rearrange("s t q -> s q t"),
-                    vs_cols[b, h][:].unsqueeze(1).to_broadcast([P, NQ, PACK]),
-                    ALU.mult,
-                )
+            nc.scalar.copy(w[:], turned[:].rearrange("s t q -> s q t"))
             weights[b, h] = w
 
-        queries, kw_got, vs_cols, kb_cols = {}, {}, {}, {}
-        neg_scores, neg_max, page_totals, p_turned, weights = {}, {}, {}, {}, {}
+        queries, kw_got, kb_cols = {}, {}, {}
+        neg_scores, neg_max, page_totals, probs, weights = {}, {}, {}, {}, {}
 
         spread_token_scales()
         gather_bias(0, None)
         ks_got = sb([P, B * N], U8, "ks_got")
         nc.vector.tensor_copy(ks_got[:], ks_pool[:].bitcast(U8).indirect(offsets[:]))
         queries[0] = quantise_queries(0)
-        gather_token_scales(0, None, N)
         gather_keys(0, 0, "first_keys")
         gather_keys(0, 1, None)
         queries[1] = quantise_queries(1)
@@ -231,23 +211,24 @@ def tile_attend_pkv8_soft_kb_kernel(
         gather_bias(1, "first_keys")
         gather_keys(1, 0, "kb_pool")
         gather_keys(1, 1, "biased01")
-        score_page(1, 0)
         weigh_page(0, 0)
         weigh_page(0, 1)
+        scale_page(0, 0)
+        score_page(1, 0)
+        scale_page(0, 1)
         score_page(1, 1)
-        gather_token_scales(1, "kb_pool", PASS)
         weigh_page(1, 0)
         weigh_page(1, 1)
 
         vw_got = sb([P, B * 2 * DV], U32, "vw_got", "biased11")
         nc.vector.tensor_copy(vw_got[:], vw_pool[:].bitcast(U32).indirect(v_offsets[:]))
-        vsc_got = sb([P, B * 2 * DV], U8, "vsc_got", "negated10")
+        scale_page(1, 0)
+        scale_page(1, 1)
+        vsc_got = sb([P, B * 2 * DV], U8, "vsc_got", "negated11")
         nc.vector.tensor_copy(vsc_got[:], vsc_pool[:].bitcast(U8).indirect(v_offsets[:]))
 
         totals = sb([P, B], F32, "totals")
         for b in range(B):
-            for h in range(2):
-                scale_page(b, h)
             nc.scalar.activation(
                 totals[:, b : b + 1], page_totals[b, 0][:], ACT.Identity, bias=page_totals[b, 1][:]
             )

@@ -21,7 +21,6 @@ ALU = mybir.AluOpType
 ACT = mybir.ActivationFunctionType
 AXIS = mybir.AxisListType
 
-ROW = P - 1
 
 FLOPS = 2 * B * NQ * N * (D + DV)
 
@@ -53,26 +52,27 @@ def tile_attend_pkv8_soft_kb_kernel(
         ident = sb([P, P], F32, "ident")
 
         vs_dealt = sb([P, PAGES, PACK], F32, "vs_dealt")
+        kb_dealt = sb([P, PAGES, PACK], F32, "kb_dealt")
 
         make_identity(nc, ident[:])
         nc.vector.memset(ks_pool[:], 0)
         nc.vector.memset(warm[:], 0.0)
-        nc.vector.memset(kb_pool[:ROW, :].bitcast(I32), 0)
         nc.vector.memset(vsc_pool[:], 0)
+
+        def load_dealt(tile, source):
+            nc.sync.dma_start(tile[:], source[0].rearrange("(u s t) -> s u t", u=PAGES, t=PACK))
 
         def load_queries(b):
             nc.sync.dma_start(q_raw[b][:], qT[b].rearrange("(p j) q -> p j q", j=PACK))
 
         nc.sync.dma_start(offsets[:], offs)
-        nc.sync.dma_start(vs_dealt[:], vs[0].rearrange("(u s t) -> s u t", u=PAGES, t=PACK))
-        nc.sync.dma_start(kb_pool[ROW:, :], kb[0:1, :])
+        load_dealt(kb_dealt, kb)
         load_queries(0)
         ks_rows = k_scales[0].bitcast(I32)
         for r in range(4):
             nc.sync.dma_start(ks_pool[r:P:32, :], ks_rows[r:16:4, :])
-        kw_rows = k_words[0].rearrange("p t r -> p (t r)").bitcast(I32)
-        nc.sync.dma_start(kw_pool[:, : T // 2], kw_rows[:, : T // 2])
-        nc.sync.dma_start(kw_pool[:, T // 2 :], kw_rows[:, T // 2 :])
+        nc.sync.dma_start(kw_pool[:], k_words[0].rearrange("p t r -> p (t r)").bitcast(I32))
+        load_dealt(vs_dealt, vs)
         load_queries(1)
         nc.sync.dma_start(v_offsets[:], voffs)
         nc.sync.dma_start(
@@ -89,15 +89,13 @@ def tile_attend_pkv8_soft_kb_kernel(
         def entries(s0, n):
             return offsets[:, s0 // LIST : (s0 + n) // LIST]
 
-        def spread_token_scales():
+        def spread(dealt, window):
             for u in range(PAGES):
-                spread = psum.tile([P, PACK, P], F32, name="spread", tag="score", bufs=3)
+                bank = psum.tile([P, PACK, P], F32, name="spread", tag="turn", bufs=3)
                 for t in range(PACK):
-                    nc.tensor.transpose(
-                        spread[:, t, :], vs_dealt[:, u, t : t + 1].to_broadcast([P, P]), ident[:]
-                    )
+                    nc.tensor.transpose(bank[:, t, :], dealt[:, u, t : t + 1].to_broadcast([P, P]), ident[:])
                 nc.scalar.activation(
-                    vs_pool[:, u * PASS : (u + 1) * PASS], spread[:].rearrange("p t s -> p (t s)"), ACT.Copy
+                    window[:, u * PASS : (u + 1) * PASS], bank[:].rearrange("p t s -> p (t s)"), ACT.Copy
                 )
 
         def quantise_queries(b):
@@ -110,71 +108,53 @@ def tile_attend_pkv8_soft_kb_kernel(
             )
             return codes, scales
 
-        def row_to_columns(name, blocks):
-            turned = psum.tile([P, 4, P], F32, name="turned", tag="turn", bufs=3)
-            for j in range(4):
-                nc.tensor.transpose(turned[:, j, :], blocks[j], ident[:])
-            cols = sb([P, 4], F32, name)
-            nc.scalar.copy(cols[:], turned[:, :, ROW])
-            return cols
-
-        def gather_bias(b, tag):
-            got = sb([P, N], F32, f"kb_got{b}", tag)
-            nc.vector.tensor_copy(got[:], kb_pool[:].indirect(entries(b * N, N)))
-            for h in range(2):
-                kb_cols[b, h] = row_to_columns(
-                    f"kb_cols{b}{h}", [got[:, (4 * h + j) * P : (4 * h + j + 1) * P] for j in range(4)]
-                )
-
-        def gather_keys(b, h, tag):
-            got = sb([P, PASS], U32, f"kw_got{b}{h}", tag)
+        def gather_keys(b, h):
+            got = sb([P, PASS], U32, f"kw_got{b}{h}")
             nc.vector.tensor_copy(got[:], kw_pool[:].bitcast(U32).indirect(entries(b * N + h * PASS, PASS)))
             kw_got[b, h] = got
 
-        def score_page(b, h):
-            raw = psum.tile([P, 4, NQ], F32, name="raw", tag="turn", bufs=3)
-            for j in range(4):
-                c0 = b * N + h * PASS + j * P
+        def raw_scores(b):
+            raw = sb([P, 2, PACK, P], F32, f"raw{b}")
+            for h in range(2):
+                s0 = b * N + h * PASS
+                bank = psum.tile([P, PASS], F32, name="score", tag="score", bufs=3)
                 nc.tensor.matmul_mx(
-                    out=raw[:, j, :],
-                    lhsT=kw_got[b, h][:, j * P : (j + 1) * P].bitcast(FP8X4),
-                    lhsT_scale=ks_got[:, c0 : c0 + P],
-                    rhs=queries[b][0][:].bitcast(FP8X4),
-                    rhs_scale=queries[b][1][:],
+                    out=bank[:],
+                    lhsT=queries[b][0][:].bitcast(FP8X4),
+                    lhsT_scale=queries[b][1][:],
+                    rhs=kw_got[b, h][:].bitcast(FP8X4),
+                    rhs_scale=ks_got[:, s0 : s0 + PASS],
                     start=True,
                     stop=True,
                 )
-            biased = sb([P, 4, NQ], F32, f"biased{b}{h}")
-            for j in range(4):
-                nc.scalar.activation(
-                    biased[:, j, :], raw[:, j, :], ACT.Identity, bias=kb_cols[b, h][:, j : j + 1]
+                nc.scalar.copy(
+                    raw[:, h].rearrange("q t s -> q s t"), bank[:].rearrange("q (s t) -> q s t", t=PACK)
                 )
-            bank = psum.tile([P, PASS], F32, name="score", tag="score", bufs=3)
-            for j in range(4):
-                nc.tensor.transpose(bank[:, j * P : (j + 1) * P], biased[:, j, :], ident[:])
-            negated = sb([P, PASS], F32, f"negated{b}{h}")
-            least = sb([P, 1], F32, f"least{b}{h}")
-            nc.vector.tensor_scalar(
-                negated[:],
-                bank[:],
-                -1.0,
-                None if h == 0 else neg_max[b, 0][:],
-                ALU.mult,
-                ALU.min,
-                accum_out=least[:],
+            return raw
+
+        def add_bias(b, raw):
+            biased = sb([P, N], F32, f"biased{b}")
+            nc.vector.tensor_tensor(
+                biased[:],
+                kb_pool[:].indirect(entries(b * N, N)),
+                raw[:].rearrange("q h t s -> q (h t s)"),
+                ALU.add,
             )
-            neg_scores[b, h] = negated
-            neg_max[b, h] = least
+            scores[b] = biased
+
+        def row_maximum(b):
+            least = sb([P, 1], F32, f"neg_max{b}")
+            nc.vector.tensor_reduce(least[:], scores[b][:], AXIS.X, ALU.max, negate=True)
+            neg_max[b] = least
 
         def weigh_page(b, h):
             p = sb([P, PACK, P], F32, f"p{b}{h}")
             total = sb([P, 1], F32, f"total{b}{h}")
             nc.scalar.activation(
-                p[:].rearrange("q t s -> q s t"),
-                neg_scores[b, h][:].rearrange("q (s t) -> q s t", t=PACK),
+                p[:].rearrange("q t s -> q (t s)"),
+                scores[b][:, h * PASS : (h + 1) * PASS],
                 ACT.Exp,
-                bias=neg_max[b, 1][:],
-                scale=-1.0,
+                bias=neg_max[b][:],
                 accum_out=total[:],
             )
             page_totals[b, h] = total
@@ -195,36 +175,31 @@ def tile_attend_pkv8_soft_kb_kernel(
             nc.scalar.copy(w[:], turned[:].rearrange("s t q -> s q t"))
             weights[b, h] = w
 
-        queries, kw_got, kb_cols = {}, {}, {}
-        neg_scores, neg_max, page_totals, probs, weights = {}, {}, {}, {}, {}
+        queries, kw_got, scores, neg_max, page_totals, probs, weights = {}, {}, {}, {}, {}, {}, {}
 
-        spread_token_scales()
-        gather_bias(0, None)
+        spread(kb_dealt, kb_pool)
         ks_got = sb([P, B * N], U8, "ks_got")
         nc.vector.tensor_copy(ks_got[:], ks_pool[:].bitcast(U8).indirect(offsets[:]))
-        queries[0] = quantise_queries(0)
-        gather_keys(0, 0, "first_keys")
-        gather_keys(0, 1, None)
-        queries[1] = quantise_queries(1)
-        score_page(0, 0)
-        score_page(0, 1)
-        gather_bias(1, "first_keys")
-        gather_keys(1, 0, "kb_pool")
-        gather_keys(1, 1, "biased01")
-        weigh_page(0, 0)
-        weigh_page(0, 1)
-        scale_page(0, 0)
-        score_page(1, 0)
-        scale_page(0, 1)
-        score_page(1, 1)
-        weigh_page(1, 0)
-        weigh_page(1, 1)
+        raws = []
+        for b in range(B):
+            queries[b] = quantise_queries(b)
+            for h in range(2):
+                gather_keys(b, h)
+            raws.append(raw_scores(b))
+        spread(vs_dealt, vs_pool)
+        for b in range(B):
+            add_bias(b, raws[b])
+        for b in range(B):
+            row_maximum(b)
+            for h in range(2):
+                weigh_page(b, h)
+        for b in range(B):
+            for h in range(2):
+                scale_page(b, h)
 
-        vw_got = sb([P, B * 2 * DV], U32, "vw_got", "biased11")
+        vw_got = sb([P, B * 2 * DV], U32, "vw_got", "biased1")
         nc.vector.tensor_copy(vw_got[:], vw_pool[:].bitcast(U32).indirect(v_offsets[:]))
-        scale_page(1, 0)
-        scale_page(1, 1)
-        vsc_got = sb([P, B * 2 * DV], U8, "vsc_got", "negated11")
+        vsc_got = sb([P, B * 2 * DV], U8, "vsc_got", "neg_max1")
         nc.vector.tensor_copy(vsc_got[:], vsc_pool[:].bitcast(U8).indirect(v_offsets[:]))
 
         totals = sb([P, B], F32, "totals")

@@ -22,6 +22,8 @@ ACT = mybir.ActivationFunctionType
 AXIS = mybir.AxisListType
 
 
+FIRST = P - T // P
+
 FLOPS = 2 * B * NQ * N * (D + DV)
 
 
@@ -51,51 +53,54 @@ def tile_attend_pkv8_soft_kb_kernel(
         warm_out = sb([P, 1], F32, "warm_out")
         ident = sb([P, P], F32, "ident")
 
-        vs_dealt = sb([P, PAGES, PACK], F32, "vs_dealt")
-        kb_dealt = sb([P, PAGES, PACK], F32, "kb_dealt")
+        kb_rows = sb([P, P], F32, "kb_rows")
 
-        make_identity(nc, ident[:])
         nc.vector.memset(ks_pool[:], 0)
         nc.vector.memset(warm[:], 0.0)
+        nc.vector.memset(ident[:], 0.0)
+        make_identity(nc, ident[:], nomemset=True)
+        nc.vector.memset(kb_rows[:FIRST, :], 0.0)
         nc.vector.memset(vsc_pool[:], 0)
-
-        def load_dealt(tile, source):
-            nc.sync.dma_start(tile[:], source[0].rearrange("(u s t) -> s u t", u=PAGES, t=PACK))
 
         def load_queries(b):
             nc.sync.dma_start(q_raw[b][:], qT[b].rearrange("(p j) q -> p j q", j=PACK))
 
         nc.sync.dma_start(offsets[:], offs)
-        load_dealt(kb_dealt, kb)
-        load_queries(0)
+        nc.sync.dma_start(kb_rows[FIRST:, :], kb[0].rearrange("(c n) -> c n", n=P))
+        nc.sync.dma_start(v_offsets[:], voffs)
         ks_rows = k_scales[0].bitcast(I32)
         for r in range(4):
             nc.sync.dma_start(ks_pool[r:P:32, :], ks_rows[r:16:4, :])
         nc.sync.dma_start(kw_pool[:], k_words[0].rearrange("p t r -> p (t r)").bitcast(I32))
-        load_dealt(vs_dealt, vs)
+        load_queries(0)
         load_queries(1)
-        nc.sync.dma_start(v_offsets[:], voffs)
-        nc.sync.dma_start(
-            vw_pool[:].rearrange("p (u e) -> p u e", u=PAGES),
-            v_words.rearrange("u p e r -> p u (e r)").bitcast(I32),
-        )
         vsc_rows = v_scales.bitcast(I32).rearrange("u f c -> f u c")
         for r in range(4):
             nc.sync.dma_start(
                 vsc_pool[r:P:32, :].rearrange("p (u c) -> p u c", u=PAGES), vsc_rows[r:16:4]
             )
+        nc.sync.dma_start(vs_pool[:], vs)
+        nc.sync.dma_start(
+            vw_pool[:].rearrange("p (u e) -> p u e", u=PAGES),
+            v_words.rearrange("u p e r -> p u (e r)").bitcast(I32),
+        )
         nc.scalar.activation(warm_out[:], warm[:], ACT.Exp)
 
         def entries(s0, n):
             return offsets[:, s0 // LIST : (s0 + n) // LIST]
 
-        def spread(dealt, window):
+        def spread_bias():
+            turned = psum.tile([P, P], F32, name="turned", tag="turn", bufs=3)
+            nc.tensor.transpose(turned[:], kb_rows[:], ident[:])
+            kb_cols = sb([P, T // P], F32, "kb_cols")
+            nc.scalar.copy(kb_cols[:], turned[:, FIRST:])
             for u in range(PAGES):
                 bank = psum.tile([P, PACK, P], F32, name="spread", tag="turn", bufs=3)
-                for t in range(PACK):
-                    nc.tensor.transpose(bank[:, t, :], dealt[:, u, t : t + 1].to_broadcast([P, P]), ident[:])
+                for j in range(4):
+                    c = 4 * u + j
+                    nc.tensor.transpose(bank[:, j, :], kb_cols[:, c : c + 1].to_broadcast([P, P]), ident[:])
                 nc.scalar.activation(
-                    window[:, u * PASS : (u + 1) * PASS], bank[:].rearrange("p t s -> p (t s)"), ACT.Copy
+                    kb_pool[:, u * PASS : (u + 1) * PASS], bank[:].rearrange("p j n -> p (j n)"), ACT.Copy
                 )
 
         def quantise_queries(b):
@@ -109,12 +114,12 @@ def tile_attend_pkv8_soft_kb_kernel(
             return codes, scales
 
         def gather_keys(b, h):
-            got = sb([P, PASS], U32, f"kw_got{b}{h}")
+            got = sb([P, PASS], U32, f"kw_got{b}{h}", {(1, 0): "q_raw0", (1, 1): "q_bf0"}.get((b, h)))
             nc.vector.tensor_copy(got[:], kw_pool[:].bitcast(U32).indirect(entries(b * N + h * PASS, PASS)))
             kw_got[b, h] = got
 
         def raw_scores(b):
-            raw = sb([P, 2, PACK, P], F32, f"raw{b}")
+            raw = sb([P, N], F32, f"raw{b}")
             for h in range(2):
                 s0 = b * N + h * PASS
                 bank = psum.tile([P, PASS], F32, name="score", tag="score", bufs=3)
@@ -127,9 +132,7 @@ def tile_attend_pkv8_soft_kb_kernel(
                     start=True,
                     stop=True,
                 )
-                nc.scalar.copy(
-                    raw[:, h].rearrange("q t s -> q s t"), bank[:].rearrange("q (s t) -> q s t", t=PACK)
-                )
+                nc.scalar.copy(raw[:, h * PASS : (h + 1) * PASS], bank[:])
             return raw
 
         def add_bias(b, raw):
@@ -137,7 +140,7 @@ def tile_attend_pkv8_soft_kb_kernel(
             nc.vector.tensor_tensor(
                 biased[:],
                 kb_pool[:].indirect(entries(b * N, N)),
-                raw[:].rearrange("q h t s -> q (h t s)"),
+                raw[:],
                 ALU.add,
             )
             scores[b] = biased
@@ -148,10 +151,10 @@ def tile_attend_pkv8_soft_kb_kernel(
             neg_max[b] = least
 
         def weigh_page(b, h):
-            p = sb([P, PACK, P], F32, f"p{b}{h}")
+            p = sb([P, PASS], F32, f"p{b}{h}")
             total = sb([P, 1], F32, f"total{b}{h}")
             nc.scalar.activation(
-                p[:].rearrange("q t s -> q (t s)"),
+                p[:],
                 scores[b][:, h * PASS : (h + 1) * PASS],
                 ACT.Exp,
                 bias=neg_max[b][:],
@@ -162,31 +165,40 @@ def tile_attend_pkv8_soft_kb_kernel(
 
         def scale_page(b, h):
             w32 = sb([P, PASS], F32, f"w32{b}{h}")
-            nc.vector.tensor_tensor(
-                w32[:],
-                vs_pool[:].indirect(entries(b * N + h * PASS, PASS)),
-                probs[b, h][:].rearrange("q t s -> q (t s)"),
-                ALU.mult,
+            w_bf = sb([P, 2, P, 2], BF16, f"w_bf{b}{h}")
+            piece = PASS
+            for c0 in range(0, PASS, piece):
+                nc.vector.tensor_tensor(
+                    w32[:, c0 : c0 + piece],
+                    vs_pool[:].indirect(entries(b * N + h * PASS + c0, piece)),
+                    probs[b, h][:, c0 : c0 + piece],
+                    ALU.mult,
+                )
+                nc.scalar.copy(
+                    w_bf[:, :, c0 // PACK : (c0 + piece) // PACK, :],
+                    w32[:, c0 : c0 + piece].rearrange("q (s u e) -> q u s e", u=2, e=2),
+                )
+            pairs = w_bf[:].rearrange("q u s e -> q (u s e)").bitcast(F32)
+            turned = psum.tile([P, 2, NQ], F32, name="w_turned", tag="score", bufs=3)
+            for u in range(2):
+                nc.tensor.transpose(turned[:, u, :], pairs[:, u * P : (u + 1) * P], ident[:])
+            nc.scalar.copy(
+                weights[b][:, h].rearrange("s q t -> s (q t)").bitcast(F32).rearrange("s (q u) -> s q u", u=2),
+                turned[:].rearrange("s u q -> s q u"),
             )
-            turned = psum.tile([P, PACK, NQ], F32, name="w_turned", tag="score", bufs=3)
-            for t in range(PACK):
-                nc.tensor.transpose(turned[:, t, :], w32[:, t * P : (t + 1) * P], ident[:])
-            w = sb([P, NQ, PACK], BF16, f"w{b}{h}")
-            nc.scalar.copy(w[:], turned[:].rearrange("s t q -> s q t"))
-            weights[b, h] = w
 
-        queries, kw_got, scores, neg_max, page_totals, probs, weights = {}, {}, {}, {}, {}, {}, {}
+        queries, kw_got, scores, neg_max, page_totals, probs = {}, {}, {}, {}, {}, {}
+        weights = [sb([P, 2, NQ, PACK], BF16, f"w{b}") for b in range(B)]
 
-        spread(kb_dealt, kb_pool)
+        spread_bias()
         ks_got = sb([P, B * N], U8, "ks_got")
         nc.vector.tensor_copy(ks_got[:], ks_pool[:].bitcast(U8).indirect(offsets[:]))
         raws = []
         for b in range(B):
-            queries[b] = quantise_queries(b)
             for h in range(2):
                 gather_keys(b, h)
+            queries[b] = quantise_queries(b)
             raws.append(raw_scores(b))
-        spread(vs_dealt, vs_pool)
         for b in range(B):
             add_bias(b, raws[b])
         for b in range(B):
@@ -197,34 +209,37 @@ def tile_attend_pkv8_soft_kb_kernel(
             for h in range(2):
                 scale_page(b, h)
 
-        vw_got = sb([P, B * 2 * DV], U32, "vw_got", "biased1")
-        nc.vector.tensor_copy(vw_got[:], vw_pool[:].bitcast(U32).indirect(v_offsets[:]))
-        vsc_got = sb([P, B * 2 * DV], U8, "vsc_got", "neg_max1")
-        nc.vector.tensor_copy(vsc_got[:], vsc_pool[:].bitcast(U8).indirect(v_offsets[:]))
-
         totals = sb([P, B], F32, "totals")
         for b in range(B):
             nc.scalar.activation(
                 totals[:, b : b + 1], page_totals[b, 0][:], ACT.Identity, bias=page_totals[b, 1][:]
             )
+        vw_got = sb([P, B * 2 * DV], U32, "vw_got", "total10")
+        nc.vector.tensor_copy(vw_got[:], vw_pool[:].bitcast(U32).indirect(v_offsets[:]))
+
+        vsc_got = sb([P, B * 2 * DV], U8, "vsc_got", "total11")
+        nc.vector.tensor_copy(vsc_got[:], vsc_pool[:].bitcast(U8).indirect(v_offsets[:]))
         inverse = sb([P, B], F32, "inverse")
         nc.vector.reciprocal(inverse[:], totals[:])
 
         for b in range(B):
             y = psum.tile([P, DV], F32, name="y", tag="y", bufs=2)
-            for h in range(2):
-                w_codes = sb([P, NQ], U32, f"w_codes{b}{h}")
-                w_scales = sb([P, NQ], U8, f"w_scales{b}{h}")
+            w_codes = sb([P, 2 * NQ], U32, f"w_codes{b}", ("p11", "vw_pool")[b])
+            w_scales = sb([P, 2 * NQ], U8, f"w_scales{b}")
+            w_flat = weights[b][:].rearrange("s h q t -> s (h q t)")
+            width = 2 * NQ if b == 0 else NQ
+            for c0 in range(0, 2 * NQ, width):
                 nc.vector.quantize_mx(
-                    out=w_codes[:].bitcast(FP8X4),
-                    scales=w_scales[:],
-                    in_=weights[b, h][:].rearrange("s q t -> s (q t)"),
+                    out=w_codes[:, c0 : c0 + width].bitcast(FP8X4),
+                    scales=w_scales[:, c0 : c0 + width],
+                    in_=w_flat[:, PACK * c0 : PACK * (c0 + width)],
                 )
+            for h in range(2):
                 page = slice((2 * b + h) * DV, (2 * b + h + 1) * DV)
                 nc.tensor.matmul_mx(
                     out=y[:],
-                    lhsT=w_codes[:].bitcast(FP8X4),
-                    lhsT_scale=w_scales[:],
+                    lhsT=w_codes[:, h * NQ : (h + 1) * NQ].bitcast(FP8X4),
+                    lhsT_scale=w_scales[:, h * NQ : (h + 1) * NQ],
                     rhs=vw_got[:, page].bitcast(FP8X4),
                     rhs_scale=vsc_got[:, page],
                     start=(h == 0),

@@ -49,14 +49,12 @@ def tile_attend_pkv8_soft_kb_kernel(
         kb_pool = sb([P, T], F32, "kb_pool")
         vsc_pool = sb([P, PAGES * DV // 4], I32, "vsc_pool")
         q_raw = [sb([P, PACK, NQ], F32, f"q_raw{b}") for b in range(B)]
-        warm = sb([P, 1], F32, "warm")
-        warm_out = sb([P, 1], F32, "warm_out")
         ident = sb([P, P], F32, "ident")
 
         kb_rows = sb([P, P], F32, "kb_rows")
 
-        nc.vector.memset(ks_pool[:], 0)
-        nc.vector.memset(warm[:], 0.0)
+        nc.gpsimd.memset(ks_pool[:, : T // 8], 0)
+        nc.vector.memset(ks_pool[:, T // 8 :], 0)
         nc.vector.memset(ident[:], 0.0)
         make_identity(nc, ident[:], nomemset=True)
         nc.vector.memset(kb_rows[:FIRST, :], 0.0)
@@ -65,15 +63,15 @@ def tile_attend_pkv8_soft_kb_kernel(
         def load_queries(b):
             nc.sync.dma_start(q_raw[b][:], qT[b].rearrange("(p j) q -> p j q", j=PACK))
 
+        load_queries(0)
         nc.sync.dma_start(offsets[:], offs)
         nc.sync.dma_start(kb_rows[FIRST:, :], kb[0].rearrange("(c n) -> c n", n=P))
-        nc.sync.dma_start(v_offsets[:], voffs)
         ks_rows = k_scales[0].bitcast(I32)
         for r in range(4):
             nc.sync.dma_start(ks_pool[r:P:32, :], ks_rows[r:16:4, :])
         nc.sync.dma_start(kw_pool[:], k_words[0].rearrange("p t r -> p (t r)").bitcast(I32))
-        load_queries(0)
         load_queries(1)
+        nc.sync.dma_start(v_offsets[:], voffs)
         vsc_rows = v_scales.bitcast(I32).rearrange("u f c -> f u c")
         for r in range(4):
             nc.sync.dma_start(
@@ -84,7 +82,6 @@ def tile_attend_pkv8_soft_kb_kernel(
             vw_pool[:].rearrange("p (u e) -> p u e", u=PAGES),
             v_words.rearrange("u p e r -> p u (e r)").bitcast(I32),
         )
-        nc.scalar.activation(warm_out[:], warm[:], ACT.Exp)
 
         def entries(s0, n):
             return offsets[:, s0 // LIST : (s0 + n) // LIST]
@@ -113,10 +110,13 @@ def tile_attend_pkv8_soft_kb_kernel(
             )
             return codes, scales
 
-        def gather_keys(b, h):
-            got = sb([P, PASS], U32, f"kw_got{b}{h}", {(1, 0): "q_raw0", (1, 1): "q_bf0"}.get((b, h)))
-            nc.vector.tensor_copy(got[:], kw_pool[:].bitcast(U32).indirect(entries(b * N + h * PASS, PASS)))
-            kw_got[b, h] = got
+        def gather_keys(b, piece):
+            got = sb([P, N], U32, f"kw_got{b}")
+            for c0 in range(0, N, piece):
+                nc.vector.tensor_copy(
+                    got[:, c0 : c0 + piece], kw_pool[:].bitcast(U32).indirect(entries(b * N + c0, piece))
+                )
+            kw_got[b] = got
 
         def raw_scores(b):
             raw = sb([P, N], F32, f"raw{b}")
@@ -127,7 +127,7 @@ def tile_attend_pkv8_soft_kb_kernel(
                     out=bank[:],
                     lhsT=queries[b][0][:].bitcast(FP8X4),
                     lhsT_scale=queries[b][1][:],
-                    rhs=kw_got[b, h][:].bitcast(FP8X4),
+                    rhs=kw_got[b][:, h * PASS : (h + 1) * PASS].bitcast(FP8X4),
                     rhs_scale=ks_got[:, s0 : s0 + PASS],
                     start=True,
                     stop=True,
@@ -195,9 +195,8 @@ def tile_attend_pkv8_soft_kb_kernel(
         nc.vector.tensor_copy(ks_got[:], ks_pool[:].bitcast(U8).indirect(offsets[:]))
         raws = []
         for b in range(B):
-            for h in range(2):
-                gather_keys(b, h)
             queries[b] = quantise_queries(b)
+            gather_keys(b, PASS if b == 0 else N)
             raws.append(raw_scores(b))
         for b in range(B):
             add_bias(b, raws[b])

@@ -4,11 +4,18 @@ import concourse.mybir as mybir
 from concourse.masks import make_identity
 
 B, N, T, D, DV, NQ = 2, 1024, 4096, 512, 128, 128
-PAGES = 8
 P = 128
 PACK = 4
-PASS = P * PACK
+PAGE = P * PACK
+POOL_PAGES = T // PAGE
+SEQ_PAGES = N // PAGE
 LIST = 16
+SCALE_ROWS = 16
+QUADRANT = 32
+KS_WORDS = T // 4
+BIAS_ROWS = T // P
+BIAS_FIRST = P - BIAS_ROWS
+LAST_PIECE = P
 
 F32 = mybir.dt.float32
 BF16 = mybir.dt.bfloat16
@@ -20,9 +27,6 @@ FP8X4 = mybir.dt.float8_e4m3fn_x4
 ALU = mybir.AluOpType
 ACT = mybir.ActivationFunctionType
 AXIS = mybir.AxisListType
-
-
-FIRST = P - T // P
 
 FLOPS = 2 * B * NQ * N * (D + DV)
 
@@ -36,213 +40,218 @@ def tile_attend_pkv8_soft_kb_kernel(
         keep = ctx.enter_context(tc.tile_pool(name="keep", bufs=1))
         psum = ctx.enter_context(tc.psum_pool(name="psum", bufs=1))
 
-        def sb(shape, dtype, name, tag=None):
-            return keep.tile(shape, dtype, name=name, tag=tag or name, align_bytes=64)
+        def sb(shape, dtype, name, reuses=None):
+            return keep.tile(shape, dtype, name=name, tag=reuses or name, align_bytes=64)
+
+        def spread_bank(shape, name):
+            return psum.tile(shape, F32, name=name, tag="spread", bufs=3)
+
+        def page_bank(shape, name):
+            return psum.tile(shape, F32, name=name, tag="page", bufs=3)
 
         offsets = lists.tile([P, B * N // LIST], U16, name="offsets")
-        v_offsets = lists.tile([P, B * 2 * DV // LIST], U16, name="v_offsets")
+        v_offsets = lists.tile([P, B * SEQ_PAGES * DV // LIST], U16, name="v_offsets")
 
-        ks_pool = sb([P, T // 4], I32, "ks_pool")
+        ks_pool = sb([P, KS_WORDS], I32, "ks_pool")
         kw_pool = sb([P, T], I32, "kw_pool")
-        vw_pool = sb([P, PAGES * DV], I32, "vw_pool")
+        vw_pool = sb([P, POOL_PAGES * DV], I32, "vw_pool")
         vs_pool = sb([P, T], F32, "vs_pool")
         kb_pool = sb([P, T], F32, "kb_pool")
-        vsc_pool = sb([P, PAGES * DV // 4], I32, "vsc_pool")
+        vsc_pool = sb([P, POOL_PAGES * DV // 4], I32, "vsc_pool")
         q_raw = [sb([P, PACK, NQ], F32, f"q_raw{b}") for b in range(B)]
         ident = sb([P, P], F32, "ident")
-
         kb_rows = sb([P, P], F32, "kb_rows")
 
-        nc.gpsimd.memset(ks_pool[:, : T // 8], 0)
-        nc.vector.memset(ks_pool[:, T // 8 :], 0)
+        nc.gpsimd.memset(ks_pool[:, : KS_WORDS // 2], 0)
+        nc.vector.memset(ks_pool[:, KS_WORDS // 2 :], 0)
         nc.vector.memset(ident[:], 0.0)
         make_identity(nc, ident[:], nomemset=True)
-        nc.vector.memset(kb_rows[:FIRST, :], 0.0)
+        nc.vector.memset(kb_rows[:BIAS_FIRST, :], 0.0)
         nc.vector.memset(vsc_pool[:], 0)
 
         def load_queries(b):
-            nc.sync.dma_start(q_raw[b][:], qT[b].rearrange("(p j) q -> p j q", j=PACK))
+            nc.sync.dma_start(q_raw[b][:], qT[b].rearrange("(s t) q -> s t q", t=PACK))
 
         load_queries(0)
         nc.sync.dma_start(offsets[:], offs)
-        nc.sync.dma_start(kb_rows[FIRST:, :], kb[0].rearrange("(c n) -> c n", n=P))
+        nc.sync.dma_start(kb_rows[BIAS_FIRST:, :], kb[0].rearrange("(c n) -> c n", n=P))
         ks_rows = k_scales[0].bitcast(I32)
         for r in range(4):
-            nc.sync.dma_start(ks_pool[r:P:32, :], ks_rows[r:16:4, :])
-        nc.sync.dma_start(kw_pool[:], k_words[0].rearrange("p t r -> p (t r)").bitcast(I32))
+            nc.sync.dma_start(ks_pool[r:P:QUADRANT, :], ks_rows[r:SCALE_ROWS:4, :])
+        nc.sync.dma_start(kw_pool[:], k_words[0].rearrange("s n t -> s (n t)").bitcast(I32))
         load_queries(1)
         nc.sync.dma_start(v_offsets[:], voffs)
         vsc_rows = v_scales.bitcast(I32).rearrange("u f c -> f u c")
         for r in range(4):
             nc.sync.dma_start(
-                vsc_pool[r:P:32, :].rearrange("p (u c) -> p u c", u=PAGES), vsc_rows[r:16:4]
+                vsc_pool[r:P:QUADRANT, :].rearrange("s (u c) -> s u c", u=POOL_PAGES),
+                vsc_rows[r:SCALE_ROWS:4],
             )
         nc.sync.dma_start(vs_pool[:], vs)
         nc.sync.dma_start(
-            vw_pool[:].rearrange("p (u e) -> p u e", u=PAGES),
-            v_words.rearrange("u p e r -> p u (e r)").bitcast(I32),
+            vw_pool[:].rearrange("s (u e) -> s u e", u=POOL_PAGES),
+            v_words.rearrange("u s e t -> s u (e t)").bitcast(I32),
         )
 
-        def entries(s0, n):
-            return offsets[:, s0 // LIST : (s0 + n) // LIST]
+        def entries(first, count):
+            return offsets[:, first // LIST : (first + count) // LIST]
 
         def spread_bias():
-            turned = psum.tile([P, P], F32, name="turned", tag="turn", bufs=3)
+            turned = spread_bank([P, P], "kb_turned")
             nc.tensor.transpose(turned[:], kb_rows[:], ident[:])
-            kb_cols = sb([P, T // P], F32, "kb_cols")
-            nc.scalar.copy(kb_cols[:], turned[:, FIRST:])
-            for u in range(PAGES):
-                bank = psum.tile([P, PACK, P], F32, name="spread", tag="turn", bufs=3)
-                for j in range(4):
-                    c = 4 * u + j
+            kb_cols = sb([P, BIAS_ROWS], F32, "kb_cols")
+            nc.scalar.copy(kb_cols[:], turned[:, BIAS_FIRST:])
+            for u in range(POOL_PAGES):
+                bank = spread_bank([P, PAGE // P, P], "kb_spread")
+                for j in range(PAGE // P):
+                    c = u * (PAGE // P) + j
                     nc.tensor.transpose(bank[:, j, :], kb_cols[:, c : c + 1].to_broadcast([P, P]), ident[:])
                 nc.scalar.activation(
-                    kb_pool[:, u * PASS : (u + 1) * PASS], bank[:].rearrange("p j n -> p (j n)"), ACT.Copy
+                    kb_pool[:, u * PAGE : (u + 1) * PAGE], bank[:].rearrange("q j n -> q (j n)"), ACT.Copy
                 )
 
         def quantise_queries(b):
             q_bf = sb([P, NQ, PACK], BF16, f"q_bf{b}")
-            nc.scalar.copy(q_bf[:], q_raw[b][:].rearrange("p j q -> p q j"))
+            nc.scalar.copy(q_bf[:], q_raw[b][:].rearrange("s t q -> s q t"))
             codes = sb([P, NQ], U32, f"q_codes{b}")
             scales = sb([P, NQ], U8, f"q_scales{b}")
             nc.vector.quantize_mx(
-                out=codes[:].bitcast(FP8X4), scales=scales[:], in_=q_bf[:].rearrange("p q j -> p (q j)")
+                out=codes[:].bitcast(FP8X4), scales=scales[:], in_=q_bf[:].rearrange("s q t -> s (q t)")
             )
             return codes, scales
 
-        def gather_keys(b, piece):
+        def gather_key_words(b, piece):
             got = sb([P, N], U32, f"kw_got{b}")
             for c0 in range(0, N, piece):
                 nc.vector.tensor_copy(
                     got[:, c0 : c0 + piece], kw_pool[:].bitcast(U32).indirect(entries(b * N + c0, piece))
                 )
-            kw_got[b] = got
+            return got
 
-        def raw_scores(b):
+        def raw_scores(b, q_codes, q_scales, kw_got):
             raw = sb([P, N], F32, f"raw{b}")
-            for h in range(2):
-                s0 = b * N + h * PASS
-                bank = psum.tile([P, PASS], F32, name="score", tag="score", bufs=3)
+            for h in range(SEQ_PAGES):
+                bank = page_bank([P, PAGE], "raw_page")
                 nc.tensor.matmul_mx(
                     out=bank[:],
-                    lhsT=queries[b][0][:].bitcast(FP8X4),
-                    lhsT_scale=queries[b][1][:],
-                    rhs=kw_got[b][:, h * PASS : (h + 1) * PASS].bitcast(FP8X4),
-                    rhs_scale=ks_got[:, s0 : s0 + PASS],
+                    lhsT=q_codes[:].bitcast(FP8X4),
+                    lhsT_scale=q_scales[:],
+                    rhs=kw_got[:, h * PAGE : (h + 1) * PAGE].bitcast(FP8X4),
+                    rhs_scale=ks_got[:, b * N + h * PAGE : b * N + (h + 1) * PAGE],
                     start=True,
                     stop=True,
                 )
-                nc.scalar.copy(raw[:, h * PASS : (h + 1) * PASS], bank[:])
+                nc.scalar.copy(raw[:, h * PAGE : (h + 1) * PAGE], bank[:])
             return raw
 
         def add_bias(b, raw):
             biased = sb([P, N], F32, f"biased{b}")
-            nc.vector.tensor_tensor(
-                biased[:],
-                kb_pool[:].indirect(entries(b * N, N)),
-                raw[:],
-                ALU.add,
-            )
-            scores[b] = biased
+            nc.vector.tensor_tensor(biased[:], kb_pool[:].indirect(entries(b * N, N)), raw[:], ALU.add)
+            return biased
 
-        def row_maximum(b):
-            least = sb([P, 1], F32, f"neg_max{b}")
-            nc.vector.tensor_reduce(least[:], scores[b][:], AXIS.X, ALU.max, negate=True)
-            neg_max[b] = least
+        def softmax_numerators(b, biased):
+            neg_max = sb([P, 1], F32, f"neg_max{b}")
+            nc.vector.tensor_reduce(neg_max[:], biased[:], AXIS.X, ALU.max, negate=True)
+            for h in range(SEQ_PAGES):
+                probs[b, h] = sb([P, PAGE], F32, f"p{b}{h}")
+                page_sums[b, h] = sb([P, 1], F32, f"page_sum{b}{h}")
+                nc.scalar.activation(
+                    probs[b, h][:],
+                    biased[:, h * PAGE : (h + 1) * PAGE],
+                    ACT.Exp,
+                    bias=neg_max[:],
+                    accum_out=page_sums[b, h][:],
+                )
 
-        def weigh_page(b, h):
-            p = sb([P, PASS], F32, f"p{b}{h}")
-            total = sb([P, 1], F32, f"total{b}{h}")
-            nc.scalar.activation(
-                p[:],
-                scores[b][:, h * PASS : (h + 1) * PASS],
-                ACT.Exp,
-                bias=neg_max[b][:],
-                accum_out=total[:],
-            )
-            page_totals[b, h] = total
-            probs[b, h] = p
-
-        def scale_page(b, h):
-            w32 = sb([P, PASS], F32, f"w32{b}{h}")
-            w_bf = sb([P, 2, P, 2], BF16, f"w_bf{b}{h}")
-            piece = PASS
-            for c0 in range(0, PASS, piece):
+        def weigh_and_turn(b, h, cuts, turned):
+            w32 = sb([P, PAGE], F32, f"w32_{b}{h}")
+            w_pairs = sb([P, 2, P, 2], BF16, f"w_pairs{b}{h}")
+            for c0, c1 in zip(cuts, cuts[1:]):
                 nc.vector.tensor_tensor(
-                    w32[:, c0 : c0 + piece],
-                    vs_pool[:].indirect(entries(b * N + h * PASS + c0, piece)),
-                    probs[b, h][:, c0 : c0 + piece],
+                    w32[:, c0:c1],
+                    vs_pool[:].indirect(entries(b * N + h * PAGE + c0, c1 - c0)),
+                    probs[b, h][:, c0:c1],
                     ALU.mult,
                 )
                 nc.scalar.copy(
-                    w_bf[:, :, c0 // PACK : (c0 + piece) // PACK, :],
-                    w32[:, c0 : c0 + piece].rearrange("q (s u e) -> q u s e", u=2, e=2),
+                    w_pairs[:, :, c0 // PACK : c1 // PACK, :],
+                    w32[:, c0:c1].rearrange("q (s u e) -> q u s e", u=2, e=2),
                 )
-            pairs = w_bf[:].rearrange("q u s e -> q (u s e)").bitcast(F32)
-            turned = psum.tile([P, 2, NQ], F32, name="w_turned", tag="score", bufs=3)
+            words = w_pairs[:].rearrange("q u s e -> q (u s e)").bitcast(F32)
             for u in range(2):
-                nc.tensor.transpose(turned[:, u, :], pairs[:, u * P : (u + 1) * P], ident[:])
+                nc.tensor.transpose(turned[:, u, :], words[:, u * P : (u + 1) * P], ident[:])
+
+        def interleave(grouped, turned):
             nc.scalar.copy(
-                weights[b][:, h].rearrange("s q t -> s (q t)").bitcast(F32).rearrange("s (q u) -> s q u", u=2),
-                turned[:].rearrange("s u q -> s q u"),
+                grouped.rearrange("s h q t -> s h (q t)").bitcast(F32).rearrange("s h (q u) -> s h q u", u=2),
+                turned.rearrange("s h u q -> s h q u"),
             )
 
-        queries, kw_got, scores, neg_max, page_totals, probs = {}, {}, {}, {}, {}, {}
-        weights = [sb([P, 2, NQ, PACK], BF16, f"w{b}") for b in range(B)]
+        probs, page_sums = {}, {}
+        w_grouped = [sb([P, SEQ_PAGES, NQ, PACK], BF16, f"w_grouped{b}") for b in range(B)]
 
         spread_bias()
         ks_got = sb([P, B * N], U8, "ks_got")
         nc.vector.tensor_copy(ks_got[:], ks_pool[:].bitcast(U8).indirect(offsets[:]))
+
         raws = []
         for b in range(B):
-            queries[b] = quantise_queries(b)
-            gather_keys(b, PASS if b == 0 else N)
-            raws.append(raw_scores(b))
-        for b in range(B):
-            add_bias(b, raws[b])
-        for b in range(B):
-            row_maximum(b)
-            for h in range(2):
-                weigh_page(b, h)
-        for b in range(B):
-            for h in range(2):
-                scale_page(b, h)
+            q_codes, q_scales = quantise_queries(b)
+            kw_got = gather_key_words(b, PAGE if b == 0 else N)
+            raws.append(raw_scores(b, q_codes, q_scales, kw_got))
+        scores = [add_bias(b, raws[b]) for b in range(B)]
 
-        totals = sb([P, B], F32, "totals")
+        vsc_got = sb([P, B * SEQ_PAGES * DV], U8, "vsc_got", reuses="kw_got1")
+        nc.vector.tensor_copy(vsc_got[:], vsc_pool[:].bitcast(U8).indirect(v_offsets[:]))
+
+        for b in range(B):
+            softmax_numerators(b, scores[b])
+
+        first_turned = page_bank([P, SEQ_PAGES, 2, NQ], "first_turned")
+        for h in range(SEQ_PAGES):
+            weigh_and_turn(0, h, (0, PAGE), first_turned[:, h])
+        last_turned = []
+        for h, cuts in enumerate(((0, PAGE), (0, PAGE - LAST_PIECE, PAGE))):
+            last_turned.append(page_bank([P, 1, 2, NQ], "last_turned"))
+            weigh_and_turn(1, h, cuts, last_turned[h][:, 0])
+        interleave(w_grouped[0][:], first_turned[:])
+        for h in range(SEQ_PAGES):
+            interleave(w_grouped[1][:, h : h + 1], last_turned[h][:])
+
+        row_sums = sb([P, B], F32, "row_sums")
         for b in range(B):
             nc.scalar.activation(
-                totals[:, b : b + 1], page_totals[b, 0][:], ACT.Identity, bias=page_totals[b, 1][:]
+                row_sums[:, b : b + 1], page_sums[b, 0][:], ACT.Identity, bias=page_sums[b, 1][:]
             )
-        vw_got = sb([P, B * 2 * DV], U32, "vw_got", "total10")
+
+        vw_got = sb([P, B * SEQ_PAGES * DV], U32, "vw_got", reuses="page_sum10")
         nc.vector.tensor_copy(vw_got[:], vw_pool[:].bitcast(U32).indirect(v_offsets[:]))
 
-        vsc_got = sb([P, B * 2 * DV], U8, "vsc_got", "total11")
-        nc.vector.tensor_copy(vsc_got[:], vsc_pool[:].bitcast(U8).indirect(v_offsets[:]))
         inverse = sb([P, B], F32, "inverse")
-        nc.vector.reciprocal(inverse[:], totals[:])
+        nc.vector.reciprocal(inverse[:], row_sums[:])
 
         for b in range(B):
-            y = psum.tile([P, DV], F32, name="y", tag="y", bufs=2)
-            w_codes = sb([P, 2 * NQ], U32, f"w_codes{b}", ("p11", "vw_pool")[b])
-            w_scales = sb([P, 2 * NQ], U8, f"w_scales{b}")
-            w_flat = weights[b][:].rearrange("s h q t -> s (h q t)")
-            width = 2 * NQ if b == 0 else NQ
-            for c0 in range(0, 2 * NQ, width):
+            y = page_bank([P, DV], "y")
+            w_codes = sb([P, SEQ_PAGES * NQ], U32, f"w_codes{b}", reuses=("p11", "vw_pool")[b])
+            w_scales = sb([P, SEQ_PAGES * NQ], U8, f"w_scales{b}")
+            w_flat = w_grouped[b][:].rearrange("s h q t -> s (h q t)")
+            width = SEQ_PAGES * NQ if b == 0 else NQ
+            for c0 in range(0, SEQ_PAGES * NQ, width):
                 nc.vector.quantize_mx(
                     out=w_codes[:, c0 : c0 + width].bitcast(FP8X4),
                     scales=w_scales[:, c0 : c0 + width],
                     in_=w_flat[:, PACK * c0 : PACK * (c0 + width)],
                 )
-            for h in range(2):
-                page = slice((2 * b + h) * DV, (2 * b + h + 1) * DV)
+            for h in range(SEQ_PAGES):
+                page_cols = slice((SEQ_PAGES * b + h) * DV, (SEQ_PAGES * b + h + 1) * DV)
                 nc.tensor.matmul_mx(
                     out=y[:],
                     lhsT=w_codes[:, h * NQ : (h + 1) * NQ].bitcast(FP8X4),
                     lhsT_scale=w_scales[:, h * NQ : (h + 1) * NQ],
-                    rhs=vw_got[:, page].bitcast(FP8X4),
-                    rhs_scale=vsc_got[:, page],
+                    rhs=vw_got[:, page_cols].bitcast(FP8X4),
+                    rhs_scale=vsc_got[:, page_cols],
                     start=(h == 0),
-                    stop=(h == 1),
+                    stop=(h == SEQ_PAGES - 1),
                 )
             result = sb([P, DV], F32, f"result{b}")
             nc.scalar.activation(result[:], y[:], ACT.Copy, scale=inverse[:, b : b + 1])

@@ -15,6 +15,7 @@ QUADRANT = 32
 KS_WORDS = T // 4
 BIAS_ROWS = T // P
 BIAS_FIRST = P - BIAS_ROWS
+FIRST_SUM = 2 * P
 LAST_PIECE = P
 
 F32 = mybir.dt.float32
@@ -80,6 +81,7 @@ def tile_attend_pkv8_soft_kb_kernel(
             nc.sync.dma_start(ks_pool[r:P:QUADRANT, :], ks_rows[r:SCALE_ROWS:4, :])
         nc.sync.dma_start(kw_pool[:], k_words[0].rearrange("s n t -> s (n t)").bitcast(I32))
         load_queries(1)
+        nc.sync.dma_start(vs_pool[:], vs)
         nc.sync.dma_start(v_offsets[:], voffs)
         vsc_rows = v_scales.bitcast(I32).rearrange("u f c -> f u c")
         for r in range(4):
@@ -87,7 +89,6 @@ def tile_attend_pkv8_soft_kb_kernel(
                 vsc_pool[r:P:QUADRANT, :].rearrange("s (u c) -> s u c", u=POOL_PAGES),
                 vsc_rows[r:SCALE_ROWS:4],
             )
-        nc.sync.dma_start(vs_pool[:], vs)
         nc.sync.dma_start(
             vw_pool[:].rearrange("s (u e) -> s u e", u=POOL_PAGES),
             v_words.rearrange("u s e t -> s u (e t)").bitcast(I32),
@@ -144,13 +145,13 @@ def tile_attend_pkv8_soft_kb_kernel(
                 nc.scalar.copy(raw[:, h * PAGE : (h + 1) * PAGE], bank[:])
             return raw
 
-        def add_bias(b, raw):
-            biased = sb([P, N], F32, f"biased{b}")
-            nc.vector.tensor_tensor(biased[:], kb_pool[:].indirect(entries(b * N, N)), raw[:], ALU.add)
-            return biased
+        def add_bias(b, c0, c1):
+            nc.vector.tensor_tensor(
+                scores[b][:, c0:c1], kb_pool[:].indirect(entries(b * N + c0, c1 - c0)), raws[b][:, c0:c1], ALU.add
+            )
 
         def softmax_numerators(b, biased):
-            neg_max = sb([P, 1], F32, f"neg_max{b}")
+            neg_max = sb([P, 1], F32, f"neg_max{b}", reuses="neg_max0")
             nc.vector.tensor_reduce(neg_max[:], biased[:], AXIS.X, ALU.max, negate=True)
             for h in range(SEQ_PAGES):
                 probs[b, h] = sb([P, PAGE], F32, f"p{b}{h}")
@@ -194,18 +195,17 @@ def tile_attend_pkv8_soft_kb_kernel(
         ks_got = sb([P, B * N], U8, "ks_got")
         nc.vector.tensor_copy(ks_got[:], ks_pool[:].bitcast(U8).indirect(offsets[:]))
 
+        queries = [quantise_queries(b) for b in range(B)]
         raws = []
         for b in range(B):
-            q_codes, q_scales = quantise_queries(b)
             kw_got = gather_key_words(b, PAGE if b == 0 else N)
-            raws.append(raw_scores(b, q_codes, q_scales, kw_got))
-        scores = [add_bias(b, raws[b]) for b in range(B)]
-
-        vsc_got = sb([P, B * SEQ_PAGES * DV], U8, "vsc_got", reuses="kw_got1")
-        nc.vector.tensor_copy(vsc_got[:], vsc_pool[:].bitcast(U8).indirect(v_offsets[:]))
-
-        for b in range(B):
-            softmax_numerators(b, scores[b])
+            raws.append(raw_scores(b, *queries[b], kw_got))
+        scores = [sb([P, N], F32, f"biased{b}") for b in range(B)]
+        add_bias(0, 0, N)
+        add_bias(1, 0, FIRST_SUM)
+        softmax_numerators(0, scores[0])
+        add_bias(1, FIRST_SUM, N)
+        softmax_numerators(1, scores[1])
 
         first_turned = page_bank([P, SEQ_PAGES, 2, NQ], "first_turned")
         for h in range(SEQ_PAGES):
@@ -224,6 +224,8 @@ def tile_attend_pkv8_soft_kb_kernel(
                 row_sums[:, b : b + 1], page_sums[b, 0][:], ACT.Identity, bias=page_sums[b, 1][:]
             )
 
+        vsc_got = sb([P, B * SEQ_PAGES * DV], U8, "vsc_got", reuses="page_sum11")
+        nc.vector.tensor_copy(vsc_got[:], vsc_pool[:].bitcast(U8).indirect(v_offsets[:]))
         vw_got = sb([P, B * SEQ_PAGES * DV], U32, "vw_got", reuses="page_sum10")
         nc.vector.tensor_copy(vw_got[:], vw_pool[:].bitcast(U32).indirect(v_offsets[:]))
 
@@ -233,7 +235,7 @@ def tile_attend_pkv8_soft_kb_kernel(
         for b in range(B):
             y = page_bank([P, DV], "y")
             w_codes = sb([P, SEQ_PAGES * NQ], U32, f"w_codes{b}", reuses=("p11", "vw_pool")[b])
-            w_scales = sb([P, SEQ_PAGES * NQ], U8, f"w_scales{b}")
+            w_scales = sb([P, SEQ_PAGES * NQ], U8, f"w_scales{b}", reuses=("vsc_pool", None)[b])
             w_flat = w_grouped[b][:].rearrange("s h q t -> s (h q t)")
             width = SEQ_PAGES * NQ if b == 0 else NQ
             for c0 in range(0, SEQ_PAGES * NQ, width):

@@ -63,8 +63,7 @@ def tile_attend_pkv8_soft_kb_kernel(
         ident = sb([P, P], F32, "ident")
         kb_rows = sb([P, P], F32, "kb_rows")
 
-        nc.gpsimd.memset(ks_pool[:, : KS_WORDS // 2], 0)
-        nc.vector.memset(ks_pool[:, KS_WORDS // 2 :], 0)
+        nc.vector.memset(ks_pool[:], 0)
         nc.vector.memset(ident[:], 0.0)
         make_identity(nc, ident[:], nomemset=True)
         nc.vector.memset(kb_rows[:BIAS_FIRST, :], 0.0)

@@ -15,7 +15,7 @@ QUADRANT = 32
 KS_WORDS = T // 4
 BIAS_ROWS = T // P
 BIAS_FIRST = P - BIAS_ROWS
-FIRST_SUM = 2 * P
+FIRST_SUM = P
 LAST_PIECE = P
 
 F32 = mybir.dt.float32
@@ -120,12 +120,11 @@ def tile_attend_pkv8_soft_kb_kernel(
             )
             return codes, scales
 
-        def gather_key_words(b, piece):
-            got = sb([P, N], U32, f"kw_got{b}")
-            for c0 in range(0, N, piece):
-                nc.vector.tensor_copy(
-                    got[:, c0 : c0 + piece], kw_pool[:].bitcast(U32).indirect(entries(b * N + c0, piece))
-                )
+        def gather_key_words(b):
+            got = []
+            for h in range(SEQ_PAGES):
+                got.append(sb([P, PAGE], U32, f"kw_got{b}{h}", reuses="q_raw1" if (b, h) == (1, 1) else None))
+                nc.vector.tensor_copy(got[h][:], kw_pool[:].bitcast(U32).indirect(entries(b * N + h * PAGE, PAGE)))
             return got
 
         def raw_scores(b, q_codes, q_scales, kw_got):
@@ -136,7 +135,7 @@ def tile_attend_pkv8_soft_kb_kernel(
                     out=bank[:],
                     lhsT=q_codes[:].bitcast(FP8X4),
                     lhsT_scale=q_scales[:],
-                    rhs=kw_got[:, h * PAGE : (h + 1) * PAGE].bitcast(FP8X4),
+                    rhs=kw_got[h][:].bitcast(FP8X4),
                     rhs_scale=ks_got[:, b * N + h * PAGE : b * N + (h + 1) * PAGE],
                     start=True,
                     stop=True,
@@ -150,7 +149,7 @@ def tile_attend_pkv8_soft_kb_kernel(
             )
 
         def softmax_numerators(b, biased):
-            neg_max = sb([P, 1], F32, f"neg_max{b}", reuses="neg_max0")
+            neg_max = sb([P, 1], F32, f"neg_max{b}", reuses="q_raw1")
             nc.vector.tensor_reduce(neg_max[:], biased[:], AXIS.X, ALU.max, negate=True)
             for h in range(SEQ_PAGES):
                 probs[b, h] = sb([P, PAGE], F32, f"p{b}{h}")
@@ -197,10 +196,11 @@ def tile_attend_pkv8_soft_kb_kernel(
         queries = [quantise_queries(b) for b in range(B)]
         raws = []
         for b in range(B):
-            kw_got = gather_key_words(b, PAGE if b == 0 else N)
+            kw_got = gather_key_words(b)
             raws.append(raw_scores(b, *queries[b], kw_got))
         scores = [sb([P, N], F32, f"biased{b}") for b in range(B)]
-        add_bias(0, 0, N)
+        add_bias(0, 0, PAGE)
+        add_bias(0, PAGE, N)
         add_bias(1, 0, FIRST_SUM)
         softmax_numerators(0, scores[0])
         add_bias(1, FIRST_SUM, N)
@@ -223,9 +223,9 @@ def tile_attend_pkv8_soft_kb_kernel(
                 row_sums[:, b : b + 1], page_sums[b, 0][:], ACT.Identity, bias=page_sums[b, 1][:]
             )
 
-        vsc_got = sb([P, B * SEQ_PAGES * DV], U8, "vsc_got", reuses="page_sum11")
+        vsc_got = sb([P, B * SEQ_PAGES * DV], U8, "vsc_got", reuses="p10")
         nc.vector.tensor_copy(vsc_got[:], vsc_pool[:].bitcast(U8).indirect(v_offsets[:]))
-        vw_got = sb([P, B * SEQ_PAGES * DV], U32, "vw_got", reuses="page_sum10")
+        vw_got = sb([P, B * SEQ_PAGES * DV], U32, "vw_got", reuses="w32_10")
         nc.vector.tensor_copy(vw_got[:], vw_pool[:].bitcast(U32).indirect(v_offsets[:]))
 
         inverse = sb([P, B], F32, "inverse")

@@ -9,14 +9,15 @@ PACK = 4
 PAGE = P * PACK
 POOL_PAGES = T // PAGE
 SEQ_PAGES = N // PAGE
+PAGES = B * SEQ_PAGES
 LIST = 16
 SCALE_ROWS = 16
 QUADRANT = 32
 KS_WORDS = T // 4
-BIAS_ROWS = T // P
-BIAS_FIRST = P - BIAS_ROWS
-FIRST_SUM = P
-LAST_PIECE = P
+ROW = P - 1
+KB_ON_GPSIMD = 1792
+VS_ON_VECTOR = 1536
+VS_PIECE = 640
 
 F32 = mybir.dt.float32
 BF16 = mybir.dt.bfloat16
@@ -27,7 +28,6 @@ U8 = mybir.dt.uint8
 FP8X4 = mybir.dt.float8_e4m3fn_x4
 ALU = mybir.AluOpType
 ACT = mybir.ActivationFunctionType
-AXIS = mybir.AxisListType
 
 FLOPS = 2 * B * NQ * N * (D + DV)
 
@@ -44,14 +44,11 @@ def tile_attend_pkv8_soft_kb_kernel(
         def sb(shape, dtype, name, reuses=None):
             return keep.tile(shape, dtype, name=name, tag=reuses or name, align_bytes=64)
 
-        def spread_bank(shape, name):
-            return psum.tile(shape, F32, name=name, tag="spread", bufs=3)
-
-        def page_bank(shape, name):
-            return psum.tile(shape, F32, name=name, tag="page", bufs=3)
+        def bank(shape, name, tag, bufs):
+            return psum.tile(shape, F32, name=name, tag=tag, bufs=bufs)
 
         offsets = lists.tile([P, B * N // LIST], U16, name="offsets")
-        v_offsets = lists.tile([P, B * SEQ_PAGES * DV // LIST], U16, name="v_offsets")
+        v_offsets = lists.tile([P, PAGES * DV // LIST], U16, name="v_offsets")
 
         ks_pool = sb([P, KS_WORDS], I32, "ks_pool")
         kw_pool = sb([P, T], I32, "kw_pool")
@@ -61,26 +58,33 @@ def tile_attend_pkv8_soft_kb_kernel(
         vsc_pool = sb([P, POOL_PAGES * DV // 4], I32, "vsc_pool")
         q_raw = [sb([P, PACK, NQ], F32, f"q_raw{b}") for b in range(B)]
         ident = sb([P, P], F32, "ident")
-        kb_rows = sb([P, P], F32, "kb_rows")
 
-        nc.vector.memset(ks_pool[:], 0)
-        nc.vector.memset(ident[:], 0.0)
-        make_identity(nc, ident[:], nomemset=True)
-        nc.vector.memset(kb_rows[:BIAS_FIRST, :], 0.0)
-        nc.vector.memset(vsc_pool[:], 0)
+        def zero_on_vector(pool, c0, c1):
+            mid = (c0 + c1) // 2 - 1
+            nc.vector.memset(pool[:ROW, c0:mid], 0.0)
+            nc.vector.memset(pool[:ROW, mid:c1], 0.0)
+
+        nc.gpsimd.memset(ks_pool[:], 0)
+        nc.gpsimd.memset(kb_pool[:ROW, :KB_ON_GPSIMD], 0.0)
+        zero_on_vector(kb_pool, KB_ON_GPSIMD, T)
+        make_identity(nc, ident[:])
+        nc.gpsimd.memset(vsc_pool[:], 0)
+        zero_on_vector(vs_pool, 0, VS_ON_VECTOR)
+        for c0 in range(VS_ON_VECTOR, T, VS_PIECE):
+            nc.gpsimd.memset(vs_pool[:ROW, c0 : c0 + VS_PIECE], 0.0)
 
         def load_queries(b):
             nc.sync.dma_start(q_raw[b][:], qT[b].rearrange("(s t) q -> s t q", t=PACK))
 
         load_queries(0)
         nc.sync.dma_start(offsets[:], offs)
-        nc.sync.dma_start(kb_rows[BIAS_FIRST:, :], kb[0].rearrange("(c n) -> c n", n=P))
+        nc.sync.dma_start(kb_pool[ROW:, :], kb[0:1, :])
+        nc.sync.dma_start(vs_pool[ROW:, :], vs[0:1, :])
         ks_rows = k_scales[0].bitcast(I32)
         for r in range(4):
             nc.sync.dma_start(ks_pool[r:P:QUADRANT, :], ks_rows[r:SCALE_ROWS:4, :])
         nc.sync.dma_start(kw_pool[:], k_words[0].rearrange("s n t -> s (n t)").bitcast(I32))
         load_queries(1)
-        nc.sync.dma_start(vs_pool[:], vs)
         nc.sync.dma_start(v_offsets[:], voffs)
         vsc_rows = v_scales.bitcast(I32).rearrange("u f c -> f u c")
         for r in range(4):
@@ -93,26 +97,15 @@ def tile_attend_pkv8_soft_kb_kernel(
             v_words.rearrange("u s e t -> s u (e t)").bitcast(I32),
         )
 
-        def entries(first, count):
-            return offsets[:, first // LIST : (first + count) // LIST]
+        def entries(g):
+            return offsets[:, g * PAGE // LIST : (g + 1) * PAGE // LIST]
 
-        def spread_bias():
-            turned = spread_bank([P, P], "kb_turned")
-            nc.tensor.transpose(turned[:], kb_rows[:], ident[:])
-            kb_cols = sb([P, BIAS_ROWS], F32, "kb_cols")
-            nc.scalar.copy(kb_cols[:], turned[:, BIAS_FIRST:])
-            for u in range(POOL_PAGES):
-                bank = spread_bank([P, PAGE // P, P], "kb_spread")
-                for j in range(PAGE // P):
-                    c = u * (PAGE // P) + j
-                    nc.tensor.transpose(bank[:, j, :], kb_cols[:, c : c + 1].to_broadcast([P, P]), ident[:])
-                nc.scalar.activation(
-                    kb_pool[:, u * PAGE : (u + 1) * PAGE], bank[:].rearrange("q j n -> q (j n)"), ACT.Copy
-                )
-
-        def quantise_queries(b):
+        def round_queries(b, copy):
             q_bf = sb([P, NQ, PACK], BF16, f"q_bf{b}")
-            nc.scalar.copy(q_bf[:], q_raw[b][:].rearrange("s t q -> s q t"))
+            copy(q_bf[:], q_raw[b][:].rearrange("s t q -> s q t"))
+            return q_bf
+
+        def quantise_queries(b, q_bf):
             codes = sb([P, NQ], U32, f"q_codes{b}")
             scales = sb([P, NQ], U8, f"q_scales{b}")
             nc.vector.quantize_mx(
@@ -120,135 +113,143 @@ def tile_attend_pkv8_soft_kb_kernel(
             )
             return codes, scales
 
-        def gather_key_words(b):
-            got = []
-            for h in range(SEQ_PAGES):
-                got.append(sb([P, PAGE], U32, f"kw_got{b}{h}", reuses="q_raw1" if (b, h) == (1, 1) else None))
-                nc.vector.tensor_copy(got[h][:], kw_pool[:].bitcast(U32).indirect(entries(b * N + h * PAGE, PAGE)))
-            return got
+        q_bf0 = round_queries(0, nc.scalar.copy)
 
-        def raw_scores(b, q_codes, q_scales, kw_got):
-            raw = sb([P, N], F32, f"raw{b}")
-            for h in range(SEQ_PAGES):
-                bank = page_bank([P, PAGE], "raw_page")
+        kb_cols = sb([P, PAGES, PACK], F32, "kb_cols")
+        for g in range(PAGES):
+            kb_got = sb([P, PAGE], F32, f"kb_got{g}")
+            nc.scalar.activation(kb_got[:], kb_pool[:].indirect(entries(g)), ACT.Copy)
+            turned = bank([P, PACK, P], "kb_turned", "turn", 3)
+            for c in range(PACK):
+                nc.tensor.transpose(turned[:, c, :], kb_got[:, c * P : (c + 1) * P], ident[:])
+            nc.scalar.copy(kb_cols[:, g, :], turned[:, :, ROW])
+
+        vs_cols = []
+        for g in range(PAGES):
+            vs_got = sb([P, PAGE], F32, f"vs_got{g}")
+            nc.scalar.activation(vs_got[:], vs_pool[:].indirect(entries(g)), ACT.Copy)
+            vs_cols.append(sb([P, 1, PACK], F32, f"vs_cols{g}"))
+            nc.sync.dma_start(vs_cols[g][:, 0, :], vs_got[ROW:, :].rearrange("o (s t) -> o s t", t=PACK))
+
+        ks_got = sb([P, B * N], U8, "ks_got")
+        nc.vector.tensor_copy(ks_got[:], ks_pool[:].bitcast(U8).indirect(offsets[:]))
+        queries = [quantise_queries(0, q_bf0)]
+
+        kw_got, scores = [], []
+
+        def gather_keys(g):
+            kw_got.append(sb([P, PAGE], U32, f"kw_got{g}"))
+            nc.vector.tensor_copy(kw_got[g][:], kw_pool[:].bitcast(U32).indirect(entries(g)))
+
+        def score_page(g):
+            q_codes, q_scales = queries[g // SEQ_PAGES]
+            raw = bank([P, PACK, NQ], "raw", "raw", 2)
+            for c in range(PACK):
                 nc.tensor.matmul_mx(
-                    out=bank[:],
-                    lhsT=q_codes[:].bitcast(FP8X4),
-                    lhsT_scale=q_scales[:],
-                    rhs=kw_got[h][:].bitcast(FP8X4),
-                    rhs_scale=ks_got[:, b * N + h * PAGE : b * N + (h + 1) * PAGE],
+                    out=raw[:, c, :],
+                    lhsT=kw_got[g][:, c * P : (c + 1) * P].bitcast(FP8X4),
+                    lhsT_scale=ks_got[:, g * PAGE + c * P : g * PAGE + (c + 1) * P],
+                    rhs=q_codes[:].bitcast(FP8X4),
+                    rhs_scale=q_scales[:],
                     start=True,
                     stop=True,
                 )
-                nc.scalar.copy(raw[:, h * PAGE : (h + 1) * PAGE], bank[:])
-            return raw
+            biased = sb([P, PACK, NQ], F32, f"biased{g}")
+            for c in range(PACK):
+                nc.scalar.activation(biased[:, c, :], raw[:, c, :], ACT.Identity, bias=kb_cols[:, g, c : c + 1])
+            scores.append(bank([P, PAGE], "scores", "scores", 3))
+            for c in range(PACK):
+                nc.tensor.transpose(scores[g][:, c * P : (c + 1) * P], biased[:, c, :], ident[:])
 
-        def add_bias(b, c0, c1):
-            nc.vector.tensor_tensor(
-                scores[b][:, c0:c1], kb_pool[:].indirect(entries(b * N + c0, c1 - c0)), raws[b][:, c0:c1], ALU.add
+        gather_keys(0)
+        score_page(0)
+        gather_keys(1)
+        score_page(1)
+        q_bf1 = round_queries(1, nc.vector.tensor_copy)
+        gather_keys(2)
+        queries.append(quantise_queries(1, q_bf1))
+        score_page(2)
+        gather_keys(3)
+        score_page(3)
+
+        negated, neg_max, probs, page_sums = [], [], [], []
+
+        def page_maximum(g):
+            negated.append(sb([P, PACK, P], F32, f"negated{g}"))
+            neg_max.append(sb([P, 1], F32, f"neg_max{g}"))
+            nc.vector.tensor_scalar(
+                negated[g][:],
+                scores[g][:].rearrange("q (s t) -> q t s", t=PACK),
+                -1.0,
+                neg_max[g - 1][:] if g % SEQ_PAGES else None,
+                ALU.mult,
+                ALU.min,
+                accum_out=neg_max[g][:],
             )
 
-        def softmax_numerators(b, biased):
-            neg_max = sb([P, 1], F32, f"neg_max{b}", reuses="q_raw1")
-            nc.vector.tensor_reduce(neg_max[:], biased[:], AXIS.X, ALU.max, negate=True)
-            for h in range(SEQ_PAGES):
-                probs[b, h] = sb([P, PAGE], F32, f"p{b}{h}")
-                page_sums[b, h] = sb([P, 1], F32, f"page_sum{b}{h}")
+        turned_p = []
+
+        def numerators(b):
+            for g in range(b * SEQ_PAGES, (b + 1) * SEQ_PAGES):
+                probs.append(sb([P, PACK, P], F32, f"p{g}"))
+                page_sums.append(sb([P, 1], F32, f"page_sum{g}"))
                 nc.scalar.activation(
-                    probs[b, h][:],
-                    biased[:, h * PAGE : (h + 1) * PAGE],
+                    probs[g][:],
+                    negated[g][:],
                     ACT.Exp,
-                    bias=neg_max[:],
-                    accum_out=page_sums[b, h][:],
+                    bias=neg_max[(b + 1) * SEQ_PAGES - 1][:],
+                    scale=-1.0,
+                    accum_out=page_sums[g][:],
                 )
+                turned_p.append(bank([P, PACK, NQ], "turned_p", "turn", 3))
+                for t in range(PACK):
+                    nc.tensor.transpose(turned_p[g][:, t, :], probs[g][:, t, :], ident[:])
 
-        def weigh_and_turn(b, h, cuts, turned):
-            w32 = sb([P, PAGE], F32, f"w32_{b}{h}")
-            w_pairs = sb([P, 2, P, 2], BF16, f"w_pairs{b}{h}")
-            for c0, c1 in zip(cuts, cuts[1:]):
-                nc.vector.tensor_tensor(
-                    w32[:, c0:c1],
-                    vs_pool[:].indirect(entries(b * N + h * PAGE + c0, c1 - c0)),
-                    probs[b, h][:, c0:c1],
-                    ALU.mult,
-                )
-                nc.scalar.copy(
-                    w_pairs[:, :, c0 // PACK : c1 // PACK, :],
-                    w32[:, c0:c1].rearrange("q (s u e) -> q u s e", u=2, e=2),
-                )
-            words = w_pairs[:].rearrange("q u s e -> q (u s e)").bitcast(F32)
-            for u in range(2):
-                nc.tensor.transpose(turned[:, u, :], words[:, u * P : (u + 1) * P], ident[:])
-
-        def interleave(grouped, turned):
-            nc.scalar.copy(
-                grouped.rearrange("s h q t -> s h (q t)").bitcast(F32).rearrange("s h (q u) -> s h q u", u=2),
-                turned.rearrange("s h u q -> s h q u"),
-            )
-
-        probs, page_sums = {}, {}
-        w_grouped = [sb([P, SEQ_PAGES, NQ, PACK], BF16, f"w_grouped{b}") for b in range(B)]
-
-        spread_bias()
-        ks_got = sb([P, B * N], U8, "ks_got")
-        nc.vector.tensor_copy(ks_got[:], ks_pool[:].bitcast(U8).indirect(offsets[:]))
-
-        queries = [quantise_queries(b) for b in range(B)]
-        raws = []
-        for b in range(B):
-            kw_got = gather_key_words(b)
-            raws.append(raw_scores(b, *queries[b], kw_got))
-        scores = [sb([P, N], F32, f"biased{b}") for b in range(B)]
-        add_bias(0, 0, PAGE)
-        add_bias(0, PAGE, N)
-        add_bias(1, 0, FIRST_SUM)
-        softmax_numerators(0, scores[0])
-        add_bias(1, FIRST_SUM, N)
-        softmax_numerators(1, scores[1])
-
-        first_turned = page_bank([P, SEQ_PAGES, 2, NQ], "first_turned")
-        for h in range(SEQ_PAGES):
-            weigh_and_turn(0, h, (0, PAGE), first_turned[:, h])
-        last_turned = []
-        for h, cuts in enumerate(((0, PAGE), (0, PAGE - LAST_PIECE, PAGE))):
-            last_turned.append(page_bank([P, 1, 2, NQ], "last_turned"))
-            weigh_and_turn(1, h, cuts, last_turned[h][:, 0])
-        interleave(w_grouped[0][:], first_turned[:])
-        for h in range(SEQ_PAGES):
-            interleave(w_grouped[1][:, h : h + 1], last_turned[h][:])
+        vsc_got = sb([P, PAGES * DV], U8, "vsc_got")
+        vw_got = sb([P, PAGES * DV], U32, "vw_got")
+        page_maximum(0)
+        nc.vector.tensor_copy(vsc_got[:], vsc_pool[:].bitcast(U8).indirect(v_offsets[:]))
+        page_maximum(1)
+        numerators(0)
+        page_maximum(2)
+        nc.vector.tensor_copy(vw_got[:], vw_pool[:].bitcast(U32).indirect(v_offsets[:]))
+        page_maximum(3)
+        numerators(1)
 
         row_sums = sb([P, B], F32, "row_sums")
         for b in range(B):
             nc.scalar.activation(
-                row_sums[:, b : b + 1], page_sums[b, 0][:], ACT.Identity, bias=page_sums[b, 1][:]
+                row_sums[:, b : b + 1], page_sums[2 * b][:], ACT.Identity, bias=page_sums[2 * b + 1][:]
+            )
+        inverse = sb([P, B], F32, "inverse")
+
+        w = [sb([P, SEQ_PAGES, NQ, PACK], BF16, f"w{b}") for b in range(B)]
+        w_codes = [sb([P, SEQ_PAGES * NQ], U32, f"w_codes{b}") for b in range(B)]
+        w_scales = [sb([P, SEQ_PAGES * NQ], U8, f"w_scales{b}") for b in range(B)]
+
+        def weigh(g):
+            nc.vector.tensor_tensor(
+                w[g // SEQ_PAGES][:, g % SEQ_PAGES],
+                turned_p[g][:].rearrange("s t q -> s q t"),
+                vs_cols[g][:].to_broadcast([P, NQ, PACK]),
+                ALU.mult,
             )
 
-        vsc_got = sb([P, B * SEQ_PAGES * DV], U8, "vsc_got", reuses="p10")
-        nc.vector.tensor_copy(vsc_got[:], vsc_pool[:].bitcast(U8).indirect(v_offsets[:]))
-        vw_got = sb([P, B * SEQ_PAGES * DV], U32, "vw_got", reuses="w32_10")
-        nc.vector.tensor_copy(vw_got[:], vw_pool[:].bitcast(U32).indirect(v_offsets[:]))
+        def quantise_weights(b, c0, c1):
+            nc.vector.quantize_mx(
+                out=w_codes[b][:, c0:c1].bitcast(FP8X4),
+                scales=w_scales[b][:, c0:c1],
+                in_=w[b][:].rearrange("s h q t -> s (h q t)")[:, PACK * c0 : PACK * c1],
+            )
 
-        inverse = sb([P, B], F32, "inverse")
-        nc.vector.reciprocal(inverse[:], row_sums[:])
-
-        for b in range(B):
-            y = page_bank([P, DV], "y")
-            w_codes = sb([P, SEQ_PAGES * NQ], U32, f"w_codes{b}", reuses=("p11", "vw_pool")[b])
-            w_scales = sb([P, SEQ_PAGES * NQ], U8, f"w_scales{b}", reuses=("vsc_pool", None)[b])
-            w_flat = w_grouped[b][:].rearrange("s h q t -> s (h q t)")
-            width = SEQ_PAGES * NQ if b == 0 else NQ
-            for c0 in range(0, SEQ_PAGES * NQ, width):
-                nc.vector.quantize_mx(
-                    out=w_codes[:, c0 : c0 + width].bitcast(FP8X4),
-                    scales=w_scales[:, c0 : c0 + width],
-                    in_=w_flat[:, PACK * c0 : PACK * (c0 + width)],
-                )
+        def finish(b):
+            y = bank([P, DV], "y", "raw", 2)
             for h in range(SEQ_PAGES):
                 page_cols = slice((SEQ_PAGES * b + h) * DV, (SEQ_PAGES * b + h + 1) * DV)
                 nc.tensor.matmul_mx(
                     out=y[:],
-                    lhsT=w_codes[:, h * NQ : (h + 1) * NQ].bitcast(FP8X4),
-                    lhsT_scale=w_scales[:, h * NQ : (h + 1) * NQ],
+                    lhsT=w_codes[b][:, h * NQ : (h + 1) * NQ].bitcast(FP8X4),
+                    lhsT_scale=w_scales[b][:, h * NQ : (h + 1) * NQ],
                     rhs=vw_got[:, page_cols].bitcast(FP8X4),
                     rhs_scale=vsc_got[:, page_cols],
                     start=(h == 0),
@@ -257,3 +258,14 @@ def tile_attend_pkv8_soft_kb_kernel(
             result = sb([P, DV], F32, f"result{b}")
             nc.scalar.activation(result[:], y[:], ACT.Copy, scale=inverse[:, b : b + 1])
             nc.sync.dma_start(out[b], result[:])
+
+        weigh(0)
+        weigh(1)
+        weigh(2)
+        quantise_weights(0, 0, SEQ_PAGES * NQ)
+        nc.vector.reciprocal(inverse[:], row_sums[:])
+        weigh(3)
+        quantise_weights(1, 0, NQ)
+        quantise_weights(1, NQ, SEQ_PAGES * NQ)
+        finish(0)
+        finish(1)

@@ -16,8 +16,8 @@ QUADRANT = 32
 KS_WORDS = T // 4
 ROW = P - 1
 KB_ON_GPSIMD = 1792
-VS_ON_VECTOR = 1536
-VS_PIECE = 640
+VS_ON_VECTOR = 512
+VS_PIECE = 512
 
 F32 = mybir.dt.float32
 BF16 = mybir.dt.bfloat16
@@ -53,8 +53,8 @@ def tile_attend_pkv8_soft_kb_kernel(
         ks_pool = sb([P, KS_WORDS], I32, "ks_pool")
         kw_pool = sb([P, T], I32, "kw_pool")
         vw_pool = sb([P, POOL_PAGES * DV], I32, "vw_pool")
-        vs_pool = sb([P, T], F32, "vs_pool")
         kb_pool = sb([P, T], F32, "kb_pool")
+        vs_pool = sb([P, T], F32, "vs_pool")
         vsc_pool = sb([P, POOL_PAGES * DV // 4], I32, "vsc_pool")
         q_raw = [sb([P, PACK, NQ], F32, f"q_raw{b}") for b in range(B)]
         ident = sb([P, P], F32, "ident")
@@ -68,21 +68,21 @@ def tile_attend_pkv8_soft_kb_kernel(
         nc.gpsimd.memset(kb_pool[:ROW, :KB_ON_GPSIMD], 0.0)
         zero_on_vector(kb_pool, KB_ON_GPSIMD, T)
         make_identity(nc, ident[:])
-        nc.gpsimd.memset(vsc_pool[:], 0)
         zero_on_vector(vs_pool, 0, VS_ON_VECTOR)
         for c0 in range(VS_ON_VECTOR, T, VS_PIECE):
             nc.gpsimd.memset(vs_pool[:ROW, c0 : c0 + VS_PIECE], 0.0)
+        nc.gpsimd.memset(vsc_pool[:], 0)
 
         def load_queries(b):
             nc.sync.dma_start(q_raw[b][:], qT[b].rearrange("(s t) q -> s t q", t=PACK))
 
-        load_queries(0)
         nc.sync.dma_start(offsets[:], offs)
-        nc.sync.dma_start(kb_pool[ROW:, :], kb[0:1, :])
-        nc.sync.dma_start(vs_pool[ROW:, :], vs[0:1, :])
+        nc.scalar.dma_start(kb_pool[ROW:, :], kb[0:1, :])
+        load_queries(0)
         ks_rows = k_scales[0].bitcast(I32)
         for r in range(4):
             nc.sync.dma_start(ks_pool[r:P:QUADRANT, :], ks_rows[r:SCALE_ROWS:4, :])
+        nc.sync.dma_start(vs_pool[ROW:, :], vs[0:1, :])
         nc.sync.dma_start(kw_pool[:], k_words[0].rearrange("s n t -> s (n t)").bitcast(I32))
         load_queries(1)
         nc.sync.dma_start(v_offsets[:], voffs)
@@ -125,8 +125,9 @@ def tile_attend_pkv8_soft_kb_kernel(
             nc.scalar.copy(kb_cols[:, g, :], turned[:, :, ROW])
 
         vs_cols = []
-        for g in range(PAGES):
-            vs_got = sb([P, PAGE], F32, f"vs_got{g}")
+
+        def gather_token_scales(g, reuses=None):
+            vs_got = sb([P, PAGE], F32, f"vs_got{g}", reuses=reuses)
             nc.scalar.activation(vs_got[:], vs_pool[:].indirect(entries(g)), ACT.Copy)
             vs_cols.append(sb([P, 1, PACK], F32, f"vs_cols{g}"))
             nc.sync.dma_start(vs_cols[g][:, 0, :], vs_got[ROW:, :].rearrange("o (s t) -> o s t", t=PACK))
@@ -137,8 +138,8 @@ def tile_attend_pkv8_soft_kb_kernel(
 
         kw_got, scores = [], []
 
-        def gather_keys(g):
-            kw_got.append(sb([P, PAGE], U32, f"kw_got{g}"))
+        def gather_keys(g, reuses=None):
+            kw_got.append(sb([P, PAGE], U32, f"kw_got{g}", reuses=reuses))
             nc.vector.tensor_copy(kw_got[g][:], kw_pool[:].bitcast(U32).indirect(entries(g)))
 
         def score_page(g):
@@ -154,22 +155,25 @@ def tile_attend_pkv8_soft_kb_kernel(
                     start=True,
                     stop=True,
                 )
-            biased = sb([P, PACK, NQ], F32, f"biased{g}")
+            biased = [sb([P, NQ], F32, f"biased{g}{c}") for c in range(PACK)]
             for c in range(PACK):
-                nc.scalar.activation(biased[:, c, :], raw[:, c, :], ACT.Identity, bias=kb_cols[:, g, c : c + 1])
+                nc.scalar.activation(biased[c][:], raw[:, c, :], ACT.Identity, bias=kb_cols[:, g, c : c + 1])
             scores.append(bank([P, PAGE], "scores", "scores", 3))
             for c in range(PACK):
-                nc.tensor.transpose(scores[g][:, c * P : (c + 1) * P], biased[:, c, :], ident[:])
+                nc.tensor.transpose(scores[g][:, c * P : (c + 1) * P], biased[c][:], ident[:])
 
         gather_keys(0)
-        score_page(0)
         gather_keys(1)
-        score_page(1)
+        for g in range(PAGES - 1):
+            gather_token_scales(g)
+        score_page(0)
         q_bf1 = round_queries(1, nc.vector.tensor_copy)
-        gather_keys(2)
+        gather_keys(2, reuses="kw_got0")
+        score_page(1)
         queries.append(quantise_queries(1, q_bf1))
+        gather_keys(3, reuses="kw_got1")
+        gather_token_scales(PAGES - 1, reuses="biased10")
         score_page(2)
-        gather_keys(3)
         score_page(3)
 
         negated, neg_max, probs, page_sums = [], [], [], []
@@ -205,13 +209,13 @@ def tile_attend_pkv8_soft_kb_kernel(
                 for t in range(PACK):
                     nc.tensor.transpose(turned_p[g][:, t, :], probs[g][:, t, :], ident[:])
 
-        vsc_got = sb([P, PAGES * DV], U8, "vsc_got")
-        vw_got = sb([P, PAGES * DV], U32, "vw_got")
         page_maximum(0)
+        vsc_got = sb([P, PAGES * DV], U8, "vsc_got", reuses="biased03")
         nc.vector.tensor_copy(vsc_got[:], vsc_pool[:].bitcast(U8).indirect(v_offsets[:]))
         page_maximum(1)
         numerators(0)
         page_maximum(2)
+        vw_got = sb([P, PAGES * DV], U32, "vw_got", reuses="biased23")
         nc.vector.tensor_copy(vw_got[:], vw_pool[:].bitcast(U32).indirect(v_offsets[:]))
         page_maximum(3)
         numerators(1)
@@ -261,11 +265,12 @@ def tile_attend_pkv8_soft_kb_kernel(
 
         weigh(0)
         weigh(1)
+        quantise_weights(0, 0, NQ)
         weigh(2)
-        quantise_weights(0, 0, SEQ_PAGES * NQ)
-        nc.vector.reciprocal(inverse[:], row_sums[:])
+        quantise_weights(0, NQ, SEQ_PAGES * NQ)
         weigh(3)
         quantise_weights(1, 0, NQ)
+        nc.vector.reciprocal(inverse[:], row_sums[:])
         quantise_weights(1, NQ, SEQ_PAGES * NQ)
         finish(0)
         finish(1)

@@ -16,8 +16,8 @@ QUADRANT = 32
 KS_WORDS = T // 4
 ROW = P - 1
 KB_ON_GPSIMD = 1792
-VS_ON_VECTOR = 512
-VS_PIECE = 512
+VS_ON_VECTOR = 1024
+VS_PIECE = 1024
 
 F32 = mybir.dt.float32
 BF16 = mybir.dt.bfloat16
@@ -52,7 +52,6 @@ def tile_attend_pkv8_soft_kb_kernel(
 
         ks_pool = sb([P, KS_WORDS], I32, "ks_pool")
         kw_pool = sb([P, T], I32, "kw_pool")
-        vw_pool = sb([P, POOL_PAGES * DV], I32, "vw_pool")
         kb_pool = sb([P, T], F32, "kb_pool")
         vs_pool = sb([P, T], F32, "vs_pool")
         vsc_pool = sb([P, POOL_PAGES * DV // 4], I32, "vsc_pool")
@@ -71,7 +70,8 @@ def tile_attend_pkv8_soft_kb_kernel(
         zero_on_vector(vs_pool, 0, VS_ON_VECTOR)
         for c0 in range(VS_ON_VECTOR, T, VS_PIECE):
             nc.gpsimd.memset(vs_pool[:ROW, c0 : c0 + VS_PIECE], 0.0)
-        nc.gpsimd.memset(vsc_pool[:], 0)
+        nc.vector.memset(vsc_pool[:, :127], 0)
+        nc.vector.memset(vsc_pool[:, 127:], 0)
 
         def load_queries(b):
             nc.sync.dma_start(q_raw[b][:], qT[b].rearrange("(s t) q -> s t q", t=PACK))
@@ -92,10 +92,6 @@ def tile_attend_pkv8_soft_kb_kernel(
                 vsc_pool[r:P:QUADRANT, :].rearrange("s (u c) -> s u c", u=POOL_PAGES),
                 vsc_rows[r:SCALE_ROWS:4],
             )
-        nc.sync.dma_start(
-            vw_pool[:].rearrange("s (u e) -> s u e", u=POOL_PAGES),
-            v_words.rearrange("u s e t -> s u (e t)").bitcast(I32),
-        )
 
         def entries(g):
             return offsets[:, g * PAGE // LIST : (g + 1) * PAGE // LIST]
@@ -124,17 +120,25 @@ def tile_attend_pkv8_soft_kb_kernel(
                 nc.tensor.transpose(turned[:, c, :], kb_got[:, c * P : (c + 1) * P], ident[:])
             nc.scalar.copy(kb_cols[:, g, :], turned[:, :, ROW])
 
-        vs_cols = []
+        vs_cols = {}
 
         def gather_token_scales(g, reuses=None):
             vs_got = sb([P, PAGE], F32, f"vs_got{g}", reuses=reuses)
-            nc.scalar.activation(vs_got[:], vs_pool[:].indirect(entries(g)), ACT.Copy)
-            vs_cols.append(sb([P, 1, PACK], F32, f"vs_cols{g}"))
+            if g == PAGES - 1:
+                nc.vector.tensor_copy(vs_got[:], vs_pool[:].indirect(entries(g)))
+            else:
+                nc.scalar.activation(vs_got[:], vs_pool[:].indirect(entries(g)), ACT.Copy)
+            vs_cols[g] = sb([P, 1, PACK], F32, f"vs_cols{g}")
             nc.sync.dma_start(vs_cols[g][:, 0, :], vs_got[ROW:, :].rearrange("o (s t) -> o s t", t=PACK))
 
         ks_got = sb([P, B * N], U8, "ks_got")
         nc.vector.tensor_copy(ks_got[:], ks_pool[:].bitcast(U8).indirect(offsets[:]))
         queries = [quantise_queries(0, q_bf0)]
+        vw_pool = sb([P, POOL_PAGES * DV], I32, "vw_pool", reuses="ks_pool")
+        nc.sync.dma_start(
+            vw_pool[:].rearrange("s (u e) -> s u e", u=POOL_PAGES),
+            v_words.rearrange("u s e t -> s u (e t)").bitcast(I32),
+        )
 
         kw_got, scores = [], []
 
@@ -162,17 +166,18 @@ def tile_attend_pkv8_soft_kb_kernel(
             for c in range(PACK):
                 nc.tensor.transpose(scores[g][:, c * P : (c + 1) * P], biased[c][:], ident[:])
 
+        gather_token_scales(0)
+        gather_token_scales(1)
+        gather_token_scales(3)
         gather_keys(0)
         gather_keys(1)
-        for g in range(PAGES - 1):
-            gather_token_scales(g)
         score_page(0)
         q_bf1 = round_queries(1, nc.vector.tensor_copy)
         gather_keys(2, reuses="kw_got0")
         score_page(1)
         queries.append(quantise_queries(1, q_bf1))
         gather_keys(3, reuses="kw_got1")
-        gather_token_scales(PAGES - 1, reuses="biased10")
+        gather_token_scales(2, reuses="biased10")
         score_page(2)
         score_page(3)
 

@@ -13,7 +13,6 @@ PAGES = B * SEQ_PAGES
 LIST = 16
 SCALE_ROWS = 16
 QUADRANT = 32
-KS_WORDS = T // 4
 ROW = P - 1
 KB_ON_GPSIMD = 1792
 VS_ON_VECTOR = 1024
@@ -44,14 +43,21 @@ def tile_attend_pkv8_soft_kb_kernel(
         def sb(shape, dtype, name, reuses=None):
             return keep.tile(shape, dtype, name=name, tag=reuses or name, align_bytes=64)
 
-        def bank(shape, name, tag, bufs):
-            return psum.tile(shape, F32, name=name, tag=tag, bufs=bufs)
+        def raw_bank(shape, name):
+            return psum.tile(shape, F32, name=name, tag="raw", bufs=2)
+
+        def scores_bank():
+            return psum.tile([P, PAGE], F32, name="scores", tag="scores", bufs=3)
+
+        def turn_bank(name):
+            return psum.tile([P, PACK, P], F32, name=name, tag="turn", bufs=3)
 
         offsets = lists.tile([P, B * N // LIST], U16, name="offsets")
         v_offsets = lists.tile([P, PAGES * DV // LIST], U16, name="v_offsets")
 
-        ks_pool = sb([P, KS_WORDS], I32, "ks_pool")
+        ks_pool = sb([P, T // 4], I32, "ks_pool")
         kw_pool = sb([P, T], I32, "kw_pool")
+        vw_pool = sb([P, POOL_PAGES * DV], I32, "vw_pool")
         kb_pool = sb([P, T], F32, "kb_pool")
         vs_pool = sb([P, T], F32, "vs_pool")
         vsc_pool = sb([P, POOL_PAGES * DV // 4], I32, "vsc_pool")
@@ -70,8 +76,7 @@ def tile_attend_pkv8_soft_kb_kernel(
         zero_on_vector(vs_pool, 0, VS_ON_VECTOR)
         for c0 in range(VS_ON_VECTOR, T, VS_PIECE):
             nc.gpsimd.memset(vs_pool[:ROW, c0 : c0 + VS_PIECE], 0.0)
-        nc.vector.memset(vsc_pool[:, :127], 0)
-        nc.vector.memset(vsc_pool[:, 127:], 0)
+        nc.gpsimd.memset(vsc_pool[:], 0)
 
         def load_queries(b):
             nc.sync.dma_start(q_raw[b][:], qT[b].rearrange("(s t) q -> s t q", t=PACK))
@@ -92,13 +97,17 @@ def tile_attend_pkv8_soft_kb_kernel(
                 vsc_pool[r:P:QUADRANT, :].rearrange("s (u c) -> s u c", u=POOL_PAGES),
                 vsc_rows[r:SCALE_ROWS:4],
             )
+        nc.sync.dma_start(
+            vw_pool[:].rearrange("s (u e) -> s u e", u=POOL_PAGES),
+            v_words.rearrange("u s e t -> s u (e t)").bitcast(I32),
+        )
 
         def entries(g):
             return offsets[:, g * PAGE // LIST : (g + 1) * PAGE // LIST]
 
-        def round_queries(b, copy):
+        def round_queries(b):
             q_bf = sb([P, NQ, PACK], BF16, f"q_bf{b}")
-            copy(q_bf[:], q_raw[b][:].rearrange("s t q -> s q t"))
+            nc.scalar.copy(q_bf[:], q_raw[b][:].rearrange("s t q -> s q t"))
             return q_bf
 
         def quantise_queries(b, q_bf):
@@ -109,36 +118,28 @@ def tile_attend_pkv8_soft_kb_kernel(
             )
             return codes, scales
 
-        q_bf0 = round_queries(0, nc.scalar.copy)
+        q_bf0 = round_queries(0)
 
         kb_cols = sb([P, PAGES, PACK], F32, "kb_cols")
         for g in range(PAGES):
             kb_got = sb([P, PAGE], F32, f"kb_got{g}")
             nc.scalar.activation(kb_got[:], kb_pool[:].indirect(entries(g)), ACT.Copy)
-            turned = bank([P, PACK, P], "kb_turned", "turn", 3)
+            turned = turn_bank("kb_turned")
             for c in range(PACK):
                 nc.tensor.transpose(turned[:, c, :], kb_got[:, c * P : (c + 1) * P], ident[:])
             nc.scalar.copy(kb_cols[:, g, :], turned[:, :, ROW])
 
-        vs_cols = {}
+        vs_cols = []
 
         def gather_token_scales(g, reuses=None):
             vs_got = sb([P, PAGE], F32, f"vs_got{g}", reuses=reuses)
-            if g == PAGES - 1:
-                nc.vector.tensor_copy(vs_got[:], vs_pool[:].indirect(entries(g)))
-            else:
-                nc.scalar.activation(vs_got[:], vs_pool[:].indirect(entries(g)), ACT.Copy)
-            vs_cols[g] = sb([P, 1, PACK], F32, f"vs_cols{g}")
+            nc.scalar.activation(vs_got[:], vs_pool[:].indirect(entries(g)), ACT.Copy)
+            vs_cols.append(sb([P, 1, PACK], F32, f"vs_cols{g}"))
             nc.sync.dma_start(vs_cols[g][:, 0, :], vs_got[ROW:, :].rearrange("o (s t) -> o s t", t=PACK))
 
         ks_got = sb([P, B * N], U8, "ks_got")
         nc.vector.tensor_copy(ks_got[:], ks_pool[:].bitcast(U8).indirect(offsets[:]))
         queries = [quantise_queries(0, q_bf0)]
-        vw_pool = sb([P, POOL_PAGES * DV], I32, "vw_pool", reuses="ks_pool")
-        nc.sync.dma_start(
-            vw_pool[:].rearrange("s (u e) -> s u e", u=POOL_PAGES),
-            v_words.rearrange("u s e t -> s u (e t)").bitcast(I32),
-        )
 
         kw_got, scores = [], []
 
@@ -148,7 +149,7 @@ def tile_attend_pkv8_soft_kb_kernel(
 
         def score_page(g):
             q_codes, q_scales = queries[g // SEQ_PAGES]
-            raw = bank([P, PACK, NQ], "raw", "raw", 2)
+            raw = raw_bank([P, PACK, NQ], "raw")
             for c in range(PACK):
                 nc.tensor.matmul_mx(
                     out=raw[:, c, :],
@@ -162,26 +163,26 @@ def tile_attend_pkv8_soft_kb_kernel(
             biased = [sb([P, NQ], F32, f"biased{g}{c}") for c in range(PACK)]
             for c in range(PACK):
                 nc.scalar.activation(biased[c][:], raw[:, c, :], ACT.Identity, bias=kb_cols[:, g, c : c + 1])
-            scores.append(bank([P, PAGE], "scores", "scores", 3))
+            scores.append(scores_bank())
             for c in range(PACK):
                 nc.tensor.transpose(scores[g][:, c * P : (c + 1) * P], biased[c][:], ident[:])
 
         gather_token_scales(0)
         gather_token_scales(1)
-        gather_token_scales(3)
         gather_keys(0)
         gather_keys(1)
+        q_bf1 = round_queries(1)
         score_page(0)
-        q_bf1 = round_queries(1, nc.vector.tensor_copy)
-        gather_keys(2, reuses="kw_got0")
+        gather_keys(2)
         score_page(1)
         queries.append(quantise_queries(1, q_bf1))
         gather_keys(3, reuses="kw_got1")
         gather_token_scales(2, reuses="biased10")
         score_page(2)
         score_page(3)
+        gather_token_scales(3, reuses="biased20")
 
-        negated, neg_max, probs, page_sums = [], [], [], []
+        negated, neg_max, page_sums, turned_p = [], [], [], []
 
         def page_maximum(g):
             negated.append(sb([P, PACK, P], F32, f"negated{g}"))
@@ -196,23 +197,21 @@ def tile_attend_pkv8_soft_kb_kernel(
                 accum_out=neg_max[g][:],
             )
 
-        turned_p = []
-
         def numerators(b):
             for g in range(b * SEQ_PAGES, (b + 1) * SEQ_PAGES):
-                probs.append(sb([P, PACK, P], F32, f"p{g}"))
+                probs = sb([P, PACK, P], F32, f"p{g}")
                 page_sums.append(sb([P, 1], F32, f"page_sum{g}"))
                 nc.scalar.activation(
-                    probs[g][:],
+                    probs[:],
                     negated[g][:],
                     ACT.Exp,
                     bias=neg_max[(b + 1) * SEQ_PAGES - 1][:],
                     scale=-1.0,
                     accum_out=page_sums[g][:],
                 )
-                turned_p.append(bank([P, PACK, NQ], "turned_p", "turn", 3))
+                turned_p.append(turn_bank("turned_p"))
                 for t in range(PACK):
-                    nc.tensor.transpose(turned_p[g][:, t, :], probs[g][:, t, :], ident[:])
+                    nc.tensor.transpose(turned_p[g][:, t, :], probs[:, t, :], ident[:])
 
         page_maximum(0)
         vsc_got = sb([P, PAGES * DV], U8, "vsc_got", reuses="biased03")
@@ -227,9 +226,8 @@ def tile_attend_pkv8_soft_kb_kernel(
 
         row_sums = sb([P, B], F32, "row_sums")
         for b in range(B):
-            nc.scalar.activation(
-                row_sums[:, b : b + 1], page_sums[2 * b][:], ACT.Identity, bias=page_sums[2 * b + 1][:]
-            )
+            first, second = page_sums[b * SEQ_PAGES : (b + 1) * SEQ_PAGES]
+            nc.scalar.activation(row_sums[:, b : b + 1], first[:], ACT.Identity, bias=second[:])
         inverse = sb([P, B], F32, "inverse")
 
         w = [sb([P, SEQ_PAGES, NQ, PACK], BF16, f"w{b}") for b in range(B)]
@@ -244,38 +242,34 @@ def tile_attend_pkv8_soft_kb_kernel(
                 ALU.mult,
             )
 
-        def quantise_weights(b, c0, c1):
+        def quantise_weights(g):
+            b, c0 = g // SEQ_PAGES, g % SEQ_PAGES * NQ
             nc.vector.quantize_mx(
-                out=w_codes[b][:, c0:c1].bitcast(FP8X4),
-                scales=w_scales[b][:, c0:c1],
-                in_=w[b][:].rearrange("s h q t -> s (h q t)")[:, PACK * c0 : PACK * c1],
+                out=w_codes[b][:, c0 : c0 + NQ].bitcast(FP8X4),
+                scales=w_scales[b][:, c0 : c0 + NQ],
+                in_=w[b][:].rearrange("s h q t -> s (h q t)")[:, PACK * c0 : PACK * (c0 + NQ)],
             )
 
-        def finish(b):
-            y = bank([P, DV], "y", "raw", 2)
+        weigh(0)
+        for g in range(1, PAGES):
+            weigh(g)
+            quantise_weights(g - 1)
+        nc.vector.reciprocal(inverse[:], row_sums[:])
+        quantise_weights(PAGES - 1)
+
+        for b in range(B):
+            y = raw_bank([P, DV], "y")
             for h in range(SEQ_PAGES):
-                page_cols = slice((SEQ_PAGES * b + h) * DV, (SEQ_PAGES * b + h + 1) * DV)
+                g = SEQ_PAGES * b + h
                 nc.tensor.matmul_mx(
                     out=y[:],
                     lhsT=w_codes[b][:, h * NQ : (h + 1) * NQ].bitcast(FP8X4),
                     lhsT_scale=w_scales[b][:, h * NQ : (h + 1) * NQ],
-                    rhs=vw_got[:, page_cols].bitcast(FP8X4),
-                    rhs_scale=vsc_got[:, page_cols],
+                    rhs=vw_got[:, g * DV : (g + 1) * DV].bitcast(FP8X4),
+                    rhs_scale=vsc_got[:, g * DV : (g + 1) * DV],
                     start=(h == 0),
                     stop=(h == SEQ_PAGES - 1),
                 )
             result = sb([P, DV], F32, f"result{b}")
             nc.scalar.activation(result[:], y[:], ACT.Copy, scale=inverse[:, b : b + 1])
             nc.sync.dma_start(out[b], result[:])
-
-        weigh(0)
-        weigh(1)
-        quantise_weights(0, 0, NQ)
-        weigh(2)
-        quantise_weights(0, NQ, SEQ_PAGES * NQ)
-        weigh(3)
-        quantise_weights(1, 0, NQ)
-        nc.vector.reciprocal(inverse[:], row_sums[:])
-        quantise_weights(1, NQ, SEQ_PAGES * NQ)
-        finish(0)
-        finish(1)

@@ -14,9 +14,10 @@ LIST = 16
 SCALE_ROWS = 16
 QUADRANT = 32
 ROW = P - 1
-KB_ON_GPSIMD = 1792
-VS_ON_VECTOR = 1024
-VS_PIECE = 1024
+KS_ON_GPSIMD = 640
+KB_ON_GPSIMD = 2048
+VS_ON_VECTOR = 1664
+EARLY_WORDS = 1536
 
 F32 = mybir.dt.float32
 BF16 = mybir.dt.bfloat16
@@ -27,6 +28,7 @@ U8 = mybir.dt.uint8
 FP8X4 = mybir.dt.float8_e4m3fn_x4
 ALU = mybir.AluOpType
 ACT = mybir.ActivationFunctionType
+AXIS = mybir.AxisListType
 
 FLOPS = 2 * B * NQ * N * (D + DV)
 
@@ -43,14 +45,11 @@ def tile_attend_pkv8_soft_kb_kernel(
         def sb(shape, dtype, name, reuses=None):
             return keep.tile(shape, dtype, name=name, tag=reuses or name, align_bytes=64)
 
-        def raw_bank(shape, name):
-            return psum.tile(shape, F32, name=name, tag="raw", bufs=2)
+        def slot_bank(name):
+            return psum.tile([P, PACK, NQ], F32, name=name, tag="slot_major", bufs=4)
 
-        def scores_bank():
-            return psum.tile([P, PAGE], F32, name="scores", tag="scores", bufs=3)
-
-        def turn_bank(name):
-            return psum.tile([P, PACK, P], F32, name=name, tag="turn", bufs=3)
+        def query_bank(shape, name, g):
+            return psum.tile(shape, F32, name=name, tag=f"query_major{g}")
 
         offsets = lists.tile([P, B * N // LIST], U16, name="offsets")
         v_offsets = lists.tile([P, PAGES * DV // LIST], U16, name="v_offsets")
@@ -64,18 +63,19 @@ def tile_attend_pkv8_soft_kb_kernel(
         q_raw = [sb([P, PACK, NQ], F32, f"q_raw{b}") for b in range(B)]
         ident = sb([P, P], F32, "ident")
 
-        def zero_on_vector(pool, c0, c1):
+        def zero_on_vector(rows, c0, c1):
             mid = (c0 + c1) // 2 - 1
-            nc.vector.memset(pool[:ROW, c0:mid], 0.0)
-            nc.vector.memset(pool[:ROW, mid:c1], 0.0)
+            nc.vector.memset(rows[:, c0:mid], 0)
+            nc.vector.memset(rows[:, mid:c1], 0)
 
-        nc.gpsimd.memset(ks_pool[:], 0)
+        nc.gpsimd.memset(ks_pool[:, :KS_ON_GPSIMD], 0)
+        zero_on_vector(ks_pool[:], KS_ON_GPSIMD, T // 4)
+        nc.gpsimd.memset(ident[:], 0.0)
         nc.gpsimd.memset(kb_pool[:ROW, :KB_ON_GPSIMD], 0.0)
-        zero_on_vector(kb_pool, KB_ON_GPSIMD, T)
-        make_identity(nc, ident[:])
-        zero_on_vector(vs_pool, 0, VS_ON_VECTOR)
-        for c0 in range(VS_ON_VECTOR, T, VS_PIECE):
-            nc.gpsimd.memset(vs_pool[:ROW, c0 : c0 + VS_PIECE], 0.0)
+        zero_on_vector(kb_pool[:ROW], KB_ON_GPSIMD, T)
+        make_identity(nc, ident[:], nomemset=True)
+        zero_on_vector(vs_pool[:ROW], 0, VS_ON_VECTOR)
+        nc.gpsimd.memset(vs_pool[:ROW, VS_ON_VECTOR:], 0.0)
         nc.gpsimd.memset(vsc_pool[:], 0)
 
         def load_queries(b):
@@ -83,35 +83,37 @@ def tile_attend_pkv8_soft_kb_kernel(
 
         nc.sync.dma_start(offsets[:], offs)
         nc.scalar.dma_start(kb_pool[ROW:, :], kb[0:1, :])
+        nc.scalar.dma_start(vs_pool[ROW:, :], vs[0:1, :])
         load_queries(0)
+        key_words = k_words[0].rearrange("s n t -> s (n t)").bitcast(I32)
+        nc.sync.dma_start(kw_pool[:, :EARLY_WORDS], key_words[:, :EARLY_WORDS])
         ks_rows = k_scales[0].bitcast(I32)
         for r in range(4):
             nc.sync.dma_start(ks_pool[r:P:QUADRANT, :], ks_rows[r:SCALE_ROWS:4, :])
-        nc.sync.dma_start(vs_pool[ROW:, :], vs[0:1, :])
-        nc.sync.dma_start(kw_pool[:], k_words[0].rearrange("s n t -> s (n t)").bitcast(I32))
+        nc.sync.dma_start(kw_pool[:, EARLY_WORDS:], key_words[:, EARLY_WORDS:])
         load_queries(1)
         nc.sync.dma_start(v_offsets[:], voffs)
+        nc.sync.dma_start(
+            vw_pool[:].rearrange("s (u e) -> s u e", u=POOL_PAGES),
+            v_words.rearrange("u s e t -> s u (e t)").bitcast(I32),
+        )
         vsc_rows = v_scales.bitcast(I32).rearrange("u f c -> f u c")
         for r in range(4):
             nc.sync.dma_start(
                 vsc_pool[r:P:QUADRANT, :].rearrange("s (u c) -> s u c", u=POOL_PAGES),
                 vsc_rows[r:SCALE_ROWS:4],
             )
-        nc.sync.dma_start(
-            vw_pool[:].rearrange("s (u e) -> s u e", u=POOL_PAGES),
-            v_words.rearrange("u s e t -> s u (e t)").bitcast(I32),
-        )
 
-        def entries(g):
-            return offsets[:, g * PAGE // LIST : (g + 1) * PAGE // LIST]
+        def entries(g0, g1):
+            return offsets[:, g0 * PAGE // LIST : g1 * PAGE // LIST]
 
         def round_queries(b):
             q_bf = sb([P, NQ, PACK], BF16, f"q_bf{b}")
             nc.scalar.copy(q_bf[:], q_raw[b][:].rearrange("s t q -> s q t"))
             return q_bf
 
-        def quantise_queries(b, q_bf):
-            codes = sb([P, NQ], U32, f"q_codes{b}")
+        def quantise_queries(b, q_bf, reuses=None):
+            codes = sb([P, NQ], U32, f"q_codes{b}", reuses=reuses)
             scales = sb([P, NQ], U8, f"q_scales{b}")
             nc.vector.quantize_mx(
                 out=codes[:].bitcast(FP8X4), scales=scales[:], in_=q_bf[:].rearrange("s q t -> s (q t)")
@@ -120,113 +122,135 @@ def tile_attend_pkv8_soft_kb_kernel(
 
         q_bf0 = round_queries(0)
 
-        kb_cols = sb([P, PAGES, PACK], F32, "kb_cols")
+        kb_col = []
         for g in range(PAGES):
             kb_got = sb([P, PAGE], F32, f"kb_got{g}")
-            nc.scalar.activation(kb_got[:], kb_pool[:].indirect(entries(g)), ACT.Copy)
-            turned = turn_bank("kb_turned")
+            nc.scalar.activation(kb_got[:], kb_pool[:].indirect(entries(g, g + 1)), ACT.Copy)
+            turned = query_bank([P, PACK, P], "kb_turned", g)
             for c in range(PACK):
                 nc.tensor.transpose(turned[:, c, :], kb_got[:, c * P : (c + 1) * P], ident[:])
-            nc.scalar.copy(kb_cols[:, g, :], turned[:, :, ROW])
+            cuts = (0, PACK - 1, PACK) if g == 0 else (0, PACK)
+            cols = []
+            for c0, c1 in zip(cuts, cuts[1:]):
+                part = sb([P, c1 - c0], F32, f"kb_cols{g}{c0}")
+                nc.scalar.copy(part[:], turned[:, c0:c1, ROW])
+                cols.extend(part[:, c : c + 1] for c in range(c1 - c0))
+            kb_col.append(cols)
 
-        vs_cols = []
+        vs_cols = {}
 
         def gather_token_scales(g, reuses=None):
             vs_got = sb([P, PAGE], F32, f"vs_got{g}", reuses=reuses)
-            nc.scalar.activation(vs_got[:], vs_pool[:].indirect(entries(g)), ACT.Copy)
-            vs_cols.append(sb([P, 1, PACK], F32, f"vs_cols{g}"))
+            nc.scalar.activation(vs_got[:], vs_pool[:].indirect(entries(g, g + 1)), ACT.Copy)
+            vs_cols[g] = sb([P, 1, PACK], F32, f"vs_cols{g}")
             nc.sync.dma_start(vs_cols[g][:, 0, :], vs_got[ROW:, :].rearrange("o (s t) -> o s t", t=PACK))
 
-        ks_got = sb([P, B * N], U8, "ks_got")
-        nc.vector.tensor_copy(ks_got[:], ks_pool[:].bitcast(U8).indirect(offsets[:]))
+        ks_got = []
+
+        def gather_key_scales(g0, g1, reuses=None):
+            got = sb([P, (g1 - g0) * PAGE], U8, f"ks_got{g0}", reuses=reuses)
+            nc.vector.tensor_copy(got[:], ks_pool[:].bitcast(U8).indirect(entries(g0, g1)))
+            ks_got.extend(got[:, h * PAGE : (h + 1) * PAGE] for h in range(g1 - g0))
+
         queries = [quantise_queries(0, q_bf0)]
+        gather_key_scales(0, PAGES - 1)
+        gather_token_scales(0)
+        gather_token_scales(1)
+        q_bf1 = round_queries(1)
 
-        kw_got, scores = [], []
+        kw_got = []
+        for g in range(PAGES):
+            kw_got.append(sb([P, PAGE], U32, f"kw_got{g}"))
+            nc.vector.tensor_copy(kw_got[g][:], kw_pool[:].bitcast(U32).indirect(entries(g, g + 1)))
 
-        def gather_keys(g, reuses=None):
-            kw_got.append(sb([P, PAGE], U32, f"kw_got{g}", reuses=reuses))
-            nc.vector.tensor_copy(kw_got[g][:], kw_pool[:].bitcast(U32).indirect(entries(g)))
+        raw, scores = [], []
 
-        def score_page(g):
+        def multiply(g):
             q_codes, q_scales = queries[g // SEQ_PAGES]
-            raw = raw_bank([P, PACK, NQ], "raw")
+            raw.append(slot_bank("raw"))
             for c in range(PACK):
                 nc.tensor.matmul_mx(
-                    out=raw[:, c, :],
+                    out=raw[g][:, c, :],
                     lhsT=kw_got[g][:, c * P : (c + 1) * P].bitcast(FP8X4),
-                    lhsT_scale=ks_got[:, g * PAGE + c * P : g * PAGE + (c + 1) * P],
+                    lhsT_scale=ks_got[g][:, c * P : (c + 1) * P],
                     rhs=q_codes[:].bitcast(FP8X4),
                     rhs_scale=q_scales[:],
                     start=True,
                     stop=True,
                 )
+
+        def bias_and_turn(g, order=range(PACK)):
             biased = [sb([P, NQ], F32, f"biased{g}{c}") for c in range(PACK)]
             for c in range(PACK):
-                nc.scalar.activation(biased[c][:], raw[:, c, :], ACT.Identity, bias=kb_cols[:, g, c : c + 1])
-            scores.append(scores_bank())
-            for c in range(PACK):
+                nc.scalar.activation(biased[c][:], raw[g][:, c, :], ACT.Identity, bias=kb_col[g][c])
+            scores.append(query_bank([P, PAGE], "scores", g))
+            for c in order:
                 nc.tensor.transpose(scores[g][:, c * P : (c + 1) * P], biased[c][:], ident[:])
 
-        gather_token_scales(0)
-        gather_token_scales(1)
-        gather_keys(0)
-        gather_keys(1)
-        q_bf1 = round_queries(1)
-        score_page(0)
-        gather_keys(2)
-        score_page(1)
-        queries.append(quantise_queries(1, q_bf1))
-        gather_keys(3, reuses="kw_got1")
-        gather_token_scales(2, reuses="biased10")
-        score_page(2)
-        score_page(3)
-        gather_token_scales(3, reuses="biased20")
+        multiply(0)
+        multiply(1)
+        bias_and_turn(0)
+        queries.append(quantise_queries(1, q_bf1, reuses="kb_cols00"))
+        gather_key_scales(PAGES - 1, PAGES, reuses="kb_cols03")
+        multiply(2)
+        multiply(3)
+        bias_and_turn(1, order=(3, 0, 1, 2))
+        gather_token_scales(3, reuses="biased02")
+        bias_and_turn(2)
+        bias_and_turn(3)
+        gather_token_scales(2, reuses="biased20")
 
-        negated, neg_max, page_sums, turned_p = [], [], [], []
+        def dealt(g):
+            return scores[g][:].rearrange("q (s t) -> q t s", t=PACK)
 
-        def page_maximum(g):
-            negated.append(sb([P, PACK, P], F32, f"negated{g}"))
-            neg_max.append(sb([P, 1], F32, f"neg_max{g}"))
+        first_max, neg_max, negated = [], [], []
+
+        def first_maximum(b):
+            first_max.append(sb([P, 1], F32, f"first_max{b}"))
+            nc.vector.tensor_reduce(first_max[b][:], scores[SEQ_PAGES * b][:], AXIS.X, ALU.max, negate=True)
+
+        def row_maximum(b):
+            negated.append(sb([P, PACK, P], F32, f"negated{b}"))
+            neg_max.append(sb([P, 1], F32, f"neg_max{b}"))
             nc.vector.tensor_scalar(
-                negated[g][:],
-                scores[g][:].rearrange("q (s t) -> q t s", t=PACK),
+                negated[b][:],
+                dealt(SEQ_PAGES * b + 1),
                 -1.0,
-                neg_max[g - 1][:] if g % SEQ_PAGES else None,
+                first_max[b][:],
                 ALU.mult,
                 ALU.min,
-                accum_out=neg_max[g][:],
+                accum_out=neg_max[b][:],
             )
 
-        def numerators(b):
-            for g in range(b * SEQ_PAGES, (b + 1) * SEQ_PAGES):
-                probs = sb([P, PACK, P], F32, f"p{g}")
-                page_sums.append(sb([P, 1], F32, f"page_sum{g}"))
-                nc.scalar.activation(
-                    probs[:],
-                    negated[g][:],
-                    ACT.Exp,
-                    bias=neg_max[(b + 1) * SEQ_PAGES - 1][:],
-                    scale=-1.0,
-                    accum_out=page_sums[g][:],
-                )
-                turned_p.append(turn_bank("turned_p"))
-                for t in range(PACK):
-                    nc.tensor.transpose(turned_p[g][:, t, :], probs[:, t, :], ident[:])
+        page_sums, turned_p = {}, {}
 
-        page_maximum(0)
-        vsc_got = sb([P, PAGES * DV], U8, "vsc_got", reuses="biased03")
-        nc.vector.tensor_copy(vsc_got[:], vsc_pool[:].bitcast(U8).indirect(v_offsets[:]))
-        page_maximum(1)
-        numerators(0)
-        page_maximum(2)
-        vw_got = sb([P, PAGES * DV], U32, "vw_got", reuses="biased23")
+        def numerator(g):
+            b = g // SEQ_PAGES
+            source, sign = (negated[b][:], -1.0) if g % SEQ_PAGES else (dealt(g), 1.0)
+            probs = sb([P, PACK, P], F32, f"p{g}")
+            page_sums[g] = sb([P, 1], F32, f"page_sum{g}")
+            nc.scalar.activation(
+                probs[:], source, ACT.Exp, bias=neg_max[b][:], scale=sign, accum_out=page_sums[g][:]
+            )
+            turned_p[g] = slot_bank("turned_p")
+            for t in range(PACK):
+                nc.tensor.transpose(turned_p[g][:, t, :], probs[:, t, :], ident[:])
+
+        first_maximum(0)
+        vw_got = sb([P, PAGES * DV], U32, "vw_got", reuses="biased03")
         nc.vector.tensor_copy(vw_got[:], vw_pool[:].bitcast(U32).indirect(v_offsets[:]))
-        page_maximum(3)
-        numerators(1)
+        row_maximum(0)
+        first_maximum(1)
+        row_maximum(1)
+        vsc_got = sb([P, PAGES * DV], U8, "vsc_got", reuses="biased33")
+        nc.vector.tensor_copy(vsc_got[:], vsc_pool[:].bitcast(U8).indirect(v_offsets[:]))
+        late_order = (0, 1, 3, 2)
+        for g in late_order:
+            numerator(g)
 
         row_sums = sb([P, B], F32, "row_sums")
         for b in range(B):
-            first, second = page_sums[b * SEQ_PAGES : (b + 1) * SEQ_PAGES]
+            first, second = page_sums[b * SEQ_PAGES], page_sums[b * SEQ_PAGES + 1]
             nc.scalar.activation(row_sums[:, b : b + 1], first[:], ACT.Identity, bias=second[:])
         inverse = sb([P, B], F32, "inverse")
 
@@ -250,25 +274,25 @@ def tile_attend_pkv8_soft_kb_kernel(
                 in_=w[b][:].rearrange("s h q t -> s (h q t)")[:, PACK * c0 : PACK * (c0 + NQ)],
             )
 
-        weigh(0)
-        for g in range(1, PAGES):
+        weigh(late_order[0])
+        for before, g in zip(late_order, late_order[1:]):
             weigh(g)
-            quantise_weights(g - 1)
+            quantise_weights(before)
         nc.vector.reciprocal(inverse[:], row_sums[:])
-        quantise_weights(PAGES - 1)
+        quantise_weights(late_order[-1])
 
         for b in range(B):
-            y = raw_bank([P, DV], "y")
-            for h in range(SEQ_PAGES):
-                g = SEQ_PAGES * b + h
+            y = query_bank([P, DV], "y", SEQ_PAGES + b)
+            for step, g in enumerate(late_order[b * SEQ_PAGES : (b + 1) * SEQ_PAGES]):
+                h = g % SEQ_PAGES
                 nc.tensor.matmul_mx(
                     out=y[:],
                     lhsT=w_codes[b][:, h * NQ : (h + 1) * NQ].bitcast(FP8X4),
                     lhsT_scale=w_scales[b][:, h * NQ : (h + 1) * NQ],
                     rhs=vw_got[:, g * DV : (g + 1) * DV].bitcast(FP8X4),
                     rhs_scale=vsc_got[:, g * DV : (g + 1) * DV],
-                    start=(h == 0),
-                    stop=(h == SEQ_PAGES - 1),
+                    start=(step == 0),
+                    stop=(step == SEQ_PAGES - 1),
                 )
             result = sb([P, DV], F32, f"result{b}")
             nc.scalar.activation(result[:], y[:], ACT.Copy, scale=inverse[:, b : b + 1])

@@ -14,10 +14,10 @@ LIST = 16
 SCALE_ROWS = 16
 QUADRANT = 32
 ROW = P - 1
-KS_ON_GPSIMD = 640
-KB_ON_GPSIMD = 2048
-VS_ON_VECTOR = 1664
-EARLY_WORDS = 1536
+KB_ON_GPSIMD = 1792
+VS_ON_VECTOR = 1536
+VS_PIECE = 1280
+STRAIGHT = 1
 
 F32 = mybir.dt.float32
 BF16 = mybir.dt.bfloat16
@@ -68,14 +68,13 @@ def tile_attend_pkv8_soft_kb_kernel(
             nc.vector.memset(rows[:, c0:mid], 0)
             nc.vector.memset(rows[:, mid:c1], 0)
 
-        nc.gpsimd.memset(ks_pool[:, :KS_ON_GPSIMD], 0)
-        zero_on_vector(ks_pool[:], KS_ON_GPSIMD, T // 4)
-        nc.gpsimd.memset(ident[:], 0.0)
+        nc.gpsimd.memset(ks_pool[:], 0)
         nc.gpsimd.memset(kb_pool[:ROW, :KB_ON_GPSIMD], 0.0)
         zero_on_vector(kb_pool[:ROW], KB_ON_GPSIMD, T)
-        make_identity(nc, ident[:], nomemset=True)
+        make_identity(nc, ident[:])
         zero_on_vector(vs_pool[:ROW], 0, VS_ON_VECTOR)
-        nc.gpsimd.memset(vs_pool[:ROW, VS_ON_VECTOR:], 0.0)
+        for c0 in range(VS_ON_VECTOR, T, VS_PIECE):
+            nc.gpsimd.memset(vs_pool[:ROW, c0 : c0 + VS_PIECE], 0.0)
         nc.gpsimd.memset(vsc_pool[:], 0)
 
         def load_queries(b):
@@ -83,14 +82,12 @@ def tile_attend_pkv8_soft_kb_kernel(
 
         nc.sync.dma_start(offsets[:], offs)
         nc.scalar.dma_start(kb_pool[ROW:, :], kb[0:1, :])
-        nc.scalar.dma_start(vs_pool[ROW:, :], vs[0:1, :])
         load_queries(0)
-        key_words = k_words[0].rearrange("s n t -> s (n t)").bitcast(I32)
-        nc.sync.dma_start(kw_pool[:, :EARLY_WORDS], key_words[:, :EARLY_WORDS])
         ks_rows = k_scales[0].bitcast(I32)
         for r in range(4):
             nc.sync.dma_start(ks_pool[r:P:QUADRANT, :], ks_rows[r:SCALE_ROWS:4, :])
-        nc.sync.dma_start(kw_pool[:, EARLY_WORDS:], key_words[:, EARLY_WORDS:])
+        nc.sync.dma_start(vs_pool[ROW:, :], vs[0:1, :])
+        nc.sync.dma_start(kw_pool[:], k_words[0].rearrange("s n t -> s (n t)").bitcast(I32))
         load_queries(1)
         nc.sync.dma_start(v_offsets[:], voffs)
         nc.sync.dma_start(
@@ -137,6 +134,12 @@ def tile_attend_pkv8_soft_kb_kernel(
                 cols.extend(part[:, c : c + 1] for c in range(c1 - c0))
             kb_col.append(cols)
 
+        spread = query_bank([P, PAGE], "kb_spread", STRAIGHT)
+        for c in range(PACK):
+            nc.tensor.transpose(spread[:, c * P : (c + 1) * P], kb_col[STRAIGHT][c].to_broadcast([P, P]), ident[:])
+        kb_rows = sb([P, PACK, P], F32, "kb_rows")
+        nc.scalar.copy(kb_rows[:], spread[:].rearrange("q (s t) -> q t s", t=PACK))
+
         vs_cols = {}
 
         def gather_token_scales(g, reuses=None):
@@ -153,7 +156,7 @@ def tile_attend_pkv8_soft_kb_kernel(
             ks_got.extend(got[:, h * PAGE : (h + 1) * PAGE] for h in range(g1 - g0))
 
         queries = [quantise_queries(0, q_bf0)]
-        gather_key_scales(0, PAGES - 1)
+        gather_key_scales(0, PAGES)
         gather_token_scales(0)
         gather_token_scales(1)
         q_bf1 = round_queries(1)
@@ -163,11 +166,11 @@ def tile_attend_pkv8_soft_kb_kernel(
             kw_got.append(sb([P, PAGE], U32, f"kw_got{g}"))
             nc.vector.tensor_copy(kw_got[g][:], kw_pool[:].bitcast(U32).indirect(entries(g, g + 1)))
 
-        raw, scores = [], []
+        raw, scores = {}, {}
 
         def multiply(g):
             q_codes, q_scales = queries[g // SEQ_PAGES]
-            raw.append(slot_bank("raw"))
+            raw[g] = slot_bank("raw")
             for c in range(PACK):
                 nc.tensor.matmul_mx(
                     out=raw[g][:, c, :],
@@ -179,29 +182,38 @@ def tile_attend_pkv8_soft_kb_kernel(
                     stop=True,
                 )
 
-        def bias_and_turn(g, order=range(PACK)):
+        def bias_and_turn(g):
             biased = [sb([P, NQ], F32, f"biased{g}{c}") for c in range(PACK)]
             for c in range(PACK):
                 nc.scalar.activation(biased[c][:], raw[g][:, c, :], ACT.Identity, bias=kb_col[g][c])
-            scores.append(query_bank([P, PAGE], "scores", g))
-            for c in order:
+            scores[g] = query_bank([P, PAGE], "scores", g)
+            for c in range(PACK):
                 nc.tensor.transpose(scores[g][:, c * P : (c + 1) * P], biased[c][:], ident[:])
-
-        multiply(0)
-        multiply(1)
-        bias_and_turn(0)
-        queries.append(quantise_queries(1, q_bf1, reuses="kb_cols00"))
-        gather_key_scales(PAGES - 1, PAGES, reuses="kb_cols03")
-        multiply(2)
-        multiply(3)
-        bias_and_turn(1, order=(3, 0, 1, 2))
-        gather_token_scales(3, reuses="biased02")
-        bias_and_turn(2)
-        bias_and_turn(3)
-        gather_token_scales(2, reuses="biased20")
 
         def dealt(g):
             return scores[g][:].rearrange("q (s t) -> q t s", t=PACK)
+
+        multiply(0)
+        scores[STRAIGHT] = query_bank([P, PAGE], "scores", STRAIGHT)
+        nc.tensor.matmul_mx(
+            out=scores[STRAIGHT][:],
+            lhsT=queries[0][0][:].bitcast(FP8X4),
+            lhsT_scale=queries[0][1][:],
+            rhs=kw_got[STRAIGHT][:].bitcast(FP8X4),
+            rhs_scale=ks_got[STRAIGHT],
+            start=True,
+            stop=True,
+        )
+        bias_and_turn(0)
+        queries.append(quantise_queries(1, q_bf1, reuses="kb_cols00"))
+        straight_sum = sb([P, PACK, P], F32, "straight_sum", reuses="kb_cols03")
+        nc.vector.tensor_tensor(straight_sum[:], dealt(STRAIGHT), kb_rows[:], ALU.add)
+        gather_token_scales(3, reuses="biased00")
+        gather_token_scales(2, reuses="biased01")
+        multiply(2)
+        multiply(3)
+        bias_and_turn(2)
+        bias_and_turn(3)
 
         first_max, neg_max, negated = [], [], []
 
@@ -209,12 +221,12 @@ def tile_attend_pkv8_soft_kb_kernel(
             first_max.append(sb([P, 1], F32, f"first_max{b}"))
             nc.vector.tensor_reduce(first_max[b][:], scores[SEQ_PAGES * b][:], AXIS.X, ALU.max, negate=True)
 
-        def row_maximum(b):
+        def row_maximum(b, source):
             negated.append(sb([P, PACK, P], F32, f"negated{b}"))
             neg_max.append(sb([P, 1], F32, f"neg_max{b}"))
             nc.vector.tensor_scalar(
                 negated[b][:],
-                dealt(SEQ_PAGES * b + 1),
+                source,
                 -1.0,
                 first_max[b][:],
                 ALU.mult,
@@ -239,9 +251,9 @@ def tile_attend_pkv8_soft_kb_kernel(
         first_maximum(0)
         vw_got = sb([P, PAGES * DV], U32, "vw_got", reuses="biased03")
         nc.vector.tensor_copy(vw_got[:], vw_pool[:].bitcast(U32).indirect(v_offsets[:]))
-        row_maximum(0)
+        row_maximum(0, straight_sum[:])
         first_maximum(1)
-        row_maximum(1)
+        row_maximum(1, dealt(PAGES - 1))
         vsc_got = sb([P, PAGES * DV], U8, "vsc_got", reuses="biased33")
         nc.vector.tensor_copy(vsc_got[:], vsc_pool[:].bitcast(U8).indirect(v_offsets[:]))
         late_order = (0, 1, 3, 2)

@@ -119,26 +119,34 @@ def tile_attend_pkv8_soft_kb_kernel(
 
         q_bf0 = round_queries(0)
 
-        kb_col = []
-        for g in range(PAGES):
-            kb_got = sb([P, PAGE], F32, f"kb_got{g}")
-            nc.scalar.activation(kb_got[:], kb_pool[:].indirect(entries(g, g + 1)), ACT.Copy)
-            turned = query_bank([P, PACK, P], "kb_turned", g)
-            for c in range(PACK):
-                nc.tensor.transpose(turned[:, c, :], kb_got[:, c * P : (c + 1) * P], ident[:])
-            cuts = (0, PACK - 1, PACK) if g == 0 else (0, PACK)
-            cols = []
-            for c0, c1 in zip(cuts, cuts[1:]):
-                part = sb([P, c1 - c0], F32, f"kb_cols{g}{c0}")
-                nc.scalar.copy(part[:], turned[:, c0:c1, ROW])
-                cols.extend(part[:, c : c + 1] for c in range(c1 - c0))
-            kb_col.append(cols)
+        kb_got, kb_turned, kb_col = {}, {}, {}
 
+        def gather_biases(g):
+            kb_got[g] = sb([P, PAGE], F32, f"kb_got{g}")
+            nc.scalar.activation(kb_got[g][:], kb_pool[:].indirect(entries(g, g + 1)), ACT.Copy)
+
+        def turn_biases(g):
+            kb_turned[g] = query_bank([P, PACK, P], "kb_turned", g)
+            for c in range(PACK):
+                nc.tensor.transpose(kb_turned[g][:, c, :], kb_got[g][:, c * P : (c + 1) * P], ident[:])
+
+        def bias_columns(g, target, c0=0, c1=PACK):
+            nc.scalar.copy(target, kb_turned[g][:, c0:c1, ROW])
+            kb_col.setdefault(g, []).extend(target[:, c : c + 1] for c in range(c1 - c0))
+
+        for g in (STRAIGHT, 0):
+            gather_biases(g)
+            turn_biases(g)
+        gather_biases(2)
+        bias_columns(STRAIGHT, sb([P, PACK], F32, "kb_cols1")[:])
         spread = query_bank([P, PAGE], "kb_spread", STRAIGHT)
         for c in range(PACK):
             nc.tensor.transpose(spread[:, c * P : (c + 1) * P], kb_col[STRAIGHT][c].to_broadcast([P, P]), ident[:])
-        kb_rows = sb([P, PACK, P], F32, "kb_rows")
-        nc.scalar.copy(kb_rows[:], spread[:].rearrange("q (s t) -> q t s", t=PACK))
+        turn_biases(2)
+        gather_biases(3)
+        turn_biases(3)
+        bias_columns(0, sb([P, PACK - 1], F32, "kb_cols00")[:], 0, PACK - 1)
+        bias_columns(0, sb([P, 1], F32, "kb_cols03")[:], PACK - 1, PACK)
 
         vs_cols = {}
 
@@ -157,9 +165,14 @@ def tile_attend_pkv8_soft_kb_kernel(
 
         queries = [quantise_queries(0, q_bf0)]
         gather_key_scales(0, PAGES)
+        kb_rows = sb([P, PACK, P], F32, "kb_rows")
+        nc.vector.tensor_copy(kb_rows[:], spread[:].rearrange("q (s t) -> q t s", t=PACK))
         gather_token_scales(0)
         gather_token_scales(1)
         q_bf1 = round_queries(1)
+        late_cols = sb([P, SEQ_PAGES, PACK], F32, "late_cols", reuses="q_raw1")
+        for h in range(SEQ_PAGES):
+            bias_columns(SEQ_PAGES + h, late_cols[:, h])
 
         kw_got = []
         for g in range(PAGES):

@@ -14,10 +14,10 @@ LIST = 16
 SCALE_ROWS = 16
 QUADRANT = 32
 ROW = P - 1
+STRAIGHT = 1
 KB_ON_GPSIMD = 1792
 VS_ON_VECTOR = 1536
-VS_PIECE = 1280
-STRAIGHT = 1
+VS_PIECE = (T - VS_ON_VECTOR) // 2
 
 F32 = mybir.dt.float32
 BF16 = mybir.dt.bfloat16
@@ -63,16 +63,16 @@ def tile_attend_pkv8_soft_kb_kernel(
         q_raw = [sb([P, PACK, NQ], F32, f"q_raw{b}") for b in range(B)]
         ident = sb([P, P], F32, "ident")
 
-        def zero_on_vector(rows, c0, c1):
+        def zero_on_vector(pool, c0, c1):
             mid = (c0 + c1) // 2 - 1
-            nc.vector.memset(rows[:, c0:mid], 0)
-            nc.vector.memset(rows[:, mid:c1], 0)
+            nc.vector.memset(pool[:ROW, c0:mid], 0.0)
+            nc.vector.memset(pool[:ROW, mid:c1], 0.0)
 
         nc.gpsimd.memset(ks_pool[:], 0)
         nc.gpsimd.memset(kb_pool[:ROW, :KB_ON_GPSIMD], 0.0)
-        zero_on_vector(kb_pool[:ROW], KB_ON_GPSIMD, T)
+        zero_on_vector(kb_pool, KB_ON_GPSIMD, T)
         make_identity(nc, ident[:])
-        zero_on_vector(vs_pool[:ROW], 0, VS_ON_VECTOR)
+        zero_on_vector(vs_pool, 0, VS_ON_VECTOR)
         for c0 in range(VS_ON_VECTOR, T, VS_PIECE):
             nc.gpsimd.memset(vs_pool[:ROW, c0 : c0 + VS_PIECE], 0.0)
         nc.gpsimd.memset(vsc_pool[:], 0)
@@ -101,8 +101,8 @@ def tile_attend_pkv8_soft_kb_kernel(
                 vsc_rows[r:SCALE_ROWS:4],
             )
 
-        def entries(g0, g1):
-            return offsets[:, g0 * PAGE // LIST : g1 * PAGE // LIST]
+        def entries(g):
+            return offsets[:, g * PAGE // LIST : (g + 1) * PAGE // LIST]
 
         def round_queries(b):
             q_bf = sb([P, NQ, PACK], BF16, f"q_bf{b}")
@@ -121,9 +121,9 @@ def tile_attend_pkv8_soft_kb_kernel(
 
         kb_got, kb_turned, kb_col = {}, {}, {}
 
-        def gather_biases(g):
-            kb_got[g] = sb([P, PAGE], F32, f"kb_got{g}")
-            nc.scalar.activation(kb_got[g][:], kb_pool[:].indirect(entries(g, g + 1)), ACT.Copy)
+        def gather_biases(g, reuses=None):
+            kb_got[g] = sb([P, PAGE], F32, f"kb_got{g}", reuses=reuses)
+            nc.scalar.activation(kb_got[g][:], kb_pool[:].indirect(entries(g)), ACT.Copy)
 
         def turn_biases(g):
             kb_turned[g] = query_bank([P, PACK, P], "kb_turned", g)
@@ -143,7 +143,7 @@ def tile_attend_pkv8_soft_kb_kernel(
         for c in range(PACK):
             nc.tensor.transpose(spread[:, c * P : (c + 1) * P], kb_col[STRAIGHT][c].to_broadcast([P, P]), ident[:])
         turn_biases(2)
-        gather_biases(3)
+        gather_biases(3, reuses="kb_got1")
         turn_biases(3)
         bias_columns(0, sb([P, PACK - 1], F32, "kb_cols00")[:], 0, PACK - 1)
         bias_columns(0, sb([P, 1], F32, "kb_cols03")[:], PACK - 1, PACK)
@@ -152,19 +152,13 @@ def tile_attend_pkv8_soft_kb_kernel(
 
         def gather_token_scales(g, reuses=None):
             vs_got = sb([P, PAGE], F32, f"vs_got{g}", reuses=reuses)
-            nc.scalar.activation(vs_got[:], vs_pool[:].indirect(entries(g, g + 1)), ACT.Copy)
+            nc.scalar.activation(vs_got[:], vs_pool[:].indirect(entries(g)), ACT.Copy)
             vs_cols[g] = sb([P, 1, PACK], F32, f"vs_cols{g}")
             nc.sync.dma_start(vs_cols[g][:, 0, :], vs_got[ROW:, :].rearrange("o (s t) -> o s t", t=PACK))
 
-        ks_got = []
-
-        def gather_key_scales(g0, g1, reuses=None):
-            got = sb([P, (g1 - g0) * PAGE], U8, f"ks_got{g0}", reuses=reuses)
-            nc.vector.tensor_copy(got[:], ks_pool[:].bitcast(U8).indirect(entries(g0, g1)))
-            ks_got.extend(got[:, h * PAGE : (h + 1) * PAGE] for h in range(g1 - g0))
-
         queries = [quantise_queries(0, q_bf0)]
-        gather_key_scales(0, PAGES)
+        ks_got = sb([P, B * N], U8, "ks_got")
+        nc.vector.tensor_copy(ks_got[:], ks_pool[:].bitcast(U8).indirect(offsets[:]))
         kb_rows = sb([P, PACK, P], F32, "kb_rows")
         nc.vector.tensor_copy(kb_rows[:], spread[:].rearrange("q (s t) -> q t s", t=PACK))
         gather_token_scales(0)
@@ -177,7 +171,7 @@ def tile_attend_pkv8_soft_kb_kernel(
         kw_got = []
         for g in range(PAGES):
             kw_got.append(sb([P, PAGE], U32, f"kw_got{g}"))
-            nc.vector.tensor_copy(kw_got[g][:], kw_pool[:].bitcast(U32).indirect(entries(g, g + 1)))
+            nc.vector.tensor_copy(kw_got[g][:], kw_pool[:].bitcast(U32).indirect(entries(g)))
 
         raw, scores = {}, {}
 
@@ -188,7 +182,7 @@ def tile_attend_pkv8_soft_kb_kernel(
                 nc.tensor.matmul_mx(
                     out=raw[g][:, c, :],
                     lhsT=kw_got[g][:, c * P : (c + 1) * P].bitcast(FP8X4),
-                    lhsT_scale=ks_got[g][:, c * P : (c + 1) * P],
+                    lhsT_scale=ks_got[:, g * PAGE + c * P : g * PAGE + (c + 1) * P],
                     rhs=q_codes[:].bitcast(FP8X4),
                     rhs_scale=q_scales[:],
                     start=True,
@@ -207,13 +201,14 @@ def tile_attend_pkv8_soft_kb_kernel(
             return scores[g][:].rearrange("q (s t) -> q t s", t=PACK)
 
         multiply(0)
+        first_codes, first_scales = queries[0]
         scores[STRAIGHT] = query_bank([P, PAGE], "scores", STRAIGHT)
         nc.tensor.matmul_mx(
             out=scores[STRAIGHT][:],
-            lhsT=queries[0][0][:].bitcast(FP8X4),
-            lhsT_scale=queries[0][1][:],
+            lhsT=first_codes[:].bitcast(FP8X4),
+            lhsT_scale=first_scales[:],
             rhs=kw_got[STRAIGHT][:].bitcast(FP8X4),
-            rhs_scale=ks_got[STRAIGHT],
+            rhs_scale=ks_got[:, STRAIGHT * PAGE : (STRAIGHT + 1) * PAGE],
             start=True,
             stop=True,
         )
@@ -273,7 +268,7 @@ def tile_attend_pkv8_soft_kb_kernel(
         for g in late_order:
             numerator(g)
 
-        row_sums = sb([P, B], F32, "row_sums")
+        row_sums = sb([P, B], F32, "row_sums", reuses="negated1")
         for b in range(B):
             first, second = page_sums[b * SEQ_PAGES], page_sums[b * SEQ_PAGES + 1]
             nc.scalar.activation(row_sums[:, b : b + 1], first[:], ACT.Identity, bias=second[:])

@@ -145,8 +145,8 @@ def tile_attend_pkv8_soft_kb_kernel(
         turn_biases(2)
         gather_biases(3, reuses="kb_got1")
         turn_biases(3)
-        bias_columns(0, sb([P, PACK - 1], F32, "kb_cols00")[:], 0, PACK - 1)
-        bias_columns(0, sb([P, 1], F32, "kb_cols03")[:], PACK - 1, PACK)
+        for c0, c1 in ((0, 1), (1, PACK - 1), (PACK - 1, PACK)):
+            bias_columns(0, sb([P, c1 - c0], F32, f"kb_cols0{c0}")[:], c0, c1)
 
         vs_cols = {}
 
@@ -161,12 +161,9 @@ def tile_attend_pkv8_soft_kb_kernel(
         nc.vector.tensor_copy(ks_got[:], ks_pool[:].bitcast(U8).indirect(offsets[:]))
         kb_rows = sb([P, PACK, P], F32, "kb_rows")
         nc.vector.tensor_copy(kb_rows[:], spread[:].rearrange("q (s t) -> q t s", t=PACK))
-        gather_token_scales(0)
-        gather_token_scales(1)
+        for g in (0, 1, 3):
+            gather_token_scales(g)
         q_bf1 = round_queries(1)
-        late_cols = sb([P, SEQ_PAGES, PACK], F32, "late_cols", reuses="q_raw1")
-        for h in range(SEQ_PAGES):
-            bias_columns(SEQ_PAGES + h, late_cols[:, h])
 
         kw_got = []
         for g in range(PAGES):
@@ -213,11 +210,13 @@ def tile_attend_pkv8_soft_kb_kernel(
             stop=True,
         )
         bias_and_turn(0)
-        queries.append(quantise_queries(1, q_bf1, reuses="kb_cols00"))
+        queries.append(quantise_queries(1, q_bf1, reuses="kb_cols01"))
         straight_sum = sb([P, PACK, P], F32, "straight_sum", reuses="kb_cols03")
         nc.vector.tensor_tensor(straight_sum[:], dealt(STRAIGHT), kb_rows[:], ALU.add)
-        gather_token_scales(3, reuses="biased00")
-        gather_token_scales(2, reuses="biased01")
+        late_cols = sb([P, SEQ_PAGES, PACK], F32, "late_cols", reuses="kb_cols00")
+        for h in range(SEQ_PAGES):
+            bias_columns(SEQ_PAGES + h, late_cols[:, h])
+        gather_token_scales(2, reuses="biased00")
         multiply(2)
         multiply(3)
         bias_and_turn(2)

@@ -166,9 +166,11 @@ def tile_attend_pkv8_soft_kb_kernel(
         q_bf1 = round_queries(1)
 
         kw_got = []
-        for g in range(PAGES):
-            kw_got.append(sb([P, PAGE], U32, f"kw_got{g}"))
-            nc.vector.tensor_copy(kw_got[g][:], kw_pool[:].bitcast(U32).indirect(entries(g)))
+        for g0, g1 in ((0, 1), (1, SEQ_PAGES), (SEQ_PAGES, PAGES)):
+            keys = sb([P, (g1 - g0) * PAGE], U32, f"kw_got{g0}")
+            listed = offsets[:, g0 * PAGE // LIST : g1 * PAGE // LIST]
+            nc.vector.tensor_copy(keys[:], kw_pool[:].bitcast(U32).indirect(listed))
+            kw_got.extend(keys[:, h * PAGE : (h + 1) * PAGE] for h in range(g1 - g0))
 
         raw, scores = {}, {}
 
@@ -204,7 +206,7 @@ def tile_attend_pkv8_soft_kb_kernel(
             out=scores[STRAIGHT][:],
             lhsT=first_codes[:].bitcast(FP8X4),
             lhsT_scale=first_scales[:],
-            rhs=kw_got[STRAIGHT][:].bitcast(FP8X4),
+            rhs=kw_got[STRAIGHT].bitcast(FP8X4),
             rhs_scale=ks_got[:, STRAIGHT * PAGE : (STRAIGHT + 1) * PAGE],
             start=True,
             stop=True,

from contextlib import ExitStack

import concourse.mybir as mybir
from concourse.masks import make_identity

B, N, T, D, DV, NQ = 2, 1024, 4096, 512, 128, 128
P = 128
PACK = 4
PAGE = P * PACK
POOL_PAGES = T // PAGE
SEQ_PAGES = N // PAGE
PAGES = B * SEQ_PAGES
LIST = 16
SCALE_ROWS = 16
QUADRANT = 32
ROW = P - 1
STRAIGHT = 1
KB_ON_GPSIMD = 1792
VS_ON_VECTOR = 1536
VS_PIECE = (T - VS_ON_VECTOR) // 2

F32 = mybir.dt.float32
BF16 = mybir.dt.bfloat16
I32 = mybir.dt.int32
U32 = mybir.dt.uint32
U16 = mybir.dt.uint16
U8 = mybir.dt.uint8
FP8X4 = mybir.dt.float8_e4m3fn_x4
ALU = mybir.AluOpType
ACT = mybir.ActivationFunctionType
AXIS = mybir.AxisListType

FLOPS = 2 * B * NQ * N * (D + DV)


def tile_attend_pkv8_soft_kb_kernel(
    tc, qT, k_words, k_scales, v_words, v_scales, vs, kb, offs, voffs, out
):
    nc = tc.nc
    with ExitStack() as ctx:
        lists = ctx.enter_context(tc.tile_pool(name="lists", bufs=1))
        keep = ctx.enter_context(tc.tile_pool(name="keep", bufs=1))
        psum = ctx.enter_context(tc.psum_pool(name="psum", bufs=1))

        def sb(shape, dtype, name, reuses=None):
            return keep.tile(shape, dtype, name=name, tag=reuses or name, align_bytes=64)

        def slot_bank(name):
            return psum.tile([P, PACK, NQ], F32, name=name, tag="slot_major", bufs=4)

        def query_bank(shape, name, g):
            return psum.tile(shape, F32, name=name, tag=f"query_major{g}")

        offsets = lists.tile([P, B * N // LIST], U16, name="offsets")
        v_offsets = lists.tile([P, PAGES * DV // LIST], U16, name="v_offsets")

        ks_pool = sb([P, T // 4], I32, "ks_pool")
        kw_pool = sb([P, T], I32, "kw_pool")
        vw_pool = sb([P, POOL_PAGES * DV], I32, "vw_pool")
        kb_pool = sb([P, T], F32, "kb_pool")
        vs_pool = sb([P, T], F32, "vs_pool")
        vsc_pool = sb([P, POOL_PAGES * DV // 4], I32, "vsc_pool")
        q_raw = [sb([P, PACK, NQ], F32, f"q_raw{b}") for b in range(B)]
        ident = sb([P, P], F32, "ident")

        def zero_on_vector(pool, c0, c1):
            mid = (c0 + c1) // 2 - 1
            nc.vector.memset(pool[:ROW, c0:mid], 0.0)
            nc.vector.memset(pool[:ROW, mid:c1], 0.0)

        nc.gpsimd.memset(ks_pool[:], 0)
        nc.gpsimd.memset(kb_pool[:ROW, :KB_ON_GPSIMD], 0.0)
        zero_on_vector(kb_pool, KB_ON_GPSIMD, T)
        make_identity(nc, ident[:])
        zero_on_vector(vs_pool, 0, VS_ON_VECTOR)
        for c0 in range(VS_ON_VECTOR, T, VS_PIECE):
            nc.gpsimd.memset(vs_pool[:ROW, c0 : c0 + VS_PIECE], 0.0)
        nc.gpsimd.memset(vsc_pool[:], 0)

        def load_queries(b):
            nc.sync.dma_start(q_raw[b][:], qT[b].rearrange("(s t) q -> s t q", t=PACK))

        nc.sync.dma_start(offsets[:], offs)
        nc.scalar.dma_start(kb_pool[ROW:, :], kb[0:1, :])
        load_queries(0)
        ks_rows = k_scales[0].bitcast(I32)
        for r in range(4):
            nc.sync.dma_start(ks_pool[r:P:QUADRANT, :], ks_rows[r:SCALE_ROWS:4, :])
        nc.sync.dma_start(vs_pool[ROW:, :], vs[0:1, :])
        nc.sync.dma_start(kw_pool[:], k_words[0].rearrange("s n t -> s (n t)").bitcast(I32))
        load_queries(1)
        nc.sync.dma_start(v_offsets[:], voffs)
        nc.sync.dma_start(
            vw_pool[:].rearrange("s (u e) -> s u e", u=POOL_PAGES),
            v_words.rearrange("u s e t -> s u (e t)").bitcast(I32),
        )
        vsc_rows = v_scales.bitcast(I32).rearrange("u f c -> f u c")
        for r in range(4):
            nc.sync.dma_start(
                vsc_pool[r:P:QUADRANT, :].rearrange("s (u c) -> s u c", u=POOL_PAGES),
                vsc_rows[r:SCALE_ROWS:4],
            )

        def entries(g):
            return offsets[:, g * PAGE // LIST : (g + 1) * PAGE // LIST]

        def round_queries(b):
            q_bf = sb([P, NQ, PACK], BF16, f"q_bf{b}")
            nc.scalar.copy(q_bf[:], q_raw[b][:].rearrange("s t q -> s q t"))
            return q_bf

        def quantise_queries(b, q_bf, reuses=None):
            codes = sb([P, NQ], U32, f"q_codes{b}", reuses=reuses)
            scales = sb([P, NQ], U8, f"q_scales{b}")
            nc.vector.quantize_mx(
                out=codes[:].bitcast(FP8X4), scales=scales[:], in_=q_bf[:].rearrange("s q t -> s (q t)")
            )
            return codes, scales

        q_bf0 = round_queries(0)

        kb_got, kb_turned, kb_col = {}, {}, {}

        def gather_biases(g, reuses=None):
            kb_got[g] = sb([P, PAGE], F32, f"kb_got{g}", reuses=reuses)
            nc.scalar.activation(kb_got[g][:], kb_pool[:].indirect(entries(g)), ACT.Copy)

        def turn_biases(g):
            kb_turned[g] = query_bank([P, PACK, P], "kb_turned", g)
            for c in range(PACK):
                nc.tensor.transpose(kb_turned[g][:, c, :], kb_got[g][:, c * P : (c + 1) * P], ident[:])

        def bias_columns(g, target, c0=0, c1=PACK):
            nc.scalar.copy(target, kb_turned[g][:, c0:c1, ROW])
            kb_col.setdefault(g, []).extend(target[:, c : c + 1] for c in range(c1 - c0))

        for g in (STRAIGHT, 0):
            gather_biases(g)
            turn_biases(g)
        gather_biases(2)
        bias_columns(STRAIGHT, sb([P, PACK], F32, "kb_cols1")[:])
        spread = query_bank([P, PAGE], "kb_spread", STRAIGHT)
        for c in range(PACK):
            nc.tensor.transpose(spread[:, c * P : (c + 1) * P], kb_col[STRAIGHT][c].to_broadcast([P, P]), ident[:])
        turn_biases(2)
        gather_biases(3, reuses="kb_got1")
        turn_biases(3)
        for c0, c1 in ((0, 1), (1, PACK - 1), (PACK - 1, PACK)):
            bias_columns(0, sb([P, c1 - c0], F32, f"kb_cols0{c0}")[:], c0, c1)

        vs_cols = {}

        def gather_token_scales(g, reuses=None):
            vs_got = sb([P, PAGE], F32, f"vs_got{g}", reuses=reuses)
            nc.scalar.activation(vs_got[:], vs_pool[:].indirect(entries(g)), ACT.Copy)
            vs_cols[g] = sb([P, 1, PACK], F32, f"vs_cols{g}")
            nc.sync.dma_start(vs_cols[g][:, 0, :], vs_got[ROW:, :].rearrange("o (s t) -> o s t", t=PACK))

        queries = [quantise_queries(0, q_bf0)]
        ks_got = sb([P, B * N], U8, "ks_got")
        nc.vector.tensor_copy(ks_got[:], ks_pool[:].bitcast(U8).indirect(offsets[:]))
        kb_rows = sb([P, PACK, P], F32, "kb_rows")
        nc.vector.tensor_copy(kb_rows[:], spread[:].rearrange("q (s t) -> q t s", t=PACK))
        for g in (0, 1, 3):
            gather_token_scales(g)
        q_bf1 = round_queries(1)

        kw_got = []
        for g0, g1 in ((0, 1), (1, SEQ_PAGES), (SEQ_PAGES, PAGES)):
            keys = sb([P, (g1 - g0) * PAGE], U32, f"kw_got{g0}")
            listed = offsets[:, g0 * PAGE // LIST : g1 * PAGE // LIST]
            nc.vector.tensor_copy(keys[:], kw_pool[:].bitcast(U32).indirect(listed))
            kw_got.extend(keys[:, h * PAGE : (h + 1) * PAGE] for h in range(g1 - g0))

        raw, scores = {}, {}

        def multiply(g):
            q_codes, q_scales = queries[g // SEQ_PAGES]
            raw[g] = slot_bank("raw")
            for c in range(PACK):
                nc.tensor.matmul_mx(
                    out=raw[g][:, c, :],
                    lhsT=kw_got[g][:, c * P : (c + 1) * P].bitcast(FP8X4),
                    lhsT_scale=ks_got[:, g * PAGE + c * P : g * PAGE + (c + 1) * P],
                    rhs=q_codes[:].bitcast(FP8X4),
                    rhs_scale=q_scales[:],
                    start=True,
                    stop=True,
                )

        def bias_and_turn(g):
            biased = [sb([P, NQ], F32, f"biased{g}{c}") for c in range(PACK)]
            for c in range(PACK):
                nc.scalar.activation(biased[c][:], raw[g][:, c, :], ACT.Identity, bias=kb_col[g][c])
            scores[g] = query_bank([P, PAGE], "scores", g)
            for c in range(PACK):
                nc.tensor.transpose(scores[g][:, c * P : (c + 1) * P], biased[c][:], ident[:])

        def dealt(g):
            return scores[g][:].rearrange("q (s t) -> q t s", t=PACK)

        multiply(0)
        first_codes, first_scales = queries[0]
        scores[STRAIGHT] = query_bank([P, PAGE], "scores", STRAIGHT)
        nc.tensor.matmul_mx(
            out=scores[STRAIGHT][:],
            lhsT=first_codes[:].bitcast(FP8X4),
            lhsT_scale=first_scales[:],
            rhs=kw_got[STRAIGHT].bitcast(FP8X4),
            rhs_scale=ks_got[:, STRAIGHT * PAGE : (STRAIGHT + 1) * PAGE],
            start=True,
            stop=True,
        )
        bias_and_turn(0)
        queries.append(quantise_queries(1, q_bf1, reuses="kb_cols01"))
        straight_sum = sb([P, PACK, P], F32, "straight_sum", reuses="kb_cols03")
        nc.vector.tensor_tensor(straight_sum[:], dealt(STRAIGHT), kb_rows[:], ALU.add)
        late_cols = sb([P, SEQ_PAGES, PACK], F32, "late_cols", reuses="kb_cols00")
        for h in range(SEQ_PAGES):
            bias_columns(SEQ_PAGES + h, late_cols[:, h])
        gather_token_scales(2, reuses="biased00")
        multiply(2)
        multiply(3)
        bias_and_turn(2)
        bias_and_turn(3)

        first_max, neg_max, negated = [], [], []

        def first_maximum(b):
            first_max.append(sb([P, 1], F32, f"first_max{b}"))
            nc.vector.tensor_reduce(first_max[b][:], scores[SEQ_PAGES * b][:], AXIS.X, ALU.max, negate=True)

        def row_maximum(b, source):
            negated.append(sb([P, PACK, P], F32, f"negated{b}"))
            neg_max.append(sb([P, 1], F32, f"neg_max{b}"))
            nc.vector.tensor_scalar(
                negated[b][:],
                source,
                -1.0,
                first_max[b][:],
                ALU.mult,
                ALU.min,
                accum_out=neg_max[b][:],
            )

        page_sums, turned_p = {}, {}

        def numerator(g):
            b = g // SEQ_PAGES
            source, sign = (negated[b][:], -1.0) if g % SEQ_PAGES else (dealt(g), 1.0)
            probs = sb([P, PACK, P], F32, f"p{g}")
            page_sums[g] = sb([P, 1], F32, f"page_sum{g}")
            nc.scalar.activation(
                probs[:], source, ACT.Exp, bias=neg_max[b][:], scale=sign, accum_out=page_sums[g][:]
            )
            turned_p[g] = slot_bank("turned_p")
            for t in range(PACK):
                nc.tensor.transpose(turned_p[g][:, t, :], probs[:, t, :], ident[:])

        first_maximum(0)
        vw_got = sb([P, PAGES * DV], U32, "vw_got", reuses="biased03")
        nc.vector.tensor_copy(vw_got[:], vw_pool[:].bitcast(U32).indirect(v_offsets[:]))
        row_maximum(0, straight_sum[:])
        first_maximum(1)
        row_maximum(1, dealt(PAGES - 1))
        vsc_got = sb([P, PAGES * DV], U8, "vsc_got", reuses="biased33")
        nc.vector.tensor_copy(vsc_got[:], vsc_pool[:].bitcast(U8).indirect(v_offsets[:]))
        late_order = (0, 1, 3, 2)
        for g in late_order:
            numerator(g)

        row_sums = sb([P, B], F32, "row_sums", reuses="negated1")
        for b in range(B):
            first, second = page_sums[b * SEQ_PAGES], page_sums[b * SEQ_PAGES + 1]
            nc.scalar.activation(row_sums[:, b : b + 1], first[:], ACT.Identity, bias=second[:])
        inverse = sb([P, B], F32, "inverse")

        w = [sb([P, SEQ_PAGES, NQ, PACK], BF16, f"w{b}") for b in range(B)]
        w_codes = [sb([P, SEQ_PAGES * NQ], U32, f"w_codes{b}") for b in range(B)]
        w_scales = [sb([P, SEQ_PAGES * NQ], U8, f"w_scales{b}") for b in range(B)]

        def weigh(g):
            nc.vector.tensor_tensor(
                w[g // SEQ_PAGES][:, g % SEQ_PAGES],
                turned_p[g][:].rearrange("s t q -> s q t"),
                vs_cols[g][:].to_broadcast([P, NQ, PACK]),
                ALU.mult,
            )

        def quantise_weights(g):
            b, c0 = g // SEQ_PAGES, g % SEQ_PAGES * NQ
            nc.vector.quantize_mx(
                out=w_codes[b][:, c0 : c0 + NQ].bitcast(FP8X4),
                scales=w_scales[b][:, c0 : c0 + NQ],
                in_=w[b][:].rearrange("s h q t -> s (h q t)")[:, PACK * c0 : PACK * (c0 + NQ)],
            )

        weigh(late_order[0])
        for before, g in zip(late_order, late_order[1:]):
            weigh(g)
            quantise_weights(before)
        nc.vector.reciprocal(inverse[:], row_sums[:])
        quantise_weights(late_order[-1])

        for b in range(B):
            y = query_bank([P, DV], "y", SEQ_PAGES + b)
            for step, g in enumerate(late_order[b * SEQ_PAGES : (b + 1) * SEQ_PAGES]):
                h = g % SEQ_PAGES
                nc.tensor.matmul_mx(
                    out=y[:],
                    lhsT=w_codes[b][:, h * NQ : (h + 1) * NQ].bitcast(FP8X4),
                    lhsT_scale=w_scales[b][:, h * NQ : (h + 1) * NQ],
                    rhs=vw_got[:, g * DV : (g + 1) * DV].bitcast(FP8X4),
                    rhs_scale=vsc_got[:, g * DV : (g + 1) * DV],
                    start=(step == 0),
                    stop=(step == SEQ_PAGES - 1),
                )
            result = sb([P, DV], F32, f"result{b}")
            nc.scalar.activation(result[:], y[:], ACT.Copy, scale=inverse[:, b : b + 1])
            nc.sync.dma_start(out[b], result[:])
